import numpy as np, ml_dtypes
CORES = [2,6,10,14,18,22,26,30]
N = 8
BF = ml_dtypes.bfloat16
def gentries(a):
    return np.ascontiguousarray(a.reshape(8, 16, -1).transpose(0, 2, 1)).reshape(8, -1)
def gtable(e):
    e = np.asarray(e); return np.ascontiguousarray(e.reshape(8, -1, 16).transpose(0, 2, 1)).reshape(128, -1).astype(np.int32)
E, T, C, RO = 4096, 256, 2, 3
A = N * T
VM = 0.0625
def floats(rng, far):
    def size(n):
        if far: return np.exp2(-rng.integers(0, 3, (N, 8, 1, n))).astype(np.float32)
        return 0.75 + 0.25 * rng.random((N, 8, 1, n), dtype=np.float32)
    x = 0.25 + 0.75 * rng.random((N, 8, 16, T), dtype=np.float32)
    if far: x = x * size(T)
    u = 0.1875 * (0.5 + 0.5 * rng.random((N, 8, 16, E), dtype=np.float32)) * size(E)
    v = VM * (0.5 + 0.5 * rng.random((N, 8, 16, E), dtype=np.float32)) * size(E)
    w = np.exp(1.5 * rng.standard_normal((N, 128, 128))); w = w * np.reciprocal(np.add.reduce(w, axis=1, keepdims=True))
    one = np.arange(128)[None, :, None] == np.argsort(rng.random((N, 128)), axis=1)[:, None, :]
    share = 0.5 + 0.45 * rng.random((N, 1, 128))
    return x, u, v, (1.3 + 0.08 * rng.random((N, 1, 128))) * (share * one + (1.0 - share) * w)
def lone(rng, fl, b):
    x, u, v, m = fl; a = int(rng.integers(0, N)); c = (a + 1) % N
    u[:, b] = 0.1875 * (0.9375 + 0.0625 * rng.random((N, 16, E)))
    v[:, b] = VM * (0.875 + 0.125 * rng.random((N, 16, E)))
    level = np.where(np.argsort(rng.random(T)) < 3 * T // 8, 0.18 + 0.07 * rng.random(T), 0.0625 + 0.0125 * rng.random(T))
    x[a, b] = np.maximum(level[None, :] * (0.9375 + 0.125 * rng.random((16, T))), 0.0625)
    i = 16 * b + np.arange(16); m[a] = 0.0625 * m[a]; m[a][:, i] = 0.0
    m[a][np.ix_(i, i)] = 1.38 * (0.9 * np.eye(16) + 0.1 * 0.0625)
    p = np.argsort(rng.random(128))[:16]; w = 0.5 + 0.5 * rng.random((128, 16))
    m[c][:, p] = 1.38 * w * np.reciprocal(np.add.reduce(w, axis=0, keepdims=True))
    return x, u, v, m
def small(rng):
    q = rng.integers(-4, 5, (N, 8, 16, T), dtype=np.int32); q[:, :, 15] = rng.integers(-8, 33, (N, 8, T))
    k = rng.integers(-4, 5, (N, 8, 16, E), dtype=np.int32); k[:, :, 15] = rng.integers(-2, 3, (N, 8, E))
    return q, k, rng.integers(0, E, (N, 8, C, A), dtype=np.int32)
def pack(fl, q, k, n):
    x, u, v, m = fl
    return {"x0": x.reshape(N, 128, T).astype(BF), "rq": q.reshape(N, 128, T).astype(np.float32).astype(BF), "ke": k.reshape(N, 128, E).astype(np.float32).astype(BF),
            "ue": u.reshape(N, 128, E).astype(BF), "ve": v.reshape(N, 128, E).astype(BF), "nm": np.stack([gtable(a.reshape(8, -1)) for a in n]), "mm": m.astype(np.float32).astype(BF)}
def route(q, k, n):
    k = k.astype(np.int32); n = n.astype(np.int32)
    qa = np.ascontiguousarray(q.astype(np.int32).transpose(1, 2, 0, 3)).reshape(8, 16, A)
    h = np.zeros((8, A), np.int32); wins = []; names = []
    for l in range(RO):
        nn = (n + h[None, :, None, :]) & (E - 1); w = np.zeros((N, 8, A), np.int32)
        for s in range(N):
            c = np.take_along_axis(k[s], nn[s].reshape(8, 1, C * A), 2).reshape(8, 16, C, A)
            score = np.add.reduce(c * qa[:, :, None, :], axis=1)
            best = np.argmax(score, axis=1)
            w[s] = np.take_along_axis(nn[s], best[:, None, :], 1)[:, 0]
            count = np.bincount((w[s] + E * np.arange(8)[:, None]).reshape(-1), minlength=8 * E).reshape(8, E)
            k[s, :, 15] += np.sign(1 - count).astype(np.int32)
        h = np.roll(np.add.reduce(w, axis=0) & (E - 1), 1, axis=0).astype(np.int32)
        wins.append(w); names.append(nn)
    return wins, names, k[:, :, 15]
def setup_inputs(rng):
    return pack(floats(rng, False), *small(rng))
def setup_inputs_spread(rng):
    q = np.rint(np.exp2(5 * rng.random((N, 8, 1, T))) * (2 * rng.random((N, 8, 16, T)) - 1)).astype(np.int32)
    q[:, :, 15] = np.rint(np.exp2(5 * rng.random((N, 8, T))))
    k = np.rint(np.exp2(5 * rng.random((N, 8, 1, E))) * (2 * rng.random((N, 8, 16, E)) - 1)).astype(np.int32)
    k[:, :, 15] = np.where(rng.random((N, 8, E)) < 0.5, rng.integers(-2, 3, (N, 8, E)), rng.integers(-32, 33, (N, 8, E)))
    n = np.minimum((E * rng.random((N, 8, C, A)) ** 3).astype(np.int32), E - 1)
    return pack(floats(rng, True), q, k, n)
def setup_inputs_ends(rng):
    q = (64 * rng.integers(0, 2, (N, 8, 16, T)) - 32).astype(np.int32); a = rng.random((N, 8, 1, T))
    q = np.where(a < 0.35, 32, np.where(a < 0.5, -32, q)); q[..., T - 1] = 32; q[..., 0] = -32
    k = (64 * rng.integers(0, 2, (N, 8, 16, E)) - 32).astype(np.int32); a = rng.random((N, 8, 1, E))
    k = np.where(a < 0.3, 32, np.where(a < 0.4, -32, k))
    kind = rng.integers(0, 3, (N, 8)); kind[N - 1, 7] = 0; kind[0, 0] = 1; kind[0, 1] = 2
    k[..., E - 1] = np.where((kind < 2)[:, :, None], 32, k[..., E - 1]); k[..., 0] = np.where((kind == 0)[:, :, None], 32, np.where((kind == 1)[:, :, None], -32, k[..., 0]))
    n = (E - 1) * rng.integers(0, 2, (N, 8, C, A))
    n[:, 8 - RO:7, :, A - 1] = E - 1; n[:, 7, :, A - 1] = (E - 1) * (np.arange(C) % 2)
    wins, names, b = route(q, k, n)
    for s in range(N):
        for g in range(8):
            used = np.zeros(E, bool); last = np.zeros(E, bool)
            for l in range(RO - 1): used[names[l][s, g].reshape(-1)] = True
            last[names[RO - 1][s, g].reshape(-1)] = True
            e = np.nonzero(last & ~used)[0]
            k[s, g][:, e] = np.where(rng.random(e.size) < 0.7, 32, -32)
            if g == 7:
                e = names[RO - 1][s, g, :, A - 1]; k[s, g][:, e[~used[e]]] = 32
    return pack(floats(rng, False), q, k, n)
def setup_inputs_crowd(rng):
    q, k, n = small(rng); q[:, :6, 15] = rng.integers(1, 33, (N, 6, T)); k[:, :6, :15] = rng.integers(-4, 5, (N, 6, 15, 1))
    o = rng.permutation(A); n[:, :2] = rng.integers(0, E, (N, 2, C, 1))
    for s in range(N):
        for g in range(2, 8):
            p = rng.permutation(E); v = n[s, g]
            if g < 4:
                v[:] = p[:C, None]; v[:, o[0]] = p[C:2 * C]
            elif g < 6:
                v[:, o[:256]] = p[:C, None]; v[:, o[256:511]] = p[C:2 * C, None]; v[:, o[511:]] = p[rng.integers(2 * C, E, (C, A - 511))]
            else:
                v[:] = p[rng.integers(0, 4, (C, A))]
    return pack(floats(rng, False), q, k, n)
def setup_inputs_calm(rng):
    q, k, n = small(rng); q[:, :, 0] = rng.integers(8, 17, (N, 8, T))
    a = rng.integers(1, 33, (N, 8, T)); q[:, :, 15] = np.where(rng.random((N, 8, T)) < 0.125, -a, a)
    tp = np.argsort(rng.random((8, A)), axis=1)[:, :16]
    for g in range(8): q[tp[g] // T, g, :, tp[g] % T] = np.array([1, 1] + [32] * 13 + [1])
    for s in range(0, N, 2):
        for g in range(8):
            size = np.argsort(rng.random((A // 4, 4)), axis=1).reshape(-1) + 1
            fam = np.repeat(np.arange(size.size), size)[:A]; F = int(fam[-1]) + 1
            p = rng.permutation(E); ex = p[:F * C].reshape(F, C); pair = p[E - 16:].reshape(2, 8)
            n[s, g] = ex[fam[rng.permutation(A)]].T
            k[s, g][:, ex] = rng.integers(-4, 5, (16, F, 1))
            k[s, g, 15][ex] = np.clip(rng.choice(np.array([0, 0, 0, -32, 32]), (F, 1)) + rng.integers(-2, 3, (F, C)), -32, 32)
            lead = rng.random(F) < 0.25; d = rng.integers(0, C, F)
            k[s, g, 0][ex[lead]] = np.where(np.arange(C)[None, :] == d[lead][:, None], 32, -32)
            k[s, g][:, pair[0]] = np.array([32, 31] + [32] * 13 + [-32])[:, None]
            k[s, g][:, pair[1]] = np.array([1 - RO, 1 - RO] + [32] * 13 + [32])[:, None]
            n[s, g][:, tp[g]] = np.where(np.arange(C)[:, None] % 2 == 0, np.repeat(pair[0], 2)[None, :], np.repeat(pair[1], 2)[None, :])
        k[s + 1] = k[s][:, :, (-np.arange(E)) % E]; n[s + 1] = (-n[s]) % E
    return pack(floats(rng, False), q, k, n)
def setup_inputs_corners(rng):
    q, k, n = small(rng)
    q[:, 0] *= (rng.random((N, 1, T)) < 0.5)
    n[:, 1] = n[:, 1, :1]; n[:, 2, C // 2:] = n[:, 2, :C // 2].copy()
    n[:, 3] = rng.choice(np.array([0, 1, E // 2, E - 1]), (N, C, A))
    k[:, 4, :15] = 0; q[:, 4, 15] = rng.choice(np.array([0, 1, -1, 32, -32]), (N, T))
    k[:, 5, :15] = k[:, 5, :15, :1].copy(); q[:, 5, 15] *= (rng.random((N, T)) < 0.75)
    q[:, 6] = rng.integers(-32, 33, (N, 16, T)); k[:, 6] = rng.integers(-32, 33, (N, 16, E))
    k[:, 7] = k[:, 7][:, :, np.arange(E) // 2 * 2]
    k[:, :, 15, 0] = 32; k[:, :, 15, E - 1] = -32
    return pack(lone(rng, floats(rng, False), 6), q, k, n)
def check_ranges(d):
    bad = []
    for a, lo, hi in (("rq", -32, 32), ("ke", -32, 32), ("nm", 0, E - 1)):
        v = np.asarray(d[a]).astype(np.float64)
        if not bool(np.all((v >= lo) & (v <= hi))): bad.append("range of " + a)
        elif not bool(np.all(np.floor(v) == v)): bad.append("whole numbers of " + a)
    for a, lo, hi in (("x0", 0.0625, 1.0), ("ue", 0.0234375, 0.1875), ("ve", 0.125 * VM, VM), ("mm", 0.0, 1.4)):
        v = np.asarray(d[a]).astype(np.float64)
        if not bool(np.all((v >= lo) & (v <= hi))): bad.append("range of " + a)
    if not bool(np.all(np.add.reduce(np.asarray(d["mm"]).astype(np.float64), axis=1) <= 1.4)): bad.append("column sums of mm")
    return bad
def reference(x0, rq, ke, ue, ve, nm, mm):
    q = rq.astype(np.float32).astype(np.int32).reshape(N, 8, 16, T); k = ke.astype(np.float32).astype(np.int32).reshape(N, 8, 16, E)
    n = np.stack([gentries(a) for a in nm]).reshape(N, 8, C, A)
    wins, names, b = route(q, k, n)
    x = np.ascontiguousarray(x0.astype(np.float64).reshape(N, 8, 16, T).transpose(1, 2, 0, 3)).reshape(8, 16, A)
    u = ue.astype(np.float64).reshape(N, 8, 16, E); v = ve.astype(np.float64).reshape(N, 8, 16, E); m = mm.astype(np.float64)
    for l in range(RO):
        y = np.zeros((8, 16, A))
        for s in range(N):
            w = wins[l][s][:, None, :]
            d = np.add.reduce(np.take_along_axis(u[s], w, 2) * x, axis=1)
            y = y + (0.5 * d * (1.0 + np.tanh(0.5 * d)))[:, None, :] * np.take_along_axis(v[s], w, 2)
        z = (0.5 * x + 0.25 * y).reshape(128, N, T)
        x = np.stack([np.tanh(m[r].T @ z[:, r]) for r in range(N)], axis=1).reshape(8, 16, A)
    return {"yx": np.ascontiguousarray(x.reshape(128, N, T).transpose(1, 0, 2)).astype(np.float32), "yb": b.astype(np.float32)}

def check_inputs(d):
    bad = list(check_ranges(d))
    if not bad:
        for name, y in reference(**d).items():
            for q in range(N):
                v = np.abs(np.asarray(y[q], np.float64)); s = np.sqrt(np.mean(v * v))
                if v.max() > 7 * s or s < 2.0 ** -5: bad.append('%s of rank %d is uneven or too small' % (name, q))
    return bad

@@ -1,0 +1,556 @@
+import numpy as np
+from concourse.bass import DstId, RemoteDMATransfer
+from concourse.mybir import dt, AluOpType as A, ActivationFunctionType as F
+
+N, E, TK, RO = 8, 4096, 256, 3
+NV = (2, 2, 2)
+RING = 128
+OW = 136
+KC = 512
+
+SCRATCH = {
+    "kw": ("sbuf", [128, E], "bfloat16"), "uw": ("sbuf", [128, E], "bfloat16"), "vw": ("sbuf", [128, E], "bfloat16"),
+    "qa": ("sbuf", [128, N * TK], "bfloat16"), "nmi": ("sbuf", [128, 256], "int32"), "nmf": ("sbuf", [128, 256], "float32"),
+    "x0b": ("sbuf", [128, TK], "bfloat16"), "mmb": ("sbuf", [128, 128], "bfloat16"), "mmf": ("sbuf", [128, 128], "float32"),
+    "nl": ("sbuf", [128, 256], "uint16"), "wl": ("sbuf", [128, 128], "uint16"),
+    "gk": ("sbuf", [128, 6 * KC], "bfloat16"), "pk": ("sbuf", [128, 8 * KC], "float16"), "pw": ("sbuf", [128, 3 * KC], "float32"),
+    "sel": ("sbuf", [128, 128], "float32"),
+    "u": ("sbuf", [128, 256], "float32"), "du": ("sbuf", [128, 128], "float32"), "bas": ("sbuf", [128, 256], "float16"),
+    "rr": ("sbuf", [128, 256], "bfloat16"), "lo": ("sbuf", [128, 128], "bfloat16"), "hi": ("sbuf", [128, 128], "bfloat16"),
+    "oh": ("sbuf", [128, RING * OW], "bfloat16"), "ms": ("sbuf", [128, 4 * 68], "float32"),
+    "nb": ("sbuf", [128, 256], "bfloat16"), "bp": ("sbuf", [128, 256], "bfloat16"), "bm": ("sbuf", [128, 256], "bfloat16"),
+    "nbf": ("sbuf", [128, 256], "float32"),
+    "pf": ("sbuf", [128, N * TK], "float32"), "tt": ("sbuf", [128, 128], "float32"), "t1": ("sbuf", [128, 128], "float32"),
+    "sg": ("sbuf", [128, 128], "float32"), "hl": ("sbuf", [128, 256], "bfloat16"), "ht": ("sbuf", [128, 256], "bfloat16"),
+    "z": ("sbuf", [128, 1024], "float32"), "xs": ("sbuf", [128, TK], "float32"), "xo": ("sbuf", [128, TK], "float32"),
+    "jj": ("sbuf", [128, 128], "float32"), "ff": ("sbuf", [128, 72], "float32"), "gi": ("sbuf", [128, 8], "float32"),
+    "si": ("sbuf", [128, 1024], "bfloat16"), "sm": ("sbuf", [128, 1024], "bfloat16"),
+    "ta": ("sbuf", [128, 128], "float32"), "tb": ("sbuf", [128, 128], "float32"), "tc": ("sbuf", [128, 128], "float32"),
+    "w1": ("sbuf", [128, 128], "float32"), "w2": ("sbuf", [128, 128], "float32"),
+    "ib": ("sbuf", [128, 128], "bfloat16"), "imb": ("sbuf", [128, 128], "bfloat16"),
+    "i64b": ("sbuf", [128, 128], "bfloat16"), "im4k": ("sbuf", [128, 128], "bfloat16"), "xt": ("sbuf", [128, 256], "float32"),
+    "i64f": ("sbuf", [128, 128], "float32"), "ih": ("sbuf", [128, 128], "float16"),
+    "ga": ("sbuf", [128, 8], "float32"), "bof": ("sbuf", [128, 8], "float32"), "boh": ("sbuf", [128, 8], "float16"),
+    "bon": ("sbuf", [128, 8], "float16"), "cl": ("sbuf", [128, OW], "bfloat16"),
+}
+for _l in range(RO):
+    SCRATCH["st%d" % _l] = ("sbuf", [128, N, 2 * TK], "bfloat16")
+    SCRATCH["ld%d" % _l] = ("sbuf", [128, N, 2 * TK], "bfloat16")
+for _l in range(RO - 1):
+    SCRATCH["wd%d" % _l] = ("sbuf", [128, N * 128], "float16")
+for _b in range(8):
+    SCRATCH["B%d" % _b] = ("psum", [128, 512], "float32")
+
+SEMAPHORES = ["cv", "cs", "ct", "cg", "sent", "lq", "lk", "lu", "lv", "ln", "lx", "lm", "lb", "aq", "oy", "ob"]
+for _l in range(RO):
+    SEMAPHORES += ["aw%d" % _l, "db%d" % _l] + ["a%d_%d" % (_l, _k) for _k in range(4)]
+
+
+def rank_program(g, core, T, topo):
+    rank = T.rank_of(core)
+    if rank is None:
+        return
+    cores = list(T.cores)
+    Q = {"v": g.vector, "s": g.scalar, "t": g.tensor, "g": g, "y": g.sync}
+    ops = []
+    count = {}
+    final = {}
+    lastw, readers, bankq = {}, {}, {}
+
+    def add(q, emit, rd=(), wr=(), banks=(), sem=None, inc=1):
+        deps = []
+        for k in rd:
+            deps += lastw.get(k, [])
+        for k in wr:
+            deps += lastw.get(k, []) + readers.get(k, [])
+        for b in banks:
+            if b in bankq and bankq[b][0] != q:
+                deps.append(bankq[b])
+        whole = sem is not None
+        name = sem if whole else "c" + q
+        count[name] = count.get(name, 0) + inc
+        if whole:
+            final[name] = True
+        me = (q, name, count[name])
+        deps = [d for d in deps if not (q == "t" and d[1] == "ct") and not (whole and d[1] == name)]
+        ops.append((q, emit, name, inc, deps))
+        for k in rd:
+            readers.setdefault(k, []).append(me)
+        for k in wr:
+            lastw[k] = [me]
+            readers[k] = []
+        for b in banks:
+            bankq[b] = me
+
+    S = T.sem
+    B = [T["B%d" % b] for b in range(8)]
+
+    def vts(out, in0, s1, s2, o0, o1, rd, wr, banks=()):
+        if s2 is None:
+            add("v", lambda: g.vector.tensor_scalar(out, in0, s1, None, o0), rd, wr, banks)
+        else:
+            add("v", lambda: g.vector.tensor_scalar(out, in0, s1, s2, o0, o1), rd, wr, banks)
+
+    def vtt(out, a, b, op, rd, wr, banks=()):
+        add("v", lambda: g.vector.tensor_tensor(out, a, b, op), rd, wr, banks)
+
+    def vcp(out, a, rd, wr, banks=()):
+        add("v", lambda: g.vector.tensor_copy(out, a), rd, wr, banks)
+
+    def vms(out, c, wr):
+        add("v", lambda: g.vector.memset(out, c), (), wr)
+
+    def act(out, a, f, rd, wr, banks=(), bias=0.0, scale=1.0):
+        add("s", lambda: g.scalar.activation(out, a, f, bias=bias, scale=scale), rd, wr, banks)
+
+    def mmul(out, lhsT, rhs, start, stop, rd, wr, bank):
+        add("t", lambda: g.tensor.matmul(out, lhsT, rhs, start, stop), rd, wr, (bank,))
+
+    def dma(q, out, in_, rd, wr, sem):
+        add(q, lambda: Q[q].dma_start(out, in_), rd, wr, sem=sem, inc=16)
+
+    def iota(out, pat, base, cm, wr):
+        add("g", lambda: g.iota(out, pat, base, cm, allow_small_or_imprecise_dtypes=True), (), wr)
+
+    def bits(es):
+        return int(sum(1 << e for e in es))
+
+    def dst(c):
+        a = topo.addr(c)
+        return DstId(rid=a[0], pnc=a[1])
+
+    def plan(r0):
+        src = cores[r0]
+        rest = [(r0 + k) % N for k in range(1, N)]
+        near = [r for r in rest if topo.chip(cores[r]) == topo.chip(src)]
+        far = [r for r in rest if r not in near]
+        out = topo.engines(src, cores[far[0]])
+        home = [e for e in topo.engines(src, cores[near[0]]) if e not in out]
+        hf = len(out) // 2
+        calls = [[(far[k], out[:hf]), (far[k + 1], out[hf:])] for k in range(0, len(far), 2)] + [[(r, home) for r in near]]
+        return near, far, out, home, calls
+
+    near, far, eout, ehome, calls = plan(rank)
+    step = {rank: len(calls)}
+    gets = [0] * len(calls)
+    for s in range(N):
+        for k, c in enumerate(plan(s)[4]):
+            for r, es in c:
+                if r == rank:
+                    step[s] = k
+                    gets[k] += len(es)
+    srcs = sorted(range(N), key=lambda s: (step[s] if s != rank else 0.5, s))
+
+    def remote(transfers, engines, rd):
+        def emit():
+            g.remote_dma_fused(transfers, local_sem=S.sent)
+        add("g", emit, rd, (), sem="sent", inc=engines)
+
+    def arrive(sem, n, wr):
+        if n:
+            add("g", None, (), wr, sem=sem, inc=n)
+
+    def send_all(ap, sem, rd):
+        tr = [RemoteDMATransfer(dst_ids=[dst(cores[r]) for r in far], dma_engine_mask=bits(eout), remote_sem=S[sem], srcs=[ap], dsts=[ap] * len(far)),
+              RemoteDMATransfer(dst_ids=[dst(cores[r]) for r in near], dma_engine_mask=bits(ehome), remote_sem=S[sem], srcs=[ap], dsts=[ap] * len(near))]
+        remote(tr, len(eout) + len(ehome), rd)
+        return len(far) * len(eout) + len(near) * len(ehome)
+
+    qown = T.qa[:, rank * TK:(rank + 1) * TK]
+    dma("y", qown, T.rq[:], (), ["qown"], "lq")
+    dma("s", T.nmi[:], T.nm[:], (), ["nmi"], "ln")
+    dma("y", T.kw[:], T.ke[:], (), ["kw"], "lk")
+    iota(T.jj[:], [[1, 128]], 0, -1, ["jj"])
+    iota(T.ff[:], [[1, 72]], 0, 0, ["ff"])
+    iota(T.gi[:], [[-16, 8]], 0, 1, ["gi"])
+    n = send_all(qown, "aq", ["qown"])
+    arrive("aq", n, ["qa"])
+    iota(T.si[:], [[-8, 8], [-1, 8], [0, 16]], 0, 1, ["si"])
+    dma("y", T.uw[:], T.ue[:], ["kw"], ["uw"], "lu")
+    dma("y", T.vw[:], T.ve[:], (), ["vw"], "lv")
+    for j in range(4):
+        dma("y", T.nb[:, j * 64:(j + 1) * 64], T.ke[32 * j + 15:32 * j + 32:16, :], (), ["nb%d" % j], "lb")
+    dma("y", T.x0b[:], T.x0[:], (), ["x0b"], "lx")
+    dma("y", T.mmb[:], T.mm[:], (), ["mmb"], "lm")
+
+    vts(T.i64f[:], T.jj[:], 0.0, 64.0, A.is_equal, A.mult, ["jj"], ["i64f"])
+    vts(T.ga[:], T.gi[:], 0.0, 15.0, A.max, A.min, ["gi"], ["ga"])
+    vts(T.ib[:], T.jj[:], 0.0, None, A.is_equal, None, ["jj"], ["ib"])
+    vts(T.imb[:], T.jj[:], 0.0, -1.0, A.is_equal, A.mult, ["jj"], ["imb"])
+    vts(T.i64b[:], T.jj[:], 0.0, 64.0, A.is_equal, A.mult, ["jj"], ["i64b"])
+    vtt(T.bof[:], T.ga[:], T.gi[:], A.is_equal, ["ga", "gi"], ["bof"])
+    vtt(T.boh[:], T.ga[:], T.gi[:], A.is_equal, ["ga", "gi"], ["boh"])
+    vts(T.im4k[:], T.jj[:], 0.0, -4096.0, A.is_equal, A.mult, ["jj"], ["im4k"])
+    vts(T.ih[:], T.jj[:], 0.0, 1.0 / 64, A.is_equal, A.mult, ["jj"], ["ih"])
+    vts(T.bon[:], T.bof[:], -1.0, None, A.mult, None, ["bof"], ["bon"])
+    vts(T.ta[:], T.jj[:], 1.0, 64.0, A.is_equal, A.mult, ["jj"], ["ta"])
+    vts(T.tb[:], T.jj[:], -1.0, 64.0, A.is_equal, A.mult, ["jj"], ["tb"])
+    vts(T.tc[:], T.jj[:], 0.0, -128.0, A.is_equal, A.mult, ["jj"], ["tc"])
+    vms(T.w1[:], 0.0, ["w1"])
+    vcp(T.nl[:], T.nmi[:], ["nmi"], ["nl"])
+    vcp(T.nmf[:], T.nmi[:], ["nmi"], ["nmf"])
+    vtt(T.ta[:], T.ta[:], T.tb[:], A.add, ["ta", "tb"], ["ta"])
+    vts(T.cl[:, 0:64], T.ff[:, 0:64], -64.0, None, A.add, None, ["ff"], ["cl0"])
+    vts(T.cl[:, 64:130], T.ff[:, 0:66], 1.0 / 64, -65.0 / 128, A.mult, A.add, ["ff"], ["cl1"])
+    for h in (0, 64):
+        vtt(T.w1[h:h + 64, h:h + 64], T.ta[h:h + 64, h:h + 64], T.tc[h:h + 64, h:h + 64], A.add, ["ta", "tc", "w1"], ["w1_%d" % h])
+    for c in range(2):
+        mmul(B[1][:, c * 128:(c + 1) * 128], T.nmf[:, c * 128:(c + 1) * 128], T.i64f[:], True, True, ["nmf", "i64f"], ["xt"], 1)
+    for h in (0, 64):
+        vms(T.w1[h:h + 1, h:h + 1], -64.0, ["w1_%d" % h])
+    act(T.u[:], B[1][:, 0:256], F.Identity, ["xt"], ["u"], (1,), bias=-64.0 - 63.0 / 128, scale=1.0 / 4096)
+    vts(T.w2[:], T.w1[:], -2.0, None, A.mult, None, ["w1", "w1_0", "w1_64"], ["w2"])
+    vts(T.bas[:], B[1][:, 0:256], 1.0 / 64, -2048.0, A.mult, A.add, ["xt"], ["bas"], (1,))
+    vtt(T.du[:], T.u[:, 128:256], T.u[:, 0:128], A.subtract, ["u"], ["du"])
+
+    NB = ["nb%d" % j for j in range(4)]
+    DB = (7, 4)
+
+    def bias_sides():
+        act(T.bp[:], T.nb[:], F.Identity, NB, ["bp"], bias=1.0)
+        act(T.bm[:], T.nb[:], F.Identity, NB, ["bm"], bias=-1.0)
+
+    def first_x():
+        act(T.mmf[:], T.mmb[:], F.Identity, ["mmb"], ["mmf"])
+        act(B[6][:, 0:256], T.x0b[:], F.Identity, ["x0b"], ["x0", "x1"], (6,))
+        act(T.xs[:], T.x0b[:], F.Identity, ["x0b"], ["xs0", "xs1"], scale=0.5)
+
+    def names(c, ch):
+        return T.kw[:].indirect(T.nl[:, c * 128 + ch * 32:c * 128 + (ch + 1) * 32])
+
+    def k_vec(ch):
+        for c in range(2):
+            k = 4 * c + ch
+            vtt(T.pk[:, k * KC:(k + 1) * KC], names(c, ch), T.qa[:, ch * KC:(ch + 1) * KC], A.mult, ["kw", "nl", "qa", "qown"], ["pk%d" % k])
+        for i in range(16):
+            o = B[0][32 * ch:32 * ch + 32, i:128:16]
+            mmul(o, T.pk[:, ch * KC + i:(ch + 1) * KC:16], T.boh[:], True, False, ["pk%d" % ch, "boh"], ["sc"], 0)
+            mmul(o, T.pk[:, (4 + ch) * KC + i:(5 + ch) * KC:16], T.bon[:], False, True, ["pk%d" % (4 + ch), "bon"], ["sc"], 0)
+
+    def k_gather(ch):
+        b = 2 + ch % 2
+        for c in range(2):
+            o = T.gk[:, (2 * ch + c) * KC:(2 * ch + c + 1) * KC]
+            act(o, names(c, ch), F.Identity, ["kw", "nl"], ["gk%d_%d" % (ch, c)])
+            mmul(B[b][:], (T.ib, T.imb)[c][:], o, c == 0, c == 1, ["ib", "imb", "gk%d_%d" % (ch, c)], ["bc%d" % b], b)
+
+    def k_prod(l, ch):
+        b = 2 + ch % 2
+        wide = l == RO - 1
+        p, one = (T.pw, T.bof) if wide else (T.pk, T.boh)
+        vtt(p[:, ch * KC:(ch + 1) * KC], B[b][:], T.qa[:, ch * KC:(ch + 1) * KC], A.mult, ["bc%d" % b, "qa", "qown"], ["pk%d" % ch], (b,))
+        for i in range(16):
+            mmul(B[0][32 * ch:32 * ch + 32, i:128:16], p[:, ch * KC + i:(ch + 1) * KC:16], one[:], True, True, ["pk%d" % ch, "boh", "bof"], ["sc"], 0)
+
+    def landed(l, s):
+        return "own%d" % l if s == rank else "ld%d_%d" % (l, step[s])
+
+    def f_p(l, h, ss):
+        for s in ss:
+            o = s * TK + h * 128
+            vtt(T.pf[:, o:o + 128], T["ld%d" % l][:, s, h * 128:(h + 1) * 128], B[6][:, h * 128:(h + 1) * 128], A.mult,
+                [landed(l, s), "x%d" % h], ["pf%d_%d" % (h, s)], (6,))
+            mmul(B[DB[h]][:, s * 8:(s + 1) * 8], T.pf[:, o:o + 128], T.bof[:], True, True, ["pf%d_%d" % (h, s), "bof"], ["d%d" % h], DB[h])
+
+    def f_tanh(h):
+        c = slice(h * 64, (h + 1) * 64)
+        act(T.tt[:, c], B[DB[h]][:, 0:64], F.Tanh, ["d%d" % h], ["tt%d" % h], (DB[h],), scale=0.5)
+        act(T.t1[:, c], T.tt[:, c], F.Identity, ["tt%d" % h], ["t1%d" % h], bias=0.125, scale=0.125)
+
+    def f_sig(h):
+        c = slice(h * 64, (h + 1) * 64)
+        vtt(T.sg[:, c], B[DB[h]][:, 0:64], T.t1[:, c], A.mult, ["d%d" % h, "t1%d" % h], ["sg%d" % h], (DB[h],))
+        vtt(T.hl[:, h * 128:h * 128 + 64], B[DB[h]][:, 0:64], T.t1[:, c], A.mult, ["d%d" % h, "t1%d" % h], ["hh%d" % h], (DB[h],))
+
+    def f_lo(h):
+        c = slice(h * 64, (h + 1) * 64)
+        vtt(T.hl[:, h * 128 + 64:h * 128 + 128], T.sg[:, c], T.hl[:, h * 128:h * 128 + 64], A.subtract, ["sg%d" % h, "hh%d" % h], ["ll%d" % h])
+        mmul(B[DB[h]][:, 128:256], T.hl[:, h * 128:(h + 1) * 128], T.ib[:], True, True, ["hh%d" % h, "ll%d" % h, "ib"], ["tr%d" % h], DB[h])
+
+    def f_ht(h):
+        act(T.ht[:, h * 128:(h + 1) * 128], B[DB[h]][:, 128:256], F.Identity, ["tr%d" % h], ["ht%d" % h], (DB[h],))
+
+    def f_bc(h, yb):
+        for s in range(8):
+            b = yb[s // 4]
+            mmul(B[b][:, (s % 4) * 128:(s % 4 + 1) * 128], T.sm[:, s * 128:(s + 1) * 128], T.ht[:, h * 128:(h + 1) * 128], True, True,
+                 ["sm0", "sm1", "ht%d" % h], ["bc%d" % b], b)
+
+    def f_y(l, h, part, yb):
+        a, b = yb
+        ld = T["ld%d" % l]
+        z = T.z[:, h * 512:(h + 1) * 512]
+        c = slice(TK + h * 128, TK + (h + 1) * 128)
+        if part == 0:
+            vtt(z, B[a][:], ld[:, 0:4, c], A.mult, [landed(l, s) for s in range(4)] + ["bc%d" % a], ["z%d" % h], (a,))
+        elif part == 1:
+            vtt(B[b][:], B[b][:], ld[:, 4:8, c], A.mult, [landed(l, s) for s in range(4, 8)] + ["bc%d" % b], ["bc%d" % b], (b,))
+        else:
+            vtt(z, z, B[b][:], A.add, ["z%d" % h, "bc%d" % b], ["z%d" % h], (b,))
+
+    def f_mix(h):
+        o = B[DB[h]][:, 256:384]
+        c = slice(h * 128, (h + 1) * 128)
+        mmul(o, T.mmf[:], T.xs[:, c], True, False, ["mmf", "xs%d" % h], ["mx%d" % h], DB[h])
+        for k in range(4):
+            mmul(o, T.mmf[:], T.z[:, h * 512 + k * 128:h * 512 + (k + 1) * 128], False, k == 3, ["mmf", "z%d" % h], ["mx%d" % h], DB[h])
+
+    def f_out(l, h):
+        o = B[DB[h]][:, 256:384]
+        c = slice(h * 128, (h + 1) * 128)
+        if l < RO - 1:
+            act(B[6][:, c], o, F.Tanh, ["mx%d" % h], ["x%d" % h], (DB[h], 6))
+            act(T.xs[:, c], B[6][:, c], F.Identity, ["x%d" % h], ["xs%d" % h], (6,), scale=0.5)
+        else:
+            act(T.xo[:, c], o, F.Tanh, ["mx%d" % h], ["xo%d" % h], (DB[h],))
+            dma("y" if h == 0 else "s", T.yx[:, c], T.xo[:, c], ["xo%d" % h], (), "oy")
+
+    def pick(l, r):
+        buf = T[("ld%d" if r == rank else "st%d") % l]
+        for half, win in enumerate((T.uw, T.vw)):
+            key = "st%d_%d_%d" % (l, r, half)
+            act(buf[:, r, half * TK:(half + 1) * TK], win[:].indirect(T.wl[:, r * 16:(r + 1) * 16]), F.Identity, ["wl", "uv"[half] + "w"],
+                [key] + (["own%d" % l] if r == rank else []))
+
+    def hand(l, k):
+        if k == len(calls):
+            pick(l, rank)
+            return
+        tr, rd = [], []
+        sem = "a%d_%d" % (l, k)
+        for r, es in calls[k]:
+            pick(l, r)
+            rd += ["st%d_%d_%d" % (l, r, half) for half in range(2)]
+            tr.append(RemoteDMATransfer(dst_ids=[dst(cores[r])], dma_engine_mask=bits(es), remote_sem=S[sem],
+                                        src=T["st%d" % l][:, r, :], dst=T["ld%d" % l][:, rank, :]))
+        remote(tr, sum(len(es) for r, es in calls[k]), rd)
+        arrive(sem, gets[k], ["ld%d_%d" % (l, k)])
+
+    slot = [0]
+
+    def count_group(gr, i0=0, i1=16):
+        b, p0 = 2 + (gr // 2) % 2, (gr % 2) * 64
+        for i in range(i0, i1):
+            k = slot[0] % RING
+            slot[0] += 1
+            col = gr * 16 + i
+            o = k * OW
+            vts(T.oh[:, o:o + 130], T.cl[:, 0:130], T.lo[:, col:col + 1], T.hi[:, col:col + 1], A.max, A.min,
+                ["cl0", "cl1", "lo", "hi"], ["oh%d" % k])
+            mmul(B[b][p0:p0 + 64, 0:66], T.oh[:, o:o + 64], T.oh[:, o + 64:o + 130], i == 0, i == 15, ["oh%d" % k], ["bc%d" % b], b)
+
+    def copy_m(j):
+        b = 2 + j % 2
+        act(T.ms[:, j * 68:j * 68 + 66], B[b][:, 0:66], F.Identity, ["bc%d" % b], ["ms%d" % j], (b,))
+
+    def diffs(j):
+        o = B[5][:, j * 64:(j + 1) * 64]
+        mmul(o, T.ib[:], T.bp[:, j * 64:(j + 1) * 64], True, False, ["ib", "bp"], ["bc5"], 5)
+        for k, w in ((0, "w1"), (1, "w2"), (2, "w1")):
+            mmul(o, T[w][:], T.ms[:, j * 68 + k:j * 68 + k + 64], False, k == 2, ["w1", "w1_0", "w1_64", "w2", "ms%d" % j], ["bc5"], 5)
+
+    def new_bias(l, j):
+        c = slice(j * 64, (j + 1) * 64)
+        if l == RO - 1:
+            vtt(T.nbf[:, c], B[5][:, c], T.bm[:, c], A.max, ["bc5", "bm"], ["nbf%d" % j], (5,))
+            dma("y", T.yb[2 * j:2 * j + 2, :], T.nbf[:, c], ["nbf%d" % j], (), "ob")
+        else:
+            vtt(T.nb[:, c], B[5][:, c], T.bm[:, c], A.max, ["bc5", "bm"], ["nb%d" % j], (5,))
+            dma("y", T.kw[32 * j + 15:32 * j + 32:16, :], T.nb[:, c], ["nb%d" % j], ["kw"], "db%d" % l)
+
+    def names_sum(l):
+        wd = T["wd%d" % l]
+        for c in range(2):
+            o = B[1][:, c * 128:(c + 1) * 128]
+            mmul(o, T.ih[:], T.bas[:, c * 128:(c + 1) * 128], True, False, ["ih", "bas"], ["xt"], 1)
+            for s in range(N):
+                mmul(o, T.ih[:], wd[:, s * 128:(s + 1) * 128], False, s == N - 1, ["ih", "wd%d" % l, "wa%d" % l, "wb%d" % l], ["xt"], 1)
+
+    EARLY = 3
+    for l in range(RO):
+        last = l == RO - 1
+        f = l - 1
+        ps = srcs[EARLY:] if f == 0 else srcs
+        hp = len(ps) // 2
+        if f >= 1:
+            f_out(f - 1, 0)
+        two = NV[l] == 2
+        k_gather(0)
+        k_vec(3)
+        if f >= 0:
+            vtt(T.du[:], T.u[:, 128:256], T.u[:, 0:128], A.subtract, ["u"], ["du"])
+        if f >= 1:
+            f_out(f - 1, 1)
+        k_gather(1)
+        k_prod(l, 0)
+        if two:
+            k_vec(2)
+        else:
+            if f >= 0:
+                f_p(f, 0, ps[:hp])
+            k_gather(2)
+        k_prod(l, 1)
+        if f >= 0:
+            f_p(f, 0, ps if two else ps[hp:])
+            f_tanh(0)
+        else:
+            bias_sides()
+            first_x()
+        if not two:
+            k_prod(l, 2)
+            if f >= 0:
+                f_p(f, 1, ps)
+                f_tanh(1)
+        fill = [lambda: None] * 4
+        if f >= 0 and two:
+            fill = [lambda: f_p(f, 1, ps[:2]), lambda: f_sig(0), lambda: f_lo(0), lambda: f_ht(0)]
+        elif f >= 0:
+            fill = [lambda: f_sig(0), lambda: f_lo(0), lambda: f_sig(1), lambda: (f_lo(1), f_ht(0))]
+        vts(T.sel[:], B[0][:, 0:128], 0.0, None, A.is_lt, None, ["sc"], ["sel"], (0,))
+        fill[0]()
+        vtt(B[0][:, 256:384], T.sel[:], T.du[:], A.mult, ["sel", "du"], ["tw"], (0,))
+        fill[1]()
+        vtt(B[0][:, 384:512], B[0][:, 256:384], T.u[:, 0:128], A.add, ["tw", "u"], ["uw_"], (0,))
+        fill[2]()
+        vts(T.lo[:], B[0][:, 384:512], 12582912.0, 12582912.0, A.add, A.subtract, ["uw_"], ["lo"], (0,))
+        if not last:
+            wo = rank * 128
+            wd = T["wd%d" % l]
+            vts(wd[:, wo + 16:wo + 128], B[0][:, 384:496], 64.0, 2079.5, A.mult, A.add, ["uw_"], ["wa%d" % l], (0,))
+            vts(wd[:, wo:wo + 16], B[0][:, 496:512], 64.0, 2079.5, A.mult, A.add, ["uw_"], ["wb%d" % l], (0,))
+            n = send_all(wd[:, wo:wo + 128], "aw%d" % l, ["wa%d" % l, "wb%d" % l])
+            arrive("aw%d" % l, n, ["wd%d" % l])
+        vtt(T.hi[:], B[0][:, 384:512], T.lo[:], A.subtract, ["uw_", "lo"], ["hi"], (0,))
+        mmul(B[6][:, 256:384], T.lo[:], T.i64b[:], True, False, ["lo", "i64b"], ["wt"], 6)
+        mmul(B[6][:, 256:384], T.hi[:], T.i64b[:], False, True, ["hi", "i64b"], ["wt"], 6)
+        fill[3]()
+        count_group(0, 0, 3)
+        vts(T.wl[:], B[6][:, 256:384], 4127.5, None, A.add, None, ["wt"], ["wl"], (6,))
+        if f >= 0 and two:
+            f_p(f, 1, ps[2:])
+            hand(l, 0)
+            f_tanh(1)
+            count_group(0, 3)
+            count_group(1, 0, 8)
+            f_sig(1)
+            count_group(1, 8, 10)
+            f_lo(1)
+            f_ht(1)
+            bias_sides()
+        else:
+            if f >= 0:
+                f_ht(1)
+                bias_sides()
+            hand(l, 0)
+            count_group(0, 3)
+            count_group(1, 0, 10)
+        if f >= 0:
+            f_bc(0, (0, 4))
+        if last:
+            f_bc(1, (1, 5))
+        hand(l, 1)
+        count_group(1, 10)
+        copy_m(0)
+        hand(l, 2)
+        if last:
+            for h, yb in ((0, (0, 4)), (1, (1, 5))):
+                for part in range(3):
+                    f_y(f, h, part, yb)
+                f_mix(h)
+            f_out(f, 0)
+            f_out(f, 1)
+            hand(l, 3)
+            hand(l, 4)
+        count_group(2)
+        count_group(3)
+        diffs(0)
+        copy_m(1)
+        count_group(4)
+        new_bias(l, 0)
+        count_group(5)
+        diffs(1)
+        copy_m(2)
+        if not last:
+            hand(l, 3)
+        count_group(6)
+        new_bias(l, 1)
+        diffs(2)
+        if not last:
+            names_sum(l)
+            act(T.rr[:], B[1][:, 0:256], F.Identity, ["xt"], ["rr"], (1,), bias=140.0 + 2.0 ** -13, scale=1.0 / 64)
+            act(T.xt[:], B[1][:, 0:256], F.Identity, ["xt"], ["xts"], (1,))
+        count_group(7)
+        new_bias(l, 2)
+        copy_m(3)
+        diffs(3)
+        if not last:
+            for c in range(2):
+                o = B[1][:, 256 + c * 128:384 + c * 128]
+                mmul(o, T.xt[:, c * 128:(c + 1) * 128], T.i64f[:], True, False, ["xts", "i64f"], ["xl"], 1)
+                mmul(o, T.rr[:, c * 128:(c + 1) * 128], T.im4k[:], False, True, ["rr", "im4k"], ["xl"], 1)
+            hand(l, 4)
+            if f >= 0:
+                f_bc(1, (2, 3))
+                for part in range(3):
+                    f_y(f, 0, part, (0, 4))
+            else:
+                vts(T.sm[0:64, :], T.si[0:64, :], 0.0, None, A.is_equal, None, ["si"], ["sm0"])
+                vts(T.sm[64:128, :], T.si[64:128, :], 64.0, None, A.is_equal, None, ["si"], ["sm1"])
+            new_bias(l, 3)
+            vts(T.nl[:], B[1][:, 256:512], 575488.0, None, A.add, None, ["xl"], ["nl"], (1,))
+            if f >= 0:
+                f_mix(0)
+            mmul(B[1][:, 0:256], T.i64f[:], T.xt[:], True, False, ["i64f", "xts"], ["xt"], 1)
+            mmul(B[1][:, 0:256], T.im4k[:], T.rr[:], False, True, ["im4k", "rr"], ["xt"], 1)
+            act(T.u[:], B[1][:, 0:256], F.Identity, ["xt"], ["u"], (1,), bias=8928.0 - 63.0 / 128, scale=1.0 / 64)
+            if f >= 0:
+                for part in range(3):
+                    f_y(f, 1, part, (2, 3))
+                f_mix(1)
+            else:
+                f_p(l, 0, srcs[:EARLY])
+                f_p(l, 1, srcs[:EARLY])
+        else:
+            f_p(l, 0, srcs)
+            new_bias(l, 3)
+            f_tanh(0)
+            f_p(l, 1, srcs[:4])
+            f_sig(0)
+            f_p(l, 1, srcs[4:6])
+            f_lo(0)
+            f_ht(0)
+            f_p(l, 1, srcs[6:])
+            f_tanh(1)
+            f_bc(0, (0, 1))
+            f_y(l, 0, 0, (0, 1))
+            f_sig(1)
+            f_y(l, 0, 1, (0, 1))
+            f_lo(1)
+            f_ht(1)
+            f_bc(1, (2, 3))
+            f_y(l, 0, 2, (0, 1))
+            f_mix(0)
+            f_out(l, 0)
+            for part in range(3):
+                f_y(l, 1, part, (2, 3))
+            f_mix(1)
+            f_out(l, 1)
+
+    seen = {q: {} for q in Q}
+    for q, emit, name, inc, deps in ops:
+        if emit is None:
+            continue
+        need = {}
+        for d in deps:
+            v = count[d[1]] if d[1] in final else d[2]
+            need[d[1]] = max(need.get(d[1], 0), v)
+        for k, v in need.items():
+            if seen[q].get(k, 0) < v:
+                Q[q].wait_ge(S[k], v)
+                seen[q][k] = v
+        ins = emit()
+        if ins is not None:
+            ins.then_inc(S[name], inc)
+    for k, v in count.items():
+        if seen["g"].get(k, 0) < v:
+            g.wait_ge(S[k], v)

@@ -13,7 +13,7 @@ SCRATCH = {
     "qa": ("sbuf", [128, N * TK], "bfloat16"), "nmi": ("sbuf", [128, 256], "int32"), "nmf": ("sbuf", [128, 256], "float32"),
     "x0b": ("sbuf", [128, TK], "bfloat16"), "mmb": ("sbuf", [128, 128], "bfloat16"), "mmf": ("sbuf", [128, 128], "float32"),
     "nl": ("sbuf", [128, 256], "uint16"), "wl": ("sbuf", [128, 128], "uint16"),
-    "gk": ("sbuf", [128, 6 * KC], "bfloat16"), "pk": ("sbuf", [128, 8 * KC], "float16"), "pw": ("sbuf", [128, 3 * KC], "float32"),
+    "gk": ("sbuf", [128, 8 * KC], "bfloat16"), "pk": ("sbuf", [128, 8 * KC], "float16"), "pw": ("sbuf", [128, 3 * KC], "float32"),
     "sel": ("sbuf", [128, 128], "float32"),
     "u": ("sbuf", [128, 256], "float32"), "du": ("sbuf", [128, 128], "float32"), "bas": ("sbuf", [128, 256], "float16"),
     "rr": ("sbuf", [128, 256], "bfloat16"), "lo": ("sbuf", [128, 128], "bfloat16"), "hi": ("sbuf", [128, 128], "bfloat16"),
@@ -48,9 +48,46 @@ for _l in range(RO):
 
 def rank_program(g, core, T, topo):
     rank = T.rank_of(core)
-    if rank is None:
-        return
     cores = list(T.cores)
+
+    def bits(es):
+        return int(sum(1 << e for e in es))
+
+    def dst(c):
+        a = topo.addr(c)
+        return DstId(rid=a[0], pnc=a[1])
+
+    def plan(r0):
+        src = cores[r0]
+        rest = [(r0 + k) % N for k in range(1, N)]
+        near = [r for r in rest if topo.chip(cores[r]) == topo.chip(src)]
+        far = [r for r in rest if r not in near]
+        out = topo.engines(src, cores[far[0]])
+        home = [e for e in topo.engines(src, cores[near[0]]) if e not in out]
+        free = [c for c in topo.cores_of(src) if c not in cores and topo.die(c) == topo.die(src)]
+        free.sort(key=lambda c: sum(topo.may_write(c, cores[r]) for r in far))
+        straight = [r for r in far if topo.die(cores[r]) == topo.die(src)]
+        calls = []
+        for a in straight:
+            b = [r for r in far if r != a and topo.chip(cores[r]) == topo.chip(cores[a])][0]
+            calls.append([(b, home, [c for c in free if topo.may_write(c, cores[b])][0]), (a, out, None)])
+        calls.append([(r, home, None) for r in near])
+        return near, far, out, home, calls
+
+    if rank is None:
+        jobs = [(r0, k, r, es) for r0 in range(N) for k, c in enumerate(plan(r0)[4]) for r, es, h in c if h == core]
+        left = 0
+        for l in range(RO):
+            for r0, k, r, es in jobs:
+                out = topo.engines(core, cores[r])
+                a = topo.addr(cores[r])
+                sem = T.sem["a%d_%d" % (l, k)]
+                g.wait_ge(sem, len(es))
+                g.remote_dma(T["ld%d" % l][:, r0, :], T["st%d" % l][:, r, :], sem, T.sem.sent, a[1], a[0], bits(out))
+                left += len(out)
+        if left:
+            g.wait_ge(T.sem.sent, left)
+        return
     Q = {"v": g.vector, "s": g.scalar, "t": g.tensor, "g": g, "y": g.sync}
     ops = []
     count = {}
@@ -112,33 +149,15 @@ def rank_program(g, core, T, topo):
     def iota(out, pat, base, cm, wr):
         add("g", lambda: g.iota(out, pat, base, cm, allow_small_or_imprecise_dtypes=True), (), wr)
 
-    def bits(es):
-        return int(sum(1 << e for e in es))
-
-    def dst(c):
-        a = topo.addr(c)
-        return DstId(rid=a[0], pnc=a[1])
-
-    def plan(r0):
-        src = cores[r0]
-        rest = [(r0 + k) % N for k in range(1, N)]
-        near = [r for r in rest if topo.chip(cores[r]) == topo.chip(src)]
-        far = [r for r in rest if r not in near]
-        out = topo.engines(src, cores[far[0]])
-        home = [e for e in topo.engines(src, cores[near[0]]) if e not in out]
-        hf = len(out) // 2
-        calls = [[(far[k], out[:hf]), (far[k + 1], out[hf:])] for k in range(0, len(far), 2)] + [[(r, home) for r in near]]
-        return near, far, out, home, calls
-
     near, far, eout, ehome, calls = plan(rank)
     step = {rank: len(calls)}
     gets = [0] * len(calls)
     for s in range(N):
         for k, c in enumerate(plan(s)[4]):
-            for r, es in c:
+            for r, es, h in c:
                 if r == rank:
                     step[s] = k
-                    gets[k] += len(es)
+                    gets[k] += len(es) if h is None else len(topo.engines(h, core))
     srcs = sorted(range(N), key=lambda s: (step[s] if s != rank else 0.5, s))
 
     def remote(transfers, engines, rd):
@@ -218,24 +237,25 @@ def rank_program(g, core, T, topo):
     def names(c, ch):
         return T.kw[:].indirect(T.nl[:, c * 128 + ch * 32:c * 128 + (ch + 1) * 32])
 
-    def k_vec(ch):
-        for c in range(2):
+    def k_vec(ch, gather=True, mm=True):
+        for c in range(2 if gather else 0):
             k = 4 * c + ch
             vtt(T.pk[:, k * KC:(k + 1) * KC], names(c, ch), T.qa[:, ch * KC:(ch + 1) * KC], A.mult, ["kw", "nl", "qa", "qown"], ["pk%d" % k])
-        for i in range(16):
+        for i in range(16 if mm else 0):
             o = B[0][32 * ch:32 * ch + 32, i:128:16]
             mmul(o, T.pk[:, ch * KC + i:(ch + 1) * KC:16], T.boh[:], True, False, ["pk%d" % ch, "boh"], ["sc"], 0)
             mmul(o, T.pk[:, (4 + ch) * KC + i:(5 + ch) * KC:16], T.bon[:], False, True, ["pk%d" % (4 + ch), "bon"], ["sc"], 0)
 
-    def k_gather(ch):
-        b = 2 + ch % 2
+    def k_gather(ch, b, vec=False):
         for c in range(2):
             o = T.gk[:, (2 * ch + c) * KC:(2 * ch + c + 1) * KC]
-            act(o, names(c, ch), F.Identity, ["kw", "nl"], ["gk%d_%d" % (ch, c)])
+            if vec:
+                vcp(o, names(c, ch), ["kw", "nl"], ["gk%d_%d" % (ch, c)])
+            else:
+                act(o, names(c, ch), F.Identity, ["kw", "nl"], ["gk%d_%d" % (ch, c)])
             mmul(B[b][:], (T.ib, T.imb)[c][:], o, c == 0, c == 1, ["ib", "imb", "gk%d_%d" % (ch, c)], ["bc%d" % b], b)
 
-    def k_prod(l, ch):
-        b = 2 + ch % 2
+    def k_prod(l, ch, b):
         wide = l == RO - 1
         p, one = (T.pw, T.bof) if wide else (T.pk, T.boh)
         vtt(p[:, ch * KC:(ch + 1) * KC], B[b][:], T.qa[:, ch * KC:(ch + 1) * KC], A.mult, ["bc%d" % b, "qa", "qown"], ["pk%d" % ch], (b,))
@@ -318,12 +338,15 @@ def rank_program(g, core, T, topo):
             return
         tr, rd = [], []
         sem = "a%d_%d" % (l, k)
-        for r, es in calls[k]:
+        for r, es, h in calls[k]:
             pick(l, r)
             rd += ["st%d_%d_%d" % (l, r, half) for half in range(2)]
-            tr.append(RemoteDMATransfer(dst_ids=[dst(cores[r])], dma_engine_mask=bits(es), remote_sem=S[sem],
-                                        src=T["st%d" % l][:, r, :], dst=T["ld%d" % l][:, rank, :]))
-        remote(tr, sum(len(es) for r, es in calls[k]), rd)
+            src = T["st%d" % l][:, r, :]
+            if h is None:
+                tr.append(RemoteDMATransfer(dst_ids=[dst(cores[r])], dma_engine_mask=bits(es), remote_sem=S[sem], src=src, dst=T["ld%d" % l][:, rank, :]))
+            else:
+                tr.append(RemoteDMATransfer(dst_ids=[dst(h)], dma_engine_mask=bits(es), remote_sem=S[sem], src=src, dst=src))
+        remote(tr, sum(len(c[1]) for c in calls[k]), rd)
         arrive(sem, gets[k], ["ld%d_%d" % (l, k)])
 
     slot = [0]
@@ -372,38 +395,49 @@ def rank_program(g, core, T, topo):
         f = l - 1
         ps = srcs[EARLY:] if f == 0 else srcs
         hp = len(ps) // 2
-        if f >= 1:
-            f_out(f - 1, 0)
-        two = NV[l] == 2
-        k_gather(0)
-        k_vec(3)
-        if f >= 0:
-            vtt(T.du[:], T.u[:, 128:256], T.u[:, 0:128], A.subtract, ["u"], ["du"])
-        if f >= 1:
-            f_out(f - 1, 1)
-        k_gather(1)
-        k_prod(l, 0)
-        if two:
-            k_vec(2)
-        else:
-            if f >= 0:
-                f_p(f, 0, ps[:hp])
-            k_gather(2)
-        k_prod(l, 1)
-        if f >= 0:
-            f_p(f, 0, ps if two else ps[hp:])
-            f_tanh(0)
-        else:
+        two = True
+        if f < 0:
+            k_gather(0, 2)
+            k_gather(2, 4, vec=True)
+            k_gather(1, 3)
+            k_gather(3, 7, vec=True)
+            for ch, b in ((0, 2), (2, 4), (1, 3), (3, 7)):
+                k_prod(l, ch, b)
             bias_sides()
             first_x()
-        if not two:
-            k_prod(l, 2)
-            if f >= 0:
-                f_p(f, 1, ps)
-                f_tanh(1)
+        else:
+            k_gather(0, 2)
+            k_vec(3)
+            if f >= 1:
+                f_out(f - 1, 0)
+            k_gather(1, 3)
+            vtt(T.du[:], T.u[:, 128:256], T.u[:, 0:128], A.subtract, ["u"], ["du"])
+            if NV[l] == 2:
+                if f >= 1:
+                    f_out(f - 1, 1)
+                k_vec(2, mm=False)
+                k_prod(l, 0, 2)
+                k_vec(2, gather=False)
+                k_prod(l, 1, 3)
+                f_p(f, 0, ps)
+                f_tanh(0)
+            else:
+                k_prod(l, 0, 2)
+                k_gather(2, 2)
+                if f >= 1:
+                    f_out(f - 1, 1)
+                f_p(f, 0, ps[:-1])
+                k_prod(l, 1, 3)
+                f_p(f, 0, ps[-1:])
+                if f == 0:
+                    f_p(f, 1, ps[3:])
+                k_prod(l, 2, 2)
+                f_tanh(0)
+                if f > 0:
+                    f_p(f, 1, ps[3:])
         fill = [lambda: None] * 4
         if f >= 0 and two:
-            fill = [lambda: f_p(f, 1, ps[:2]), lambda: f_sig(0), lambda: f_lo(0), lambda: f_ht(0)]
+            fill = [lambda: f_p(f, 1, ps[0:1]), lambda: f_p(f, 1, ps[1:2]), lambda: f_p(f, 1, ps[2:3]), lambda: None]
         elif f >= 0:
             fill = [lambda: f_sig(0), lambda: f_lo(0), lambda: f_sig(1), lambda: (f_lo(1), f_ht(0))]
         vts(T.sel[:], B[0][:, 0:128], 0.0, None, A.is_lt, None, ["sc"], ["sel"], (0,))
@@ -427,16 +461,18 @@ def rank_program(g, core, T, topo):
         count_group(0, 0, 3)
         vts(T.wl[:], B[6][:, 256:384], 4127.5, None, A.add, None, ["wt"], ["wl"], (6,))
         if f >= 0 and two:
-            f_p(f, 1, ps[2:])
+            f_sig(0)
+            if NV[l] == 2:
+                f_p(f, 1, ps[3:])
+            else:
+                count_group(0, 3, 5)
+            f_lo(0)
             hand(l, 0)
             f_tanh(1)
-            count_group(0, 3)
-            count_group(1, 0, 8)
-            f_sig(1)
-            count_group(1, 8, 10)
-            f_lo(1)
-            f_ht(1)
+            f_ht(0)
             bias_sides()
+            count_group(0, 3 if NV[l] == 2 else 5)
+            count_group(1, 0, 10)
         else:
             if f >= 0:
                 f_ht(1)
@@ -444,30 +480,38 @@ def rank_program(g, core, T, topo):
             hand(l, 0)
             count_group(0, 3)
             count_group(1, 0, 10)
+        hand(l, 1)
+        count_group(1, 10)
         if f >= 0:
+            f_sig(1)
+        count_group(2, 0, 2)
+        if f >= 0:
+            f_lo(1)
+        copy_m(0)
+        count_group(2, 2, 8)
+        if f >= 0:
+            f_ht(1)
             f_bc(0, (0, 4))
         if last:
             f_bc(1, (1, 5))
-        hand(l, 1)
-        count_group(1, 10)
-        copy_m(0)
         hand(l, 2)
+        count_group(2, 8)
+        count_group(3, 0, 8)
         if last:
             for h, yb in ((0, (0, 4)), (1, (1, 5))):
                 for part in range(3):
                     f_y(f, h, part, yb)
                 f_mix(h)
+            hand(l, 3)
             f_out(f, 0)
             f_out(f, 1)
-            hand(l, 3)
             hand(l, 4)
-        count_group(2)
-        count_group(3)
+        count_group(3, 8)
         diffs(0)
         copy_m(1)
         count_group(4)
-        new_bias(l, 0)
         count_group(5)
+        new_bias(l, 0)
         diffs(1)
         copy_m(2)
         if not last:
@@ -484,31 +528,34 @@ def rank_program(g, core, T, topo):
         copy_m(3)
         diffs(3)
         if not last:
+            if f >= 0:
+                f_bc(1, (2, 3))
             for c in range(2):
                 o = B[1][:, 256 + c * 128:384 + c * 128]
                 mmul(o, T.xt[:, c * 128:(c + 1) * 128], T.i64f[:], True, False, ["xts", "i64f"], ["xl"], 1)
                 mmul(o, T.rr[:, c * 128:(c + 1) * 128], T.im4k[:], False, True, ["rr", "im4k"], ["xl"], 1)
             hand(l, 4)
             if f >= 0:
-                f_bc(1, (2, 3))
                 for part in range(3):
                     f_y(f, 0, part, (0, 4))
             else:
                 vts(T.sm[0:64, :], T.si[0:64, :], 0.0, None, A.is_equal, None, ["si"], ["sm0"])
                 vts(T.sm[64:128, :], T.si[64:128, :], 64.0, None, A.is_equal, None, ["si"], ["sm1"])
             new_bias(l, 3)
+            if f >= 0:
+                f_y(f, 1, 0, (2, 3))
+            else:
+                f_p(l, 0, srcs[:EARLY])
             vts(T.nl[:], B[1][:, 256:512], 575488.0, None, A.add, None, ["xl"], ["nl"], (1,))
+            mmul(B[5][:, 256:512], T.i64f[:], T.xt[:], True, False, ["i64f", "xts"], ["xu"], 5)
+            mmul(B[5][:, 256:512], T.im4k[:], T.rr[:], False, True, ["im4k", "rr"], ["xu"], 5)
+            act(T.u[:], B[5][:, 256:512], F.Identity, ["xu"], ["u"], (5,), bias=8928.0 - 63.0 / 128, scale=1.0 / 64)
             if f >= 0:
                 f_mix(0)
-            mmul(B[1][:, 0:256], T.i64f[:], T.xt[:], True, False, ["i64f", "xts"], ["xt"], 1)
-            mmul(B[1][:, 0:256], T.im4k[:], T.rr[:], False, True, ["im4k", "rr"], ["xt"], 1)
-            act(T.u[:], B[1][:, 0:256], F.Identity, ["xt"], ["u"], (1,), bias=8928.0 - 63.0 / 128, scale=1.0 / 64)
-            if f >= 0:
-                for part in range(3):
+                for part in (1, 2):
                     f_y(f, 1, part, (2, 3))
                 f_mix(1)
             else:
-                f_p(l, 0, srcs[:EARLY])
                 f_p(l, 1, srcs[:EARLY])
         else:
             f_p(l, 0, srcs)

@@ -3,47 +3,71 @@ from concourse.bass import DstId, RemoteDMATransfer
 from concourse.mybir import dt, AluOpType as A, ActivationFunctionType as F
 
 N, E, TK, RO = 8, 4096, 256, 3
-NV = (2, 2, 2)
-RING = 128
 OW = 136
 KC = 512
+FUSED = ((), (2, 3), (2, 3))
+VGATH = ((2, 3), (), ())
+SGROUPS = ((), (), (3, 5, 7))
+VPICK = ((), (), ((1, 0), (4, 0), (1, 1)))
+FOLD = (False, False, False)
+SPLIT = (False, False, True)
+TURN = (0, 1, 2)
+ADDV = ((1, 1), (1, 1), (1, 0))
 
 SCRATCH = {
     "kw": ("sbuf", [128, E], "bfloat16"), "uw": ("sbuf", [128, E], "bfloat16"), "vw": ("sbuf", [128, E], "bfloat16"),
-    "qa": ("sbuf", [128, N * TK], "bfloat16"), "nmi": ("sbuf", [128, 256], "int32"), "nmf": ("sbuf", [128, 256], "float32"),
+    "qa": ("sbuf", [128, N * TK], "bfloat16"), "nmi": ("sbuf", [128, 256], "int32"),
     "x0b": ("sbuf", [128, TK], "bfloat16"), "mmb": ("sbuf", [128, 128], "bfloat16"), "mmf": ("sbuf", [128, 128], "float32"),
     "nl": ("sbuf", [128, 256], "uint16"), "wl": ("sbuf", [128, 128], "uint16"),
-    "gk": ("sbuf", [128, 8 * KC], "bfloat16"), "pk": ("sbuf", [128, 8 * KC], "float16"), "pw": ("sbuf", [128, 3 * KC], "float32"),
-    "sel": ("sbuf", [128, 128], "float32"),
-    "u": ("sbuf", [128, 256], "float32"), "du": ("sbuf", [128, 128], "float32"), "bas": ("sbuf", [128, 256], "float16"),
+    "nm0": ("sbuf", [128, 256], "float16"), "nf": ("sbuf", [128, 256], "float16"),
+    "gk": ("sbuf", [128, 8 * KC], "bfloat16"), "pk": ("sbuf", [128, 8 * KC], "float16"), "pw": ("sbuf", [128, 4 * KC], "float32"),
+    "sgn": ("sbuf", [128, 128], "bfloat16"), "tw": ("sbuf", [128, 256], "bfloat16"),
     "rr": ("sbuf", [128, 256], "bfloat16"), "lo": ("sbuf", [128, 128], "bfloat16"), "hi": ("sbuf", [128, 128], "bfloat16"),
-    "oh": ("sbuf", [128, RING * OW], "bfloat16"), "ms": ("sbuf", [128, 4 * 68], "float32"),
-    "nb": ("sbuf", [128, 256], "bfloat16"), "bp": ("sbuf", [128, 256], "bfloat16"), "bm": ("sbuf", [128, 256], "bfloat16"),
-    "nbf": ("sbuf", [128, 256], "float32"),
+    "oh": ("sbuf", [128, 128 * OW], "bfloat16"), "ms": ("sbuf", [128, 4 * 68], "float32"),
+    "nb": ("sbuf", [128, 256], "bfloat16"), "bm": ("sbuf", [128, 256], "bfloat16"), "nbf": ("sbuf", [128, 256], "float32"),
     "pf": ("sbuf", [128, N * TK], "float32"), "tt": ("sbuf", [128, 128], "float32"), "t1": ("sbuf", [128, 128], "float32"),
-    "sg": ("sbuf", [128, 128], "float32"), "hl": ("sbuf", [128, 256], "bfloat16"), "ht": ("sbuf", [128, 256], "bfloat16"),
-    "z": ("sbuf", [128, 1024], "float32"), "xs": ("sbuf", [128, TK], "float32"), "xo": ("sbuf", [128, TK], "float32"),
+    "sg": ("sbuf", [128, 128], "float32"), "hl": ("sbuf", [128, 2, 2, 64], "bfloat16"), "ht": ("sbuf", [128, 256], "bfloat16"),
+    "xo": ("sbuf", [128, TK], "float32"),
     "jj": ("sbuf", [128, 128], "float32"), "ff": ("sbuf", [128, 72], "float32"), "gi": ("sbuf", [128, 8], "float32"),
-    "si": ("sbuf", [128, 1024], "bfloat16"), "sm": ("sbuf", [128, 1024], "bfloat16"),
+    "si": ("sbuf", [128, 512], "bfloat16"), "sm": ("sbuf", [128, 2, 512], "bfloat16"),
     "ta": ("sbuf", [128, 128], "float32"), "tb": ("sbuf", [128, 128], "float32"), "tc": ("sbuf", [128, 128], "float32"),
-    "w1": ("sbuf", [128, 128], "float32"), "w2": ("sbuf", [128, 128], "float32"),
     "ib": ("sbuf", [128, 128], "bfloat16"), "imb": ("sbuf", [128, 128], "bfloat16"),
-    "i64b": ("sbuf", [128, 128], "bfloat16"), "im4k": ("sbuf", [128, 128], "bfloat16"), "xt": ("sbuf", [128, 256], "float32"),
-    "i64f": ("sbuf", [128, 128], "float32"), "ih": ("sbuf", [128, 128], "float16"),
+    "i64b": ("sbuf", [128, 128], "bfloat16"), "ck": ("sbuf", [128, 256], "bfloat16"),
+    "ih": ("sbuf", [128, 128], "float16"), "sh": ("sbuf", [128, 128], "float16"),
+    "hp": ("sbuf", [128, 128], "float16"), "hm": ("sbuf", [128, 128], "float16"), "hb": ("sbuf", [128, 384], "bfloat16"),
+    "aa": ("sbuf", [128, 256], "bfloat16"), "one": ("sbuf", [128, 128], "bfloat16"), "cu": ("sbuf", [128, 256], "bfloat16"), "cb": ("sbuf", [128, 128], "bfloat16"),
     "ga": ("sbuf", [128, 8], "float32"), "bof": ("sbuf", [128, 8], "float32"), "boh": ("sbuf", [128, 8], "float16"),
-    "bon": ("sbuf", [128, 8], "float16"), "cl": ("sbuf", [128, OW], "bfloat16"),
+    "bon": ("sbuf", [128, 8], "float16"), "cl": ("sbuf", [128, OW], "bfloat16"), "cs": ("sbuf", [128, 64], "bfloat16"),
 }
+for _k in ("vv", "vs", "ss"):
+    SCRATCH["w1" + _k] = ("sbuf", [128, 128], "float32")
+    SCRATCH["w2" + _k] = ("sbuf", [128, 128], "float32")
 for _l in range(RO):
     SCRATCH["st%d" % _l] = ("sbuf", [128, N, 2 * TK], "bfloat16")
     SCRATCH["ld%d" % _l] = ("sbuf", [128, N, 2 * TK], "bfloat16")
+    SCRATCH["z%d" % _l] = ("sbuf", [128, N * TK], "float32")
+    SCRATCH["xs%d" % _l] = ("sbuf", [128, TK], "float32")
+    SCRATCH["rlz%d" % _l] = ("sbuf", [128, TK], "float32")
 for _l in range(RO - 1):
     SCRATCH["wd%d" % _l] = ("sbuf", [128, N * 128], "float16")
+SCRATCH["wd2"] = ("sbuf", [128, 128], "float16")
 for _b in range(8):
     SCRATCH["B%d" % _b] = ("psum", [128, 512], "float32")
 
-SEMAPHORES = ["cv", "cs", "ct", "cg", "sent", "lq", "lk", "lu", "lv", "ln", "lx", "lm", "lb", "aq", "oy", "ob"]
+SEMAPHORES = ["cv", "cs", "ct", "cg", "sent", "sq", "lq", "lk", "lu", "lv", "ln", "lx", "lm", "lb", "aq", "oy", "ob"]
 for _l in range(RO):
-    SEMAPHORES += ["aw%d" % _l, "db%d" % _l] + ["a%d_%d" % (_l, _k) for _k in range(4)]
+    SEMAPHORES += ["aw%d" % _l, "db%d" % _l, "fz%d" % _l] + ["%s%d_%d" % (_h, _l, _k) for _k in range(4) for _h in "ab"]
+
+DBG = []
+OPS = {}
+WIN, TURNS, WAKE = dict(v=0.3, s=0.45, t=0.0), 3, 0.23
+PERIOD = 16.0
+DUE = dict(now=(-20, -20, -20), keys=(-20.5, -21, -21), rows=(1.5, -6, 4), bias=(-3, -3, 2), sum=(-4, 12, 0), turn=(5, 25, 0), pick=(2, 3.5, -8),
+           dot=(27.5, 9.5, -5), sum4=(26, 14, -11), mix=(25, 14, 3))
+BQ = "y"
+LATE = dict(q=2.0, w=1.5, far=1.5, fold=4.0, once=(1.5, 1.5, 0.0), bias=1.5)
+LINK = 0.0032
+CY, PE, GA, HOP = 0.00083, 0.00042, 1.56, 0.1
 
 
 def rank_program(g, core, T, topo):
@@ -57,7 +81,7 @@ def rank_program(g, core, T, topo):
         a = topo.addr(c)
         return DstId(rid=a[0], pnc=a[1])
 
-    def plan(r0):
+    def plan(r0, l):
         src = cores[r0]
         rest = [(r0 + k) % N for k in range(1, N)]
         near = [r for r in rest if topo.chip(cores[r]) == topo.chip(src)]
@@ -66,18 +90,20 @@ def rank_program(g, core, T, topo):
         home = [e for e in topo.engines(src, cores[near[0]]) if e not in out]
         free = [c for c in topo.cores_of(src) if c not in cores and topo.die(c) == topo.die(src)]
         free.sort(key=lambda c: sum(topo.may_write(c, cores[r]) for r in far))
-        straight = [r for r in far if topo.die(cores[r]) == topo.die(src)]
-        calls = []
-        for a in straight:
-            b = [r for r in far if r != a and topo.chip(cores[r]) == topo.chip(cores[a])][0]
-            calls.append([(b, home, [c for c in free if topo.may_write(c, cores[b])][0]), (a, out, None)])
+        far.sort(key=lambda r: topo.die(cores[r]) == topo.die(src))
+        mate = [r for r in far if topo.mates(topo.chip(src), topo.chip(cores[r]))]
+        plane = [r for r in far if topo.same_plane(topo.chip(src), topo.chip(cores[r]))]
+        both = [r for r in far if r not in mate + plane]
+        half = len(out) // 2
+        calls = [[(a, out[:half], None), (b, out[half:], None)] for a, b in [both] + list(zip(mate, plane))]
+        calls = [calls[k] for k in TURN]
         calls.append([(r, home, None) for r in near])
-        return near, far, out, home, calls
+        return near, far, out, home, calls, free[0], both
 
     if rank is None:
-        jobs = [(r0, k, r, es) for r0 in range(N) for k, c in enumerate(plan(r0)[4]) for r, es, h in c if h == core]
         left = 0
         for l in range(RO):
+            jobs = [(r0, k, r, es) for r0 in range(N) for k, c in enumerate(plan(r0, l)[4]) for r, es, h in c if h == core]
             for r0, k, r, es in jobs:
                 out = topo.engines(core, cores[r])
                 a = topo.addr(cores[r])
@@ -85,519 +111,530 @@ def rank_program(g, core, T, topo):
                 g.wait_ge(sem, len(es))
                 g.remote_dma(T["ld%d" % l][:, r0, :], T["st%d" % l][:, r, :], sem, T.sem.sent, a[1], a[0], bits(out))
                 left += len(out)
+            for r0 in range(N):
+                if FOLD[l] and plan(r0, l)[5] == core:
+                    out = topo.engines(core, cores[r0])
+                    a = topo.addr(cores[r0])
+                    g.wait_ge(T.sem["fz%d" % l], len(out))
+                    g.remote_dma(T["rlz%d" % l][:], T["rlz%d" % l][:], T.sem["fz%d" % l], T.sem.sent, a[1], a[0], bits(out))
+                    left += len(out)
         if left:
             g.wait_ge(T.sem.sent, left)
         return
     Q = {"v": g.vector, "s": g.scalar, "t": g.tensor, "g": g, "y": g.sync}
     ops = []
-    count = {}
-    final = {}
-    lastw, readers, bankq = {}, {}, {}
+    lastw, readers = {}, {}
+    urge = [-50]
 
-    def add(q, emit, rd=(), wr=(), banks=(), sem=None, inc=1):
-        deps = []
+    def add(q, emit, hold, rd=(), wr=(), banks=(), sem=None, inc=1, late=0.0, group=None):
+        deps = set()
         for k in rd:
-            deps += lastw.get(k, [])
+            deps.update(lastw.get(k, ()))
         for k in wr:
-            deps += lastw.get(k, []) + readers.get(k, [])
-        for b in banks:
-            if b in bankq and bankq[b][0] != q:
-                deps.append(bankq[b])
-        whole = sem is not None
-        name = sem if whole else "c" + q
-        count[name] = count.get(name, 0) + inc
-        if whole:
-            final[name] = True
-        me = (q, name, count[name])
-        deps = [d for d in deps if not (q == "t" and d[1] == "ct") and not (whole and d[1] == name)]
-        ops.append((q, emit, name, inc, deps))
+            deps.update(lastw.get(k, ()))
+            deps.update(readers.get(k, ()))
+        me = len(ops)
+        ops.append(dict(q=q, emit=emit, hold=hold, late=late, deps=deps, banks=banks, sem=sem, inc=inc, urge=urge[0], group=group, tag=(list(wr) + [""])[0]))
         for k in rd:
             readers.setdefault(k, []).append(me)
         for k in wr:
             lastw[k] = [me]
             readers[k] = []
-        for b in banks:
-            bankq[b] = me
+
+    def due(l, what, more=0.0):
+        urge[0] = PERIOD * l + DUE[what][l] + more
 
     S = T.sem
     B = [T["B%d" % b] for b in range(8)]
 
-    def vts(out, in0, s1, s2, o0, o1, rd, wr, banks=()):
+    def width(ap):
+        return int(np.prod(ap.shape[1:]))
+
+    def vts(out, in0, s1, s2, o0, o1, rd, wr, banks=(), k=1.0):
+        hold = max(64, width(out) * k) * CY
         if s2 is None:
-            add("v", lambda: g.vector.tensor_scalar(out, in0, s1, None, o0), rd, wr, banks)
+            add("v", lambda: g.vector.tensor_scalar(out, in0, s1, None, o0), hold, rd, wr, banks)
         else:
-            add("v", lambda: g.vector.tensor_scalar(out, in0, s1, s2, o0, o1), rd, wr, banks)
+            add("v", lambda: g.vector.tensor_scalar(out, in0, s1, s2, o0, o1), hold, rd, wr, banks)
 
-    def vtt(out, a, b, op, rd, wr, banks=()):
-        add("v", lambda: g.vector.tensor_tensor(out, a, b, op), rd, wr, banks)
+    def vtt(out, a, b, op, rd, wr, banks=(), k=1.0):
+        add("v", lambda: g.vector.tensor_tensor(out, a, b, op), max(64, width(out) * k) * CY, rd, wr, banks)
 
-    def vcp(out, a, rd, wr, banks=()):
-        add("v", lambda: g.vector.tensor_copy(out, a), rd, wr, banks)
+    def vcp(out, a, rd, wr, banks=(), k=1.0):
+        add("v", lambda: g.vector.tensor_copy(out, a), max(64, width(out) * k) * CY, rd, wr, banks)
 
     def vms(out, c, wr):
-        add("v", lambda: g.vector.memset(out, c), (), wr)
+        add("v", lambda: g.vector.memset(out, c), 64 * CY, (), wr)
 
-    def act(out, a, f, rd, wr, banks=(), bias=0.0, scale=1.0):
-        add("s", lambda: g.scalar.activation(out, a, f, bias=bias, scale=scale), rd, wr, banks)
+    def act(out, a, f, rd, wr, banks=(), bias=0.0, scale=1.0, k=1.0):
+        add("s", lambda: g.scalar.activation(out, a, f, bias=bias, scale=scale), max(66, width(out) * k) * CY, rd, wr, banks)
 
-    def mmul(out, lhsT, rhs, start, stop, rd, wr, bank):
-        add("t", lambda: g.tensor.matmul(out, lhsT, rhs, start, stop), rd, wr, (bank,))
+    def mmul(out, lhsT, rhs, start, stop, rd, wr, bank, k=1):
+        add("t", lambda: g.tensor.matmul(out, lhsT, rhs, start, stop), max(min(64, width(lhsT)), width(rhs)) * k * PE, rd, wr, (bank,),
+            group=(start, stop), late=0.05)
 
-    def dma(q, out, in_, rd, wr, sem):
-        add(q, lambda: Q[q].dma_start(out, in_), rd, wr, sem=sem, inc=16)
+    def dma(q, out, in_, rd, wr, sem, late=2.0):
+        add(q, lambda: Q[q].dma_start(out, in_), 0.06, rd, wr, sem=sem, inc=16, late=late)
 
     def iota(out, pat, base, cm, wr):
-        add("g", lambda: g.iota(out, pat, base, cm, allow_small_or_imprecise_dtypes=True), (), wr)
+        add("g", lambda: g.iota(out, pat, base, cm, allow_small_or_imprecise_dtypes=True), 0.13 + 2 * width(out) * CY, (), wr)
 
-    near, far, eout, ehome, calls = plan(rank)
+    near, far, eout, ehome, calls, spare, both = plan(rank, 0)
     step = {rank: len(calls)}
-    gets = [0] * len(calls)
-    for s in range(N):
-        for k, c in enumerate(plan(s)[4]):
-            for r, es, h in c:
-                if r == rank:
-                    step[s] = k
-                    gets[k] += len(es) if h is None else len(topo.engines(h, core))
-    srcs = sorted(range(N), key=lambda s: (step[s] if s != rank else 0.5, s))
+    gets = [[0] * len(calls) for l in range(RO)]
+    for l in range(RO):
+        for s in range(N):
+            for k, c in enumerate(plan(s, l)[4]):
+                for r, es, h in c:
+                    if r == rank:
+                        step[s] = k
+                        gets[l][k] += len(es) if h is None else len(topo.engines(h, core))
+    srcs = sorted(range(N), key=lambda s: (step[s], s))
 
-    def remote(transfers, engines, rd):
+    def remote(transfers, engines, rd, sem, n, wr, late, wire=0.3):
+        left = "sq" if sem == "aq" else "sent"
+
         def emit():
-            g.remote_dma_fused(transfers, local_sem=S.sent)
-        add("g", emit, rd, (), sem="sent", inc=engines)
+            g.remote_dma_fused(transfers, local_sem=S[left])
+        add("g", emit, 0.3, rd, ["to" + sem] + ["remote"] * (sem[:2] not in ("aq", "fz")), sem=left, inc=engines)
+        ops[-1]["wire"] = wire
+        add("a", None, 0.0, ["to" + sem], wr, sem=sem, inc=n, late=late)
 
-    def arrive(sem, n, wr):
-        if n:
-            add("g", None, (), wr, sem=sem, inc=n)
-
-    def send_all(ap, sem, rd):
-        tr = [RemoteDMATransfer(dst_ids=[dst(cores[r]) for r in far], dma_engine_mask=bits(eout), remote_sem=S[sem], srcs=[ap], dsts=[ap] * len(far)),
-              RemoteDMATransfer(dst_ids=[dst(cores[r]) for r in near], dma_engine_mask=bits(ehome), remote_sem=S[sem], srcs=[ap], dsts=[ap] * len(near))]
-        remote(tr, len(eout) + len(ehome), rd)
-        return len(far) * len(eout) + len(near) * len(ehome)
+    def send_all(ap, sem, rd, wr, late):
+        ways = [([c[k][0] for c in calls[:-1]], calls[0][k][1]) for k in range(2)] + [(near, ehome)]
+        tr = [RemoteDMATransfer(dst_ids=[dst(cores[r]) for r in to], dma_engine_mask=bits(es), remote_sem=S[sem], srcs=[ap], dsts=[ap] * len(to)) for to, es in ways]
+        remote(tr, sum(len(es) for to, es in ways), rd, sem, sum(len(to) * len(es) for to, es in ways), wr, late, 4 * width(ap) * LINK)
 
     qown = T.qa[:, rank * TK:(rank + 1) * TK]
     dma("y", qown, T.rq[:], (), ["qown"], "lq")
     dma("s", T.nmi[:], T.nm[:], (), ["nmi"], "ln")
-    dma("y", T.kw[:], T.ke[:], (), ["kw"], "lk")
+    dma("y", T.kw[:], T.ke[:], (), ["kw"], "lk", 3.2)
     iota(T.jj[:], [[1, 128]], 0, -1, ["jj"])
-    iota(T.ff[:], [[1, 72]], 0, 0, ["ff"])
     iota(T.gi[:], [[-16, 8]], 0, 1, ["gi"])
-    n = send_all(qown, "aq", ["qown"])
-    arrive("aq", n, ["qa"])
-    iota(T.si[:], [[-8, 8], [-1, 8], [0, 16]], 0, 1, ["si"])
-    dma("y", T.uw[:], T.ue[:], ["kw"], ["uw"], "lu")
-    dma("y", T.vw[:], T.ve[:], (), ["vw"], "lv")
+    iota(T.ff[:], [[1, 72]], 0, 0, ["ff"])
+    send_all(qown, "aq", ["qown"], ["qa"], LATE["q"])
+    iota(T.si[:], [[-8, 4], [-1, 8], [0, 16]], 0, 1, ["si"])
     for j in range(4):
-        dma("y", T.nb[:, j * 64:(j + 1) * 64], T.ke[32 * j + 15:32 * j + 32:16, :], (), ["nb%d" % j], "lb")
-    dma("y", T.x0b[:], T.x0[:], (), ["x0b"], "lx")
-    dma("y", T.mmb[:], T.mm[:], (), ["mmb"], "lm")
+        dma("s", T.nb[:, j * 64:(j + 1) * 64], T.ke[32 * j + 15:32 * j + 32:16, :], (), ["nb%d" % j], "lb", 5.0)
+    dma("y", T.x0b[:], T.x0[:], (), ["x0b"], "lx", 6.0)
+    dma("y", T.mmb[:], T.mm[:], (), ["mmb"], "lm", 6.0)
+    dma("y", T.uw[:], T.ue[:], ["toaq"], ["uw"], "lu", 5.5)
+    dma("y", T.vw[:], T.ve[:], ["toaq"], ["vw"], "lv", 7.5)
 
-    vts(T.i64f[:], T.jj[:], 0.0, 64.0, A.is_equal, A.mult, ["jj"], ["i64f"])
+    def diag(name, at, value, cols=slice(0, 128), key=None):
+        vts(T[name][:, cols], T.jj[:, cols], float(at), float(value), A.is_equal, A.mult, ["jj"], [key or name])
+
+    vcp(T.nl[:], T.nmi[:], ["nmi"], ["nl"])
+    vts(T.nm0[:], T.nmi[:], -2048.0, None, A.add, None, ["nmi"], ["nm0"])
+    for name, value in (("ib", 1), ("imb", -1), ("hp", 1 / 128), ("hm", -1 / 128), ("i64b", 64)):
+        diag(name, 0, value)
+    for k in range(3):
+        vts(T.hb[:, k * 128:(k + 1) * 128], T.jj[:], 0.0, 0.5 - k % 2, A.is_equal, A.mult, ["jj"], ["hb%d" % k])
     vts(T.ga[:], T.gi[:], 0.0, 15.0, A.max, A.min, ["gi"], ["ga"])
-    vts(T.ib[:], T.jj[:], 0.0, None, A.is_equal, None, ["jj"], ["ib"])
-    vts(T.imb[:], T.jj[:], 0.0, -1.0, A.is_equal, A.mult, ["jj"], ["imb"])
-    vts(T.i64b[:], T.jj[:], 0.0, 64.0, A.is_equal, A.mult, ["jj"], ["i64b"])
     vtt(T.bof[:], T.ga[:], T.gi[:], A.is_equal, ["ga", "gi"], ["bof"])
     vtt(T.boh[:], T.ga[:], T.gi[:], A.is_equal, ["ga", "gi"], ["boh"])
-    vts(T.im4k[:], T.jj[:], 0.0, -4096.0, A.is_equal, A.mult, ["jj"], ["im4k"])
-    vts(T.ih[:], T.jj[:], 0.0, 1.0 / 64, A.is_equal, A.mult, ["jj"], ["ih"])
     vts(T.bon[:], T.bof[:], -1.0, None, A.mult, None, ["bof"], ["bon"])
-    vts(T.ta[:], T.jj[:], 1.0, 64.0, A.is_equal, A.mult, ["jj"], ["ta"])
-    vts(T.tb[:], T.jj[:], -1.0, 64.0, A.is_equal, A.mult, ["jj"], ["tb"])
-    vts(T.tc[:], T.jj[:], 0.0, -128.0, A.is_equal, A.mult, ["jj"], ["tc"])
-    vms(T.w1[:], 0.0, ["w1"])
-    vcp(T.nl[:], T.nmi[:], ["nmi"], ["nl"])
-    vcp(T.nmf[:], T.nmi[:], ["nmi"], ["nmf"])
-    vtt(T.ta[:], T.ta[:], T.tb[:], A.add, ["ta", "tb"], ["ta"])
+    act(T.one[:], T.jj[:], F.Tanh, ["jj"], ["one"], bias=20.0, scale=0.0, k=13.0)
+    vms(T.cu[:, 0:128], -1.75, ["cu0"])
+    vms(T.cu[0:64, 128:256], 3.0, ["cu1"])
+    vms(T.cu[64:128, 128:256], -63.0 / 8192, ["cu2"])
     vts(T.cl[:, 0:64], T.ff[:, 0:64], -64.0, None, A.add, None, ["ff"], ["cl0"])
     vts(T.cl[:, 64:130], T.ff[:, 0:66], 1.0 / 64, -65.0 / 128, A.mult, A.add, ["ff"], ["cl1"])
-    for h in (0, 64):
-        vtt(T.w1[h:h + 64, h:h + 64], T.ta[h:h + 64, h:h + 64], T.tc[h:h + 64, h:h + 64], A.add, ["ta", "tc", "w1"], ["w1_%d" % h])
-    for c in range(2):
-        mmul(B[1][:, c * 128:(c + 1) * 128], T.nmf[:, c * 128:(c + 1) * 128], T.i64f[:], True, True, ["nmf", "i64f"], ["xt"], 1)
-    for h in (0, 64):
-        vms(T.w1[h:h + 1, h:h + 1], -64.0, ["w1_%d" % h])
-    act(T.u[:], B[1][:, 0:256], F.Identity, ["xt"], ["u"], (1,), bias=-64.0 - 63.0 / 128, scale=1.0 / 4096)
-    vts(T.w2[:], T.w1[:], -2.0, None, A.mult, None, ["w1", "w1_0", "w1_64"], ["w2"])
-    vts(T.bas[:], B[1][:, 0:256], 1.0 / 64, -2048.0, A.mult, A.add, ["xt"], ["bas"], (1,))
-    vtt(T.du[:], T.u[:, 128:256], T.u[:, 0:128], A.subtract, ["u"], ["du"])
+    urge[0] = 0
+    vms(T.cb[:, 0:64], 1.0 / 64, ["cb0"])
+    vms(T.cb[:, 64:128], -1.0 / 128, ["cb1"])
+    diag("ih", 0, 1)
+    vms(T.ck[:], 133.0 * 32, ["ck"])
+    diag("sh", 16, 1, slice(16, 128), "sh0")
+    diag("sh", 16 - 128, 1, slice(0, 16), "sh1")
+    kinds = sorted({"vs"[2 * j in sg] + "vs"[2 * j + 1 in sg] for sg in SGROUPS for j in range(4)})
+    diag("ta", 1, 64)
+    diag("tb", -1, 64)
+    diag("tc", 0, -128)
+    vtt(T.ta[:], T.ta[:], T.tb[:], A.add, ["ta", "tb"], ["ta"], k=2)
+    for kind in kinds:
+        vms(T["w1" + kind][:], 0.0, ["w1" + kind])
+        for h in range(2):
+            if kind[h] == "v":
+                c = slice(64 * h, 64 * h + 64)
+                vtt(T["w1" + kind][c, c], T.ta[c, c], T.tc[c, c], A.add, ["ta", "tc"], ["w1" + kind], k=2)
+                vms(T["w1" + kind][64 * h:64 * h + 1, 64 * h:64 * h + 1], -64.0, ["w1" + kind])
+    if kinds != ["vv"]:
+        vts(T.cs[:], T.ff[:, 0:64], -65.0, None, A.add, None, ["ff"], ["cs"])
+        diag("ta", 0, -64)
+        diag("tb", -1, 128)
+        diag("tc", -2, -64)
+        vtt(T.ta[:], T.ta[:], T.tb[:], A.add, ["ta", "tb"], ["ta"], k=2)
+    for kind in kinds:
+        for h in range(2):
+            if kind[h] == "s":
+                c = slice(64 * h, 64 * h + 64)
+                vtt(T["w1" + kind][c, c], T.ta[c, c], T.tc[c, c], A.add, ["ta", "tc"], ["w1" + kind], k=2)
+        vts(T["w2" + kind][:], T["w1" + kind][:], -2.0, None, A.mult, None, ["w1" + kind], ["w2" + kind])
+    urge[0] = 3
+    SM = ["sm%d" % p for p in range(0, 128, 32)] + ["sz0", "sz1"]
+    for h in range(2):
+        vts(T.sm[64 - 64 * h:128 - 64 * h, h, :], T.si[64 - 64 * h:128 - 64 * h, :], 0.0, None, A.mult, None, ["si"], ["sz%d" % h], k=0.5)
+    for p in range(0, 128, 32):
+        vts(T.sm[p:p + 32, p // 64, :], T.si[p:p + 32, :], float(p), None, A.is_equal, None, ["si"], ["sm%d" % p], k=0.5)
+    act(T.mmf[:], T.mmb[:], F.Identity, ["mmb"], ["mmf"])
+    act(B[6][:, 0:256], T.x0b[:], F.Identity, ["x0b"], ["x"], (6,))
+    act(T.xs0[:], T.x0b[:], F.Identity, ["x0b"], ["xs0"], scale=0.5)
 
     NB = ["nb%d" % j for j in range(4)]
-    DB = (7, 4)
 
-    def bias_sides():
-        act(T.bp[:], T.nb[:], F.Identity, NB, ["bp"], bias=1.0)
-        act(T.bm[:], T.nb[:], F.Identity, NB, ["bm"], bias=-1.0)
+    def turn_names(nf, key):
+        vts(T.aa[:], nf[:], 1.0 / 64, 192.0 - 63.0 / 128, A.mult, A.add, [key], ["aa"], k=0.5)
+        mid, dif = B[1][:, 0:256], B[1][:, 256:512]
+        H = ["hb0", "hb1", "hb2", "aa"]
+        mmul(dif, T.aa[:, 0:128], T.hb[:, 0:256], True, False, H, ["dif"], 1)
+        mmul(dif, T.aa[:, 128:256], T.hb[:, 128:384], False, False, H, ["dif"], 1)
+        mmul(B[1][:, 384:512], nf[:, 0:128], T.hp[:], False, False, [key, "hp"], ["dif"], 1)
+        mmul(B[1][:, 384:512], nf[:, 128:256], T.hm[:], False, True, [key, "hm"], ["dif"], 1)
+        mmul(mid, T.one[:], T.cu[:], True, False, ["one", "cu0", "cu1", "cu2", "dif"], ["mid"], 1)
+        for c in range(2):
+            mmul(mid, T.aa[:, c * 128:(c + 1) * 128], T.hb[:, 0:256], False, False, H, ["mid"], 1)
+            mmul(B[1][:, 128:256], nf[:, c * 128:(c + 1) * 128], T.hp[:], False, c == 1, [key, "hp"], ["mid"], 1)
 
-    def first_x():
-        act(T.mmf[:], T.mmb[:], F.Identity, ["mmb"], ["mmf"])
-        act(B[6][:, 0:256], T.x0b[:], F.Identity, ["x0b"], ["x0", "x1"], (6,))
-        act(T.xs[:], T.x0b[:], F.Identity, ["x0b"], ["xs0", "xs1"], scale=0.5)
+    def next_names(l):
+        wd = T["wd%d" % l]
+        x = B[0][:, 128:384]
+        due(l, "sum")
+        mmul(x, T.ih[:], T.nm0[:], True, False, ["ih", "nm0", "wd%d" % l], ["xl", "wt"], 0)
+        for s in range(N):
+            for c in range(2):
+                mmul(B[0][:, (c + 1) * 128:(c + 2) * 128], T.sh[:], wd[:, s * 128:(s + 1) * 128], False, False, ["sh0", "sh1", "wd%d" % l, "wo%d" % l], ["xl"], 0)
+        mmul(x, T.one[:], T.ck[:], False, True, ["one", "ck"], ["xl"], 0)
+        due(l, "now")
+        act(T.rr[:], x, F.Identity, ["xl"], ["rr"], (0,), bias=0.5)
+        vtt(T.nf[:], x, T.rr[:], A.subtract, ["xl", "rr"], ["nf"], (0,))
+        vts(T.nl[:], T.nf[:], 2048.0, None, A.add, None, ["nf"], ["nl"], k=0.5)
+        due(l, "turn")
+        turn_names(T.nf, "nf")
 
     def names(c, ch):
         return T.kw[:].indirect(T.nl[:, c * 128 + ch * 32:c * 128 + (ch + 1) * 32])
 
-    def k_vec(ch, gather=True, mm=True):
-        for c in range(2 if gather else 0):
-            k = 4 * c + ch
-            vtt(T.pk[:, k * KC:(k + 1) * KC], names(c, ch), T.qa[:, ch * KC:(ch + 1) * KC], A.mult, ["kw", "nl", "qa", "qown"], ["pk%d" % k])
-        for i in range(16 if mm else 0):
-            o = B[0][32 * ch:32 * ch + 32, i:128:16]
-            mmul(o, T.pk[:, ch * KC + i:(ch + 1) * KC:16], T.boh[:], True, False, ["pk%d" % ch, "boh"], ["sc"], 0)
-            mmul(o, T.pk[:, (4 + ch) * KC + i:(5 + ch) * KC:16], T.bon[:], False, True, ["pk%d" % (4 + ch), "bon"], ["sc"], 0)
-
-    def k_gather(ch, b, vec=False):
-        for c in range(2):
-            o = T.gk[:, (2 * ch + c) * KC:(2 * ch + c + 1) * KC]
-            if vec:
-                vcp(o, names(c, ch), ["kw", "nl"], ["gk%d_%d" % (ch, c)])
-            else:
-                act(o, names(c, ch), F.Identity, ["kw", "nl"], ["gk%d_%d" % (ch, c)])
-            mmul(B[b][:], (T.ib, T.imb)[c][:], o, c == 0, c == 1, ["ib", "imb", "gk%d_%d" % (ch, c)], ["bc%d" % b], b)
-
-    def k_prod(l, ch, b):
+    def scores(l):
+        rest = [ch for ch in range(4) if ch not in FUSED[l]]
+        bank = dict(zip(rest, (2, 3, 4, 5) if l == 0 else (2, 3, 2, 3)))
         wide = l == RO - 1
-        p, one = (T.pw, T.bof) if wide else (T.pk, T.boh)
-        vtt(p[:, ch * KC:(ch + 1) * KC], B[b][:], T.qa[:, ch * KC:(ch + 1) * KC], A.mult, ["bc%d" % b, "qa", "qown"], ["pk%d" % ch], (b,))
-        for i in range(16):
-            mmul(B[0][32 * ch:32 * ch + 32, i:128:16], p[:, ch * KC + i:(ch + 1) * KC:16], one[:], True, True, ["pk%d" % ch, "boh", "bof"], ["sc"], 0)
+        due(l, "keys")
+        for ch in FUSED[l]:
+            for c in range(2):
+                k = 4 * c + ch
+                vtt(T.pk[:, k * KC:(k + 1) * KC], names(c, ch), T.qa[:, ch * KC:(ch + 1) * KC], A.mult, ["kw", "nl", "qa", "qown"], ["pk%d" % k], k=GA + 0.12)
+            for i in range(16):
+                o = B[0][32 * ch:32 * ch + 32, i:128:16]
+                mmul(o, T.pk[:, ch * KC + i:(ch + 1) * KC:16], T.boh[:], True, False, ["pk%d" % ch, "pk%d" % (4 + ch), "boh"], ["sc%d_%d" % (ch, i)], 0)
+                mmul(o, T.pk[:, (4 + ch) * KC + i:(5 + ch) * KC:16], T.bon[:], False, True, ["pk%d" % (4 + ch), "bon"], ["sc%d_%d" % (ch, i)], 0)
+        for ch in rest:
+            b = bank[ch]
+            due(l, "keys")
+            for c in range(2):
+                o = T.gk[:, (2 * ch + c) * KC:(2 * ch + c + 1) * KC]
+                if ch in VGATH[l]:
+                    vcp(o, names(c, ch), ["kw", "nl"], ["gk%d_%d" % (ch, c)], k=GA + 0.12)
+                else:
+                    act(o, names(c, ch), F.Identity, ["kw", "nl"], ["gk%d_%d" % (ch, c)], k=GA + 0.15)
+                mmul(B[b][:], (T.ib, T.imb)[c][:], o, c == 0, c == 1, ["ib", "imb", "gk%d_%d" % (ch, c)], ["B%d" % b], b)
+            due(l, "now")
+            p, one = (T.pw, T.bof) if wide else (T.pk, T.boh)
+            vtt(p[:, ch * KC:(ch + 1) * KC], B[b][:], T.qa[:, ch * KC:(ch + 1) * KC], A.mult, ["B%d" % b, "qa", "qown"], ["pk%d" % ch], (b,))
+            for i in range(16):
+                mmul(B[0][32 * ch:32 * ch + 32, i:128:16], p[:, ch * KC + i:(ch + 1) * KC:16], one[:], True, True, ["pk%d" % ch, "boh", "bof"],
+                     ["sc%d_%d" % (ch, i)], 0, 4 if wide else 1)
 
-    def landed(l, s):
-        return "own%d" % l if s == rank else "ld%d_%d" % (l, step[s])
-
-    def f_p(l, h, ss):
-        for s in ss:
-            o = s * TK + h * 128
-            vtt(T.pf[:, o:o + 128], T["ld%d" % l][:, s, h * 128:(h + 1) * 128], B[6][:, h * 128:(h + 1) * 128], A.mult,
-                [landed(l, s), "x%d" % h], ["pf%d_%d" % (h, s)], (6,))
-            mmul(B[DB[h]][:, s * 8:(s + 1) * 8], T.pf[:, o:o + 128], T.bof[:], True, True, ["pf%d_%d" % (h, s), "bof"], ["d%d" % h], DB[h])
-
-    def f_tanh(h):
-        c = slice(h * 64, (h + 1) * 64)
-        act(T.tt[:, c], B[DB[h]][:, 0:64], F.Tanh, ["d%d" % h], ["tt%d" % h], (DB[h],), scale=0.5)
-        act(T.t1[:, c], T.tt[:, c], F.Identity, ["tt%d" % h], ["t1%d" % h], bias=0.125, scale=0.125)
-
-    def f_sig(h):
-        c = slice(h * 64, (h + 1) * 64)
-        vtt(T.sg[:, c], B[DB[h]][:, 0:64], T.t1[:, c], A.mult, ["d%d" % h, "t1%d" % h], ["sg%d" % h], (DB[h],))
-        vtt(T.hl[:, h * 128:h * 128 + 64], B[DB[h]][:, 0:64], T.t1[:, c], A.mult, ["d%d" % h, "t1%d" % h], ["hh%d" % h], (DB[h],))
-
-    def f_lo(h):
-        c = slice(h * 64, (h + 1) * 64)
-        vtt(T.hl[:, h * 128 + 64:h * 128 + 128], T.sg[:, c], T.hl[:, h * 128:h * 128 + 64], A.subtract, ["sg%d" % h, "hh%d" % h], ["ll%d" % h])
-        mmul(B[DB[h]][:, 128:256], T.hl[:, h * 128:(h + 1) * 128], T.ib[:], True, True, ["hh%d" % h, "ll%d" % h, "ib"], ["tr%d" % h], DB[h])
-
-    def f_ht(h):
-        act(T.ht[:, h * 128:(h + 1) * 128], B[DB[h]][:, 128:256], F.Identity, ["tr%d" % h], ["ht%d" % h], (DB[h],))
-
-    def f_bc(h, yb):
-        for s in range(8):
-            b = yb[s // 4]
-            mmul(B[b][:, (s % 4) * 128:(s % 4 + 1) * 128], T.sm[:, s * 128:(s + 1) * 128], T.ht[:, h * 128:(h + 1) * 128], True, True,
-                 ["sm0", "sm1", "ht%d" % h], ["bc%d" % b], b)
-
-    def f_y(l, h, part, yb):
-        a, b = yb
-        ld = T["ld%d" % l]
-        z = T.z[:, h * 512:(h + 1) * 512]
-        c = slice(TK + h * 128, TK + (h + 1) * 128)
-        if part == 0:
-            vtt(z, B[a][:], ld[:, 0:4, c], A.mult, [landed(l, s) for s in range(4)] + ["bc%d" % a], ["z%d" % h], (a,))
-        elif part == 1:
-            vtt(B[b][:], B[b][:], ld[:, 4:8, c], A.mult, [landed(l, s) for s in range(4, 8)] + ["bc%d" % b], ["bc%d" % b], (b,))
-        else:
-            vtt(z, z, B[b][:], A.add, ["z%d" % h, "bc%d" % b], ["z%d" % h], (b,))
-
-    def f_mix(h):
-        o = B[DB[h]][:, 256:384]
-        c = slice(h * 128, (h + 1) * 128)
-        mmul(o, T.mmf[:], T.xs[:, c], True, False, ["mmf", "xs%d" % h], ["mx%d" % h], DB[h])
-        for k in range(4):
-            mmul(o, T.mmf[:], T.z[:, h * 512 + k * 128:h * 512 + (k + 1) * 128], False, k == 3, ["mmf", "z%d" % h], ["mx%d" % h], DB[h])
-
-    def f_out(l, h):
-        o = B[DB[h]][:, 256:384]
-        c = slice(h * 128, (h + 1) * 128)
-        if l < RO - 1:
-            act(B[6][:, c], o, F.Tanh, ["mx%d" % h], ["x%d" % h], (DB[h], 6))
-            act(T.xs[:, c], B[6][:, c], F.Identity, ["x%d" % h], ["xs%d" % h], (6,), scale=0.5)
-        else:
-            act(T.xo[:, c], o, F.Tanh, ["mx%d" % h], ["xo%d" % h], (DB[h],))
-            dma("y" if h == 0 else "s", T.yx[:, c], T.xo[:, c], ["xo%d" % h], (), "oy")
-
-    def pick(l, r):
-        buf = T[("ld%d" if r == rank else "st%d") % l]
-        for half, win in enumerate((T.uw, T.vw)):
-            key = "st%d_%d_%d" % (l, r, half)
-            act(buf[:, r, half * TK:(half + 1) * TK], win[:].indirect(T.wl[:, r * 16:(r + 1) * 16]), F.Identity, ["wl", "uv"[half] + "w"],
-                [key] + (["own%d" % l] if r == rank else []))
-
-    def hand(l, k):
-        if k == len(calls):
-            pick(l, rank)
+    def winners(l):
+        SC = ["sc%d_%d" % (ch, i) for ch in range(4) for i in range(16)]
+        due(l, "now")
+        act(T.sgn[:], B[0][:, 0:128], F.Sign, SC, ["sgn"], (0,), bias=0.5)
+        for k in range(2):
+            vtt(T.tw[:, k * 128:(k + 1) * 128], B[1][:, (k + 2) * 128:(k + 3) * 128], T.sgn[:], A.mult, ["dif", "sgn"], ["tw%d" % k], (1,))
+        for k, name in enumerate(("lo", "hi")):
+            vtt(T[name][:], B[1][:, k * 128:(k + 1) * 128], T.tw[:, k * 128:(k + 1) * 128], A.add, ["mid", "tw%d" % k], [name], (1,))
+        mmul(B[0][:, 256:384], T.lo[:], T.i64b[:], True, False, ["lo", "hi", "i64b"], ["wt", "xl"], 0)
+        mmul(B[0][:, 256:384], T.hi[:], T.i64b[:], False, True, ["hi", "i64b"], ["wt"], 0)
+        if l == RO - 1:
+            vts(T.wl[:], B[0][:, 256:384], 4127.5, None, A.add, None, ["wt"], ["wl"], (0,))
             return
-        tr, rd = [], []
-        sem = "a%d_%d" % (l, k)
-        for r, es, h in calls[k]:
-            pick(l, r)
-            rd += ["st%d_%d_%d" % (l, r, half) for half in range(2)]
-            src = T["st%d" % l][:, r, :]
-            if h is None:
-                tr.append(RemoteDMATransfer(dst_ids=[dst(cores[r])], dma_engine_mask=bits(es), remote_sem=S[sem], src=src, dst=T["ld%d" % l][:, rank, :]))
-            else:
-                tr.append(RemoteDMATransfer(dst_ids=[dst(h)], dma_engine_mask=bits(es), remote_sem=S[sem], src=src, dst=src))
-        remote(tr, sum(len(c[1]) for c in calls[k]), rd)
-        arrive(sem, gets[k], ["ld%d_%d" % (l, k)])
+        wo = T["wd%d" % l][:, rank * 128:(rank + 1) * 128]
+        vts(wo, B[0][:, 256:384], 2079.5, None, A.add, None, ["wt"], ["wo%d" % l], (0,))
+        vts(T.wl[:], wo, 2048.0, None, A.add, None, ["wo%d" % l], ["wl"], k=0.5)
+        send_all(wo, "aw%d" % l, ["wo%d" % l], ["wd%d" % l], LATE["w"])
 
-    slot = [0]
-
-    def count_group(gr, i0=0, i1=16):
+    def count_group(l, gr):
         b, p0 = 2 + (gr // 2) % 2, (gr % 2) * 64
-        for i in range(i0, i1):
-            k = slot[0] % RING
-            slot[0] += 1
+        byS = gr in SGROUPS[l]
+        for i in range(16):
             col = gr * 16 + i
-            o = k * OW
-            vts(T.oh[:, o:o + 130], T.cl[:, 0:130], T.lo[:, col:col + 1], T.hi[:, col:col + 1], A.max, A.min,
-                ["cl0", "cl1", "lo", "hi"], ["oh%d" % k])
-            mmul(B[b][p0:p0 + 64, 0:66], T.oh[:, o:o + 64], T.oh[:, o + 64:o + 130], i == 0, i == 15, ["oh%d" % k], ["bc%d" % b], b)
-
-    def copy_m(j):
-        b = 2 + j % 2
-        act(T.ms[:, j * 68:j * 68 + 66], B[b][:, 0:66], F.Identity, ["bc%d" % b], ["ms%d" % j], (b,))
-
-    def diffs(j):
-        o = B[5][:, j * 64:(j + 1) * 64]
-        mmul(o, T.ib[:], T.bp[:, j * 64:(j + 1) * 64], True, False, ["ib", "bp"], ["bc5"], 5)
-        for k, w in ((0, "w1"), (1, "w2"), (2, "w1")):
-            mmul(o, T[w][:], T.ms[:, j * 68 + k:j * 68 + k + 64], False, k == 2, ["w1", "w1_0", "w1_64", "w2", "ms%d" % j], ["bc5"], 5)
+            o = col * OW
+            due(l, "rows", 0.0 if byS else 0.054 * (i + 16 * len([x for x in range(gr) if x not in SGROUPS[l]])))
+            if byS:
+                act(T.oh[:, o:o + 64], T.cs[:], F.Relu, ["cs", "lo"], ["oa%d" % col], bias=T.lo[:, col:col + 1], scale=-1.0)
+                act(T.oh[:, o + 64:o + 130], T.cl[:, 64:130], F.Relu, ["cl1", "hi"], ["oh%d" % col], bias=T.hi[:, col:col + 1], scale=-1.0)
+            else:
+                vts(T.oh[:, o:o + 130], T.cl[:, 0:130], T.lo[:, col:col + 1], T.hi[:, col:col + 1], A.max, A.min,
+                    ["cl0", "cl1", "lo", "hi"], ["oh%d" % col, "oa%d" % col], k=0.5)
+        for i in range(16):
+            col = gr * 16 + i
+            o = col * OW
+            due(l, "rows", 0.054 * (i + 16 * len([x for x in range(gr) if x not in SGROUPS[l]])))
+            rows = range(gr * 16, gr * 16 + 16) if byS and i == 0 else [col]
+            mmul(B[b][p0:p0 + 64, 0:66], T.oh[:, o:o + 64], T.oh[:, o + 64:o + 130], i == 0, i == 15,
+                 ["oh%d" % c for c in rows] + ["oa%d" % c for c in rows], ["B%d" % b], b)
 
     def new_bias(l, j):
+        last = l == RO - 1
+        b = 2 + j % 2
+        due(l, "bias")
+        kind = "vs"[2 * j in SGROUPS[l]] + "vs"[2 * j + 1 in SGROUPS[l]]
+        act(T.ms[:, j * 68:j * 68 + 66], B[b][:, 0:66], F.Identity, ["B%d" % b], ["ms%d" % j], (b,))
         c = slice(j * 64, (j + 1) * 64)
-        if l == RO - 1:
-            vtt(T.nbf[:, c], B[5][:, c], T.bm[:, c], A.max, ["bc5", "bm"], ["nbf%d" % j], (5,))
+        fb = 0 if last else 7
+        o = B[fb][:, 384 + (j % 2) * 64:448 + (j % 2) * 64]
+        key = "df%d_%d" % (fb, j % 2)
+        mmul(o, T.ib[:], T.nb[:, c], True, False, ["ib", "ms%d" % j, NB[j]], [key], fb)
+        mmul(o, T.one[:], T.cb[:, 64 * last:64 * last + 64], False, False, ["one", "cb0", "cb1"], [key], fb)
+        for k, w in ((0, "w1"), (1, "w2"), (2, "w1")):
+            mmul(o, T[w + kind][:], T.ms[:, j * 68 + k:j * 68 + k + 64], False, k == 2, [w + kind, "ms%d" % j], [key], fb, 4)
+        if last:
+            vtt(T.nbf[:, c], o, T.bm[:, c], A.max, [key, "bm"], ["nbf%d" % j], (fb,))
             dma("y", T.yb[2 * j:2 * j + 2, :], T.nbf[:, c], ["nbf%d" % j], (), "ob")
         else:
-            vtt(T.nb[:, c], B[5][:, c], T.bm[:, c], A.max, ["bc5", "bm"], ["nb%d" % j], (5,))
-            dma("y", T.kw[32 * j + 15:32 * j + 32:16, :], T.nb[:, c], ["nb%d" % j], ["kw"], "db%d" % l)
+            vtt(T.nb[:, c], o, T.nb[:, c], A.max, [key], ["nb%d" % j], (fb,))
+            dma(BQ if j == 3 else "y", T.kw[32 * j + 15:32 * j + 32:16, :], T.nb[:, c], ["nb%d" % j, "kw"], ["kw%d" % j], "db%d" % l, LATE["bias"])
 
-    def names_sum(l):
-        wd = T["wd%d" % l]
-        for c in range(2):
-            o = B[1][:, c * 128:(c + 1) * 128]
-            mmul(o, T.ih[:], T.bas[:, c * 128:(c + 1) * 128], True, False, ["ih", "bas"], ["xt"], 1)
-            for s in range(N):
-                mmul(o, T.ih[:], wd[:, s * 128:(s + 1) * 128], False, s == N - 1, ["ih", "wd%d" % l, "wa%d" % l, "wb%d" % l], ["xt"], 1)
+    def counts(l):
+        due(l, "bias")
+        if l == RO - 1:
+            act(T.bm[:], T.nb[:], F.Identity, NB, ["bm"], bias=-3.0)
+        for j in range(4):
+            count_group(l, 2 * j)
+            count_group(l, 2 * j + 1)
+            new_bias(l, j)
+        if l < RO - 1:
+            lastw["kw"] = sum((lastw["kw%d" % j] for j in range(4)), [])
+            readers["kw"] = []
 
-    EARLY = 3
+    def pick(l, r, halves, byV):
+        buf = T[("ld%d" if r == rank else "st%d") % l]
+        for half in halves:
+            o = buf[:, r, half * TK:(half + 1) * TK]
+            a = (T.uw, T.vw)[half][:].indirect(T.wl[:, r * 16:(r + 1) * 16])
+            rd, wr = ["wl", "uv"[half] + "w"], ["st%d_%d_%d" % (l, r, half)]
+            if byV:
+                vcp(o, a, rd, wr, k=GA + 0.24)
+            else:
+                act(o, a, F.Identity, rd, wr, k=GA + 0.3)
+
+    def hand(l, k, halves):
+        due(l, "pick", 0.1 * k + halves[0])
+        byV = (k, halves[0]) in VPICK[l]
+        if k == len(calls):
+            pick(l, rank, halves, byV)
+            return
+        tr, rd = [], []
+        sem = "%s%d_%d" % ("ab"[halves[0]], l, k)
+        c = slice(halves[0] * TK, (halves[-1] + 1) * TK)
+        for r, es, h in calls[k]:
+            pick(l, r, halves, byV)
+            rd += ["st%d_%d_%d" % (l, r, half) for half in halves]
+            tr.append(RemoteDMATransfer(dst_ids=[dst(cores[r])], dma_engine_mask=bits(es), remote_sem=S[sem], src=T["st%d" % l][:, r, c], dst=T["ld%d" % l][:, rank, c]))
+        wire = len(halves) * TK * LINK * (0 if len(tr) == 1 else 2 if calls[k][0][0] in both else 1)
+        remote(tr, sum(len(x[1]) for x in calls[k]), rd, sem, gets[l][k], ["ld%d_%d_%d" % (l, k, half) for half in halves], LATE["far"] + LATE["once"][l], wire)
+
+    def landed(l, s, half):
+        return "st%d_%d_%d" % (l, s, half) if s == rank else "ld%d_%d_%d" % (l, step[s], half)
+
+    def tokens(l, n, yb):
+        ld = T["ld%d" % l]
+        pairs = [sorted(srcs[4 * n + 2 * k:4 * n + 2 * k + 2]) for k in range(2)]
+        c = slice(n * 64, (n + 1) * 64)
+        t = slice(n * 128, (n + 1) * 128)
+        d = B[7][:, c]
+        due(l, "dot", n)
+        for j, s in enumerate(pairs[0] + pairs[1]):
+            vtt(T.pf[:, s * TK:(s + 1) * TK], ld[:, s, 0:TK], B[6][:, 0:TK], A.mult, [landed(l, s, 0), "x"], ["pf%d" % s], (6,))
+            for h in range(2):
+                o = n * 64 + h * 32 + j * 8
+                mmul(B[7][:, o:o + 8], T.pf[:, s * TK + h * 128:s * TK + (h + 1) * 128], T.bof[:], True, True, ["pf%d" % s, "bof"], ["d%d_%d" % (h, s)], 7, 4)
+        D = ["d%d_%d" % (h, s) for s in pairs[0] + pairs[1] for h in range(2)]
+        due(l, "now")
+        act(T.tt[:, c], d, F.Tanh, D, ["tt%d" % n], (7,), scale=0.5)
+        act(T.t1[:, c], T.tt[:, c], F.Identity, ["tt%d" % n], ["t1%d" % n], bias=0.125, scale=0.125)
+        vtt(T.hl[:, n, :, 0:32], d, T.t1[:, c], A.mult, D + ["t1%d" % n], ["hh%d" % n], (7,))
+        vtt(T.sg[:, c], d, T.t1[:, c], A.mult, D + ["t1%d" % n], ["sg%d" % n], (7,))
+        vtt(T.hl[:, n, :, 32:64], T.sg[:, c], T.hl[:, n, :, 0:32], A.subtract, ["sg%d" % n, "hh%d" % n], ["ll%d" % n], k=2)
+        for h in range(2):
+            mmul(B[7][64 * h:64 * h + 64, 128 + n * 128:256 + n * 128], T.hl[:, n, h, :], T.ib[:], True, True, ["hh%d" % n, "ll%d" % n, "ib"], ["tr%d_%d" % (n, h)], 7)
+        act(T.ht[:, t], B[7][:, 128 + n * 128:256 + n * 128], F.Identity, ["tr%d_0" % n, "tr%d_1" % n], ["ht%d" % n], (7,))
+        due(l, "sum4", n)
+        for j in range(4):
+            b = yb[j // 2]
+            for h in range(2):
+                o = (j % 2) * TK + h * 128
+                mmul(B[b][:, o:o + 128], T.sm[:, h, j * 128:(j + 1) * 128], T.ht[:, t], True, True, SM + ["ht%d" % n],
+                     ["B%d" % b] + (["mid", "dif"] if b == 1 else []), b)
+        zz = T["z%d" % l]
+        addv = ADDV[l][n] and not FOLD[l]
+        z = [zz[:, (2 * n + k) * 512:(2 * n + k + 1) * 512] for k in range(2)]
+        for k, b in enumerate(yb):
+            s0, s1 = pairs[k]
+            v = ld[:, s0:s1 + 1:s1 - s0, TK:2 * TK]
+            rd = [landed(l, s0, 1), landed(l, s1, 1), "B%d" % b]
+            if k == 1 and addv:
+                vtt(B[b][:], B[b][:], v, A.mult, rd, ["B%d" % b], (b,))
+                vtt(z[0], z[0], B[b][:], A.add, ["B%d" % b], ["z%d_%d" % (l, 2 * n)], (b,))
+            else:
+                vtt(z[k], B[b][:], v, A.mult, rd, ["z%d_%d" % (l, 2 * n + k)], (b,))
+        o = B[6][:, TK:2 * TK]
+        due(l, "mix", n)
+        xs = T["xs%d" % l]
+        if FOLD[l] and n == 1:
+            es = topo.engines(core, spare)
+            tr = RemoteDMATransfer(dst_ids=[dst(spare)], dma_engine_mask=bits(es), remote_sem=S["fz%d" % l], alu_op=1,
+                                   srcs=[xs[:]] + [zz[:, k * TK:(k + 1) * TK] for k in range(N)], dsts=[T["rlz%d" % l][:]])
+            remote([tr], len(es), ["xs%d" % l] + ["z%d_%d" % (l, k) for k in range(4)], "fz%d" % l, len(es), ["zs"], LATE["fold"], 0.0)
+            mmul(o, T.mmf[:], T["rlz%d" % l][:], True, True, ["mmf", "zs"], ["mx"], 6, 4)
+        elif not FOLD[l]:
+            if n == 0:
+                mmul(o, T.mmf[:], xs[:], True, False, ["mmf", "xs%d" % l], ["mx"], 6, 4)
+            parts = 2 if addv else 4
+            for k in range(parts):
+                mmul(o, T.mmf[:], zz[:, n * 1024 + k * TK:n * 1024 + (k + 1) * TK], False, n == 1 and k == parts - 1, ["mmf", "z%d_%d" % (l, 2 * n + k // 2)], ["mx"], 6, 4)
+        due(l, "now")
+        if n == 1 and l < RO - 1:
+            act(B[6][:, 0:TK], o, F.Tanh, ["mx"], ["x"], (6,))
+            act(T["xs%d" % (l + 1)][:], B[6][:, 0:TK], F.Identity, ["x"], ["xs%d" % (l + 1)], (6,), scale=0.5)
+        elif n == 1:
+            act(T.xo[:], o, F.Tanh, ["mx"], ["xo"], (6,))
+            dma("s", T.yx[:], T.xo[:], ["xo"], (), "oy")
+
+    urge[0] = -40
+    turn_names(T.nm0, "nm0")
     for l in range(RO):
         last = l == RO - 1
-        f = l - 1
-        ps = srcs[EARLY:] if f == 0 else srcs
-        hp = len(ps) // 2
-        two = True
-        if f < 0:
-            k_gather(0, 2)
-            k_gather(2, 4, vec=True)
-            k_gather(1, 3)
-            k_gather(3, 7, vec=True)
-            for ch, b in ((0, 2), (2, 4), (1, 3), (3, 7)):
-                k_prod(l, ch, b)
-            bias_sides()
-            first_x()
-        else:
-            k_gather(0, 2)
-            k_vec(3)
-            if f >= 1:
-                f_out(f - 1, 0)
-            k_gather(1, 3)
-            vtt(T.du[:], T.u[:, 128:256], T.u[:, 0:128], A.subtract, ["u"], ["du"])
-            if NV[l] == 2:
-                if f >= 1:
-                    f_out(f - 1, 1)
-                k_vec(2, mm=False)
-                k_prod(l, 0, 2)
-                k_vec(2, gather=False)
-                k_prod(l, 1, 3)
-                f_p(f, 0, ps)
-                f_tanh(0)
-            else:
-                k_prod(l, 0, 2)
-                k_gather(2, 2)
-                if f >= 1:
-                    f_out(f - 1, 1)
-                f_p(f, 0, ps[:-1])
-                k_prod(l, 1, 3)
-                f_p(f, 0, ps[-1:])
-                if f == 0:
-                    f_p(f, 1, ps[3:])
-                k_prod(l, 2, 2)
-                f_tanh(0)
-                if f > 0:
-                    f_p(f, 1, ps[3:])
-        fill = [lambda: None] * 4
-        if f >= 0 and two:
-            fill = [lambda: f_p(f, 1, ps[0:1]), lambda: f_p(f, 1, ps[1:2]), lambda: f_p(f, 1, ps[2:3]), lambda: None]
-        elif f >= 0:
-            fill = [lambda: f_sig(0), lambda: f_lo(0), lambda: f_sig(1), lambda: (f_lo(1), f_ht(0))]
-        vts(T.sel[:], B[0][:, 0:128], 0.0, None, A.is_lt, None, ["sc"], ["sel"], (0,))
-        fill[0]()
-        vtt(B[0][:, 256:384], T.sel[:], T.du[:], A.mult, ["sel", "du"], ["tw"], (0,))
-        fill[1]()
-        vtt(B[0][:, 384:512], B[0][:, 256:384], T.u[:, 0:128], A.add, ["tw", "u"], ["uw_"], (0,))
-        fill[2]()
-        vts(T.lo[:], B[0][:, 384:512], 12582912.0, 12582912.0, A.add, A.subtract, ["uw_"], ["lo"], (0,))
+        scores(l)
+        winners(l)
         if not last:
-            wo = rank * 128
-            wd = T["wd%d" % l]
-            vts(wd[:, wo + 16:wo + 128], B[0][:, 384:496], 64.0, 2079.5, A.mult, A.add, ["uw_"], ["wa%d" % l], (0,))
-            vts(wd[:, wo:wo + 16], B[0][:, 496:512], 64.0, 2079.5, A.mult, A.add, ["uw_"], ["wb%d" % l], (0,))
-            n = send_all(wd[:, wo:wo + 128], "aw%d" % l, ["wa%d" % l, "wb%d" % l])
-            arrive("aw%d" % l, n, ["wd%d" % l])
-        vtt(T.hi[:], B[0][:, 384:512], T.lo[:], A.subtract, ["uw_", "lo"], ["hi"], (0,))
-        mmul(B[6][:, 256:384], T.lo[:], T.i64b[:], True, False, ["lo", "i64b"], ["wt"], 6)
-        mmul(B[6][:, 256:384], T.hi[:], T.i64b[:], False, True, ["hi", "i64b"], ["wt"], 6)
-        fill[3]()
-        count_group(0, 0, 3)
-        vts(T.wl[:], B[6][:, 256:384], 4127.5, None, A.add, None, ["wt"], ["wl"], (6,))
-        if f >= 0 and two:
-            f_sig(0)
-            if NV[l] == 2:
-                f_p(f, 1, ps[3:])
-            else:
-                count_group(0, 3, 5)
-            f_lo(0)
-            hand(l, 0)
-            f_tanh(1)
-            f_ht(0)
-            bias_sides()
-            count_group(0, 3 if NV[l] == 2 else 5)
-            count_group(1, 0, 10)
-        else:
-            if f >= 0:
-                f_ht(1)
-                bias_sides()
-            hand(l, 0)
-            count_group(0, 3)
-            count_group(1, 0, 10)
-        hand(l, 1)
-        count_group(1, 10)
-        if f >= 0:
-            f_sig(1)
-        count_group(2, 0, 2)
-        if f >= 0:
-            f_lo(1)
-        copy_m(0)
-        count_group(2, 2, 8)
-        if f >= 0:
-            f_ht(1)
-            f_bc(0, (0, 4))
-        if last:
-            f_bc(1, (1, 5))
-        hand(l, 2)
-        count_group(2, 8)
-        count_group(3, 0, 8)
-        if last:
-            for h, yb in ((0, (0, 4)), (1, (1, 5))):
-                for part in range(3):
-                    f_y(f, h, part, yb)
-                f_mix(h)
-            hand(l, 3)
-            f_out(f, 0)
-            f_out(f, 1)
-            hand(l, 4)
-        count_group(3, 8)
-        diffs(0)
-        copy_m(1)
-        count_group(4)
-        count_group(5)
-        new_bias(l, 0)
-        diffs(1)
-        copy_m(2)
-        if not last:
-            hand(l, 3)
-        count_group(6)
-        new_bias(l, 1)
-        diffs(2)
-        if not last:
-            names_sum(l)
-            act(T.rr[:], B[1][:, 0:256], F.Identity, ["xt"], ["rr"], (1,), bias=140.0 + 2.0 ** -13, scale=1.0 / 64)
-            act(T.xt[:], B[1][:, 0:256], F.Identity, ["xt"], ["xts"], (1,))
-        count_group(7)
-        new_bias(l, 2)
-        copy_m(3)
-        diffs(3)
-        if not last:
-            if f >= 0:
-                f_bc(1, (2, 3))
-            for c in range(2):
-                o = B[1][:, 256 + c * 128:384 + c * 128]
-                mmul(o, T.xt[:, c * 128:(c + 1) * 128], T.i64f[:], True, False, ["xts", "i64f"], ["xl"], 1)
-                mmul(o, T.rr[:, c * 128:(c + 1) * 128], T.im4k[:], False, True, ["rr", "im4k"], ["xl"], 1)
-            hand(l, 4)
-            if f >= 0:
-                for part in range(3):
-                    f_y(f, 0, part, (0, 4))
-            else:
-                vts(T.sm[0:64, :], T.si[0:64, :], 0.0, None, A.is_equal, None, ["si"], ["sm0"])
-                vts(T.sm[64:128, :], T.si[64:128, :], 64.0, None, A.is_equal, None, ["si"], ["sm1"])
-            new_bias(l, 3)
-            if f >= 0:
-                f_y(f, 1, 0, (2, 3))
-            else:
-                f_p(l, 0, srcs[:EARLY])
-            vts(T.nl[:], B[1][:, 256:512], 575488.0, None, A.add, None, ["xl"], ["nl"], (1,))
-            mmul(B[5][:, 256:512], T.i64f[:], T.xt[:], True, False, ["i64f", "xts"], ["xu"], 5)
-            mmul(B[5][:, 256:512], T.im4k[:], T.rr[:], False, True, ["im4k", "rr"], ["xu"], 5)
-            act(T.u[:], B[5][:, 256:512], F.Identity, ["xu"], ["u"], (5,), bias=8928.0 - 63.0 / 128, scale=1.0 / 64)
-            if f >= 0:
-                f_mix(0)
-                for part in (1, 2):
-                    f_y(f, 1, part, (2, 3))
-                f_mix(1)
-            else:
-                f_p(l, 1, srcs[:EARLY])
-        else:
-            f_p(l, 0, srcs)
-            new_bias(l, 3)
-            f_tanh(0)
-            f_p(l, 1, srcs[:4])
-            f_sig(0)
-            f_p(l, 1, srcs[4:6])
-            f_lo(0)
-            f_ht(0)
-            f_p(l, 1, srcs[6:])
-            f_tanh(1)
-            f_bc(0, (0, 1))
-            f_y(l, 0, 0, (0, 1))
-            f_sig(1)
-            f_y(l, 0, 1, (0, 1))
-            f_lo(1)
-            f_ht(1)
-            f_bc(1, (2, 3))
-            f_y(l, 0, 2, (0, 1))
-            f_mix(0)
-            f_out(l, 0)
-            for part in range(3):
-                f_y(l, 1, part, (2, 3))
-            f_mix(1)
-            f_out(l, 1)
+            next_names(l)
+        counts(l)
+        for halves in ([0], [1]) if SPLIT[l] else ([0, 1],):
+            for k in range(len(calls) + 1):
+                hand(l, k, halves)
+        for h in range(2):
+            tokens(l, h, (1, 4) if last and h else (4, 5))
 
+    shared = {}
+    for i, o in enumerate(ops):
+        if o["sem"]:
+            shared.setdefault(o["sem"], []).append(i)
+    after = [[] for o in ops]
+    for i, o in enumerate(ops):
+        for d in list(o["deps"]):
+            name = ops[d]["sem"]
+            if name and name != o["sem"] and o["q"] != "a":
+                o["deps"].update(shared[name])
+        for d in o["deps"]:
+            after[d].append(i)
+
+    def gap(a, b):
+        return -1.0 if ops[a]["q"] == ops[b]["q"] == "t" else 0.0 if ops[a]["q"] == ops[b]["q"] == "g" and ops[a]["sem"] else ops[a]["late"] + HOP
+
+    def lay(rank_of, back):
+        pre, post = ([o["deps"] for o in ops], after) if not back else (after, [o["deps"] for o in ops])
+        left = [len(p) for p in pre]
+        can = [0.0] * len(ops)
+        ready = {q: [] for q in "vstgya"}
+        free = {q: 0.0 for q in list(ready) + ["wire"]}
+        end, order, bankq, opened, behind = {}, [], {}, {}, {}
+        for i, o in enumerate(ops):
+            if not left[i]:
+                ready[o["q"]].append(i)
+        while len(order) < len(ops):
+            best = None
+            for q in ready:
+                c = []
+                for i in ready[q]:
+                    o = ops[i]
+                    if o["group"] and o["group"][back] and opened.get(o["banks"][0]):
+                        continue
+                    t = max([can[i]] + [end[bankq[b]] + HOP for b in o["banks"] if b in bankq and ops[bankq[b]]["q"] != q])
+                    c.append((free[q] if t <= free[q] else t + WAKE, i))
+                if c:
+                    t0 = min(c)[0]
+                    t, i = min((x for x in c if x[0] <= t0 + WIN.get(q, 0.0)), key=lambda x: rank_of[x[1]])
+                    fill = [x for x in c if x[0] + ops[x[1]]["hold"] <= t + 0.01]
+                    if fill:
+                        t, i = min(fill, key=lambda x: rank_of[x[1]])
+                    if best is None or t < best[0]:
+                        best = (t, i)
+            t, i = best
+            o = ops[i]
+            ready[o["q"]].remove(i)
+            for b in o["banks"]:
+                if b in bankq and ops[bankq[b]]["q"] != o["q"]:
+                    behind.setdefault(i, set()).add(bankq[b])
+                bankq[b] = i
+                if o["group"]:
+                    opened[b] = not o["group"][1 - back]
+            free[o["q"]] = end[i] = t + o["hold"]
+            queued = 0.0
+            if "wire" in o and not back:
+                queued = max(0.0, free["wire"] - end[i]) + o["wire"] if o["wire"] else 0.0
+                free["wire"] = max(free["wire"], end[i] + queued)
+            order.append(i)
+            for j in post[i]:
+                can[j] = max(can[j], end[i] + (queued if ops[j]["q"] != "g" else 0.0) + (gap(j, i) + ops[j].get("wire", 0.0) * (o["q"] == "a") if back else gap(i, j)))
+                left[j] -= 1
+                if not left[j]:
+                    ready[ops[j]["q"]].append(j)
+        return order, end, behind
+
+    if "hook" in OPS:
+        OPS["hook"](lay, ops)
+    best = None
+    rank_of = [(i - 1e6 if o["sem"] else o["urge"], i) for i, o in enumerate(ops)]
+    for turn in range(TURNS):
+        order, end, behind = lay(rank_of, 0)
+        span = max(end[i] + ops[i]["late"] for i in order)
+        if best is None or span < best[0]:
+            best = (span, order, end, behind)
+        if turn < TURNS - 1:
+            back = lay([-end[i] for i in range(len(ops))], 1)[1]
+            rank_of = [i - 1e6 if o["sem"] else -back[i] for i, o in enumerate(ops)]
+    span, order, end, behind = best
+    for i in order:
+        ops[i]["deps"].update(behind.get(i, ()))
+        DBG.append((core, end[i] - ops[i]["hold"], end[i], ops[i]["q"], ops[i]["tag"]))
+    OPS[core] = (ops, order, end)
+
+    count, mark = {}, {}
+    for i in order:
+        o = ops[i]
+        name = o["sem"] or "c" + o["q"]
+        count[name] = count.get(name, 0) + o["inc"]
+        mark[i] = (name, count[name])
     seen = {q: {} for q in Q}
-    for q, emit, name, inc, deps in ops:
-        if emit is None:
+    for i in order:
+        o = ops[i]
+        q = o["q"]
+        if o["emit"] is None:
             continue
         need = {}
-        for d in deps:
-            v = count[d[1]] if d[1] in final else d[2]
-            need[d[1]] = max(need.get(d[1], 0), v)
+        for d in o["deps"]:
+            name, v = mark[d]
+            if (q == "t" and name == "ct") or name == o["sem"]:
+                continue
+            need[name] = max(need.get(name, 0), count[name] if ops[d]["sem"] else v)
         for k, v in need.items():
             if seen[q].get(k, 0) < v:
                 Q[q].wait_ge(S[k], v)
                 seen[q][k] = v
-        ins = emit()
+        ins = o["emit"]()
         if ins is not None:
-            ins.then_inc(S[name], inc)
+            ins.then_inc(S[mark[i][0]], o["inc"])
     for k, v in count.items():
         if seen["g"].get(k, 0) < v:
             g.wait_ge(S[k], v)

@@ -6,12 +6,11 @@ N, E, TK, RO = 8, 4096, 256, 3
 OW = 136
 KC = 512
 FUSED = ((), (2, 3), (2, 3))
-VGATH = ((2, 3), (), ())
-SGROUPS = ((), (), (3, 5, 7))
-VPICK = ((), (), ((1, 0), (4, 0), (1, 1)))
-FOLD = (False, False, False)
-SPLIT = (False, False, True)
-TURN = (0, 1, 2)
+VGATH = ((1, 3), (), ())
+SGROUPS = ((5,), (5,), (3, 5, 7))
+VPICK = ((), (), ((0, 0), (6, 0), (7, 0)))
+BATCH = [[((3, 1), (4, 5), 0), ((0, 2), (4, 5), 1)]] * 2 + [[((3, 2), (4, 5), 0), ((0, 1), (1, 4), 1)]]
+SPLIT = (True, True, True)
 ADDV = ((1, 1), (1, 1), (1, 0))
 
 SCRATCH = {
@@ -27,9 +26,9 @@ SCRATCH = {
     "nb": ("sbuf", [128, 256], "bfloat16"), "bm": ("sbuf", [128, 256], "bfloat16"), "nbf": ("sbuf", [128, 256], "float32"),
     "pf": ("sbuf", [128, N * TK], "float32"), "tt": ("sbuf", [128, 128], "float32"), "t1": ("sbuf", [128, 128], "float32"),
     "sg": ("sbuf", [128, 128], "float32"), "hl": ("sbuf", [128, 2, 2, 64], "bfloat16"), "ht": ("sbuf", [128, 256], "bfloat16"),
-    "xo": ("sbuf", [128, TK], "float32"),
+    "z": ("sbuf", [128, N * TK], "float32"), "xs": ("sbuf", [128, TK], "float32"), "xo": ("sbuf", [128, TK], "float32"),
     "jj": ("sbuf", [128, 128], "float32"), "ff": ("sbuf", [128, 72], "float32"), "gi": ("sbuf", [128, 8], "float32"),
-    "si": ("sbuf", [128, 512], "bfloat16"), "sm": ("sbuf", [128, 2, 512], "bfloat16"),
+    "sm": ("sbuf", [128, 1024], "bfloat16"),
     "ta": ("sbuf", [128, 128], "float32"), "tb": ("sbuf", [128, 128], "float32"), "tc": ("sbuf", [128, 128], "float32"),
     "ib": ("sbuf", [128, 128], "bfloat16"), "imb": ("sbuf", [128, 128], "bfloat16"),
     "i64b": ("sbuf", [128, 128], "bfloat16"), "ck": ("sbuf", [128, 256], "bfloat16"),
@@ -43,11 +42,8 @@ for _k in ("vv", "vs", "ss"):
     SCRATCH["w1" + _k] = ("sbuf", [128, 128], "float32")
     SCRATCH["w2" + _k] = ("sbuf", [128, 128], "float32")
 for _l in range(RO):
-    SCRATCH["st%d" % _l] = ("sbuf", [128, N, 2 * TK], "bfloat16")
+    SCRATCH["st%d" % _l] = ("sbuf", [128, 2 * N * TK], "bfloat16")
     SCRATCH["ld%d" % _l] = ("sbuf", [128, N, 2 * TK], "bfloat16")
-    SCRATCH["z%d" % _l] = ("sbuf", [128, N * TK], "float32")
-    SCRATCH["xs%d" % _l] = ("sbuf", [128, TK], "float32")
-    SCRATCH["rlz%d" % _l] = ("sbuf", [128, TK], "float32")
 for _l in range(RO - 1):
     SCRATCH["wd%d" % _l] = ("sbuf", [128, N * 128], "float16")
 SCRATCH["wd2"] = ("sbuf", [128, 128], "float16")
@@ -56,18 +52,22 @@ for _b in range(8):
 
 SEMAPHORES = ["cv", "cs", "ct", "cg", "sent", "sq", "lq", "lk", "lu", "lv", "ln", "lx", "lm", "lb", "aq", "oy", "ob"]
 for _l in range(RO):
-    SEMAPHORES += ["aw%d" % _l, "db%d" % _l, "fz%d" % _l] + ["%s%d_%d" % (_h, _l, _k) for _k in range(4) for _h in "ab"]
+    SEMAPHORES += ["aw%d" % _l, "db%d" % _l, "aq%d" % _l] + ["%s%d_%d" % (_h, _l, _k) for _k in range(2) for _h in "ab"]
 
 DBG = []
 OPS = {}
-WIN, TURNS, WAKE = dict(v=0.3, s=0.45, t=0.0), 3, 0.23
+PLAN = {}
+WINS = [dict(v=0.45, s=0.6, t=0.3)]
+TURNS, WAKE = 2, 0.11
 PERIOD = 16.0
-DUE = dict(now=(-20, -20, -20), keys=(-20.5, -21, -21), rows=(1.5, -6, 4), bias=(-3, -3, 2), sum=(-4, 12, 0), turn=(5, 25, 0), pick=(2, 3.5, -8),
-           dot=(27.5, 9.5, -5), sum4=(26, 14, -11), mix=(25, 14, 3))
+DUE = dict(now=(-20, -20, -20), list=(-200, -200, -200), keys=(-27.5, -37, -19.5), rows=(5.5, -11.5, -11.5), srow=(11, 9.5, 11.5), bias=(3.5, 3.5, 15.5),
+           sum=(19, -33, 0), turn=(4, 13.5, 0), pick=(-200, -200, -200), pickv=(6, 18.5, -9.5), dot=(11.5, 17.5, 2.5), sum4=(35.5, 2.5, -6.5), mix=(-12.5, -6, 11))
 BQ = "y"
-LATE = dict(q=2.0, w=1.5, far=1.5, fold=4.0, once=(1.5, 1.5, 0.0), bias=1.5)
-LINK = 0.0032
-CY, PE, GA, HOP = 0.00083, 0.00042, 1.56, 0.1
+LATE = dict(q=2.0, w=1.0, far=1.0, hop=2.2, fold=4.0, once=1.5, spare=(0.7, 0.7, 0.0), bias=1.5)
+ISSUE = 0.7
+FAR = ((0, 2), (0, 2), (1, 1))
+LINK = 0.002
+CY, PE, GA, HOP = 0.001, 0.0005, 1.7, 0.19
 
 
 def rank_program(g, core, T, topo):
@@ -81,7 +81,7 @@ def rank_program(g, core, T, topo):
         a = topo.addr(c)
         return DstId(rid=a[0], pnc=a[1])
 
-    def plan(r0, l):
+    def plan(r0, way):
         src = cores[r0]
         rest = [(r0 + k) % N for k in range(1, N)]
         near = [r for r in rest if topo.chip(cores[r]) == topo.chip(src)]
@@ -94,30 +94,30 @@ def rank_program(g, core, T, topo):
         mate = [r for r in far if topo.mates(topo.chip(src), topo.chip(cores[r]))]
         plane = [r for r in far if topo.same_plane(topo.chip(src), topo.chip(cores[r]))]
         both = [r for r in far if r not in mate + plane]
-        half = len(out) // 2
-        calls = [[(a, out[:half], None), (b, out[half:], None)] for a, b in [both] + list(zip(mate, plane))]
-        calls = [calls[k] for k in TURN]
-        calls.append([(r, home, None) for r in near])
-        return near, far, out, home, calls, free[0], both
+        hop, straight = (plane + both, mate) if way == 2 else (plane, both + mate)
+        via = free[:len(plane)] + [[c for c in free if topo.may_write(c, cores[r])][-1] for r in hop[len(plane):]]
+        calls = [[(r, es, h if way else None) for r, es, h in zip(hop, deal(home if way else out, len(hop)), via)],
+                 [(r, es, None) for r, es in zip(straight + near, deal(out, len(straight)) + [home])]]
+        return near, mate, plane, both, out, home, calls
+
+    def deal(es, n):
+        return [es[k * len(es) // n:(k + 1) * len(es) // n] for k in range(n)]
 
     if rank is None:
         left = 0
         for l in range(RO):
-            jobs = [(r0, k, r, es) for r0 in range(N) for k, c in enumerate(plan(r0, l)[4]) for r, es, h in c if h == core]
-            for r0, k, r, es in jobs:
-                out = topo.engines(core, cores[r])
-                a = topo.addr(cores[r])
-                sem = T.sem["a%d_%d" % (l, k)]
-                g.wait_ge(sem, len(es))
-                g.remote_dma(T["ld%d" % l][:, r0, :], T["st%d" % l][:, r, :], sem, T.sem.sent, a[1], a[0], bits(out))
+            for half in range(2):
+                jobs = [(r0, r, es) for r0 in range(N) for r, es, h in plan(r0, FAR[l][half])[-1][0] if h == core]
+                if not jobs:
+                    continue
+                out = topo.engines(core, cores[jobs[0][1]])
+                c = slice(half * TK, (half + 1) * TK)
+                sem = T.sem["%s%d_0" % ("ab"[half], l)]
+                g.wait_ge(sem, sum(len(es) for r0, r, es in jobs))
+                g.remote_dma_fused([RemoteDMATransfer(dst_ids=[dst(cores[r])], dma_engine_mask=bits(mine), remote_sem=sem,
+                                                      src=T["st%d" % l][:, (half * N + r) * TK:(half * N + r + 1) * TK],
+                                                      dst=T["ld%d" % l][:, r0, c]) for (r0, r, es), mine in zip(jobs, deal(out, len(jobs)))], local_sem=T.sem.sent)
                 left += len(out)
-            for r0 in range(N):
-                if FOLD[l] and plan(r0, l)[5] == core:
-                    out = topo.engines(core, cores[r0])
-                    a = topo.addr(cores[r0])
-                    g.wait_ge(T.sem["fz%d" % l], len(out))
-                    g.remote_dma(T["rlz%d" % l][:], T["rlz%d" % l][:], T.sem["fz%d" % l], T.sem.sent, a[1], a[0], bits(out))
-                    left += len(out)
         if left:
             g.wait_ge(T.sem.sent, left)
         return
@@ -167,11 +167,11 @@ def rank_program(g, core, T, topo):
         add("v", lambda: g.vector.memset(out, c), 64 * CY, (), wr)
 
     def act(out, a, f, rd, wr, banks=(), bias=0.0, scale=1.0, k=1.0):
-        add("s", lambda: g.scalar.activation(out, a, f, bias=bias, scale=scale), max(66, width(out) * k) * CY, rd, wr, banks)
+        add("s", lambda: g.scalar.activation(out, a, f, bias=bias, scale=scale), (max(66, width(out) * k) + 14) * CY, rd, wr, banks)
 
     def mmul(out, lhsT, rhs, start, stop, rd, wr, bank, k=1):
         add("t", lambda: g.tensor.matmul(out, lhsT, rhs, start, stop), max(min(64, width(lhsT)), width(rhs)) * k * PE, rd, wr, (bank,),
-            group=(start, stop), late=0.05)
+            group=(start, stop), late=-0.07)
 
     def dma(q, out, in_, rd, wr, sem, late=2.0):
         add(q, lambda: Q[q].dma_start(out, in_), 0.06, rd, wr, sem=sem, inc=16, late=late)
@@ -179,31 +179,31 @@ def rank_program(g, core, T, topo):
     def iota(out, pat, base, cm, wr):
         add("g", lambda: g.iota(out, pat, base, cm, allow_small_or_imprecise_dtypes=True), 0.13 + 2 * width(out) * CY, (), wr)
 
-    near, far, eout, ehome, calls, spare, both = plan(rank, 0)
-    step = {rank: len(calls)}
-    gets = [[0] * len(calls) for l in range(RO)]
-    for l in range(RO):
+    near, mate, plane, both, eout, ehome, calls = plan(rank, 0)
+    step = {}
+    gets = {}
+    for l in range(3):
         for s in range(N):
-            for k, c in enumerate(plan(s, l)[4]):
+            for k, c in enumerate(plan(s, l)[-1]):
                 for r, es, h in c:
                     if r == rank:
-                        step[s] = k
-                        gets[l][k] += len(es) if h is None else len(topo.engines(h, core))
-    srcs = sorted(range(N), key=lambda s: (step[s], s))
+                        step[l, s] = k
+                        gets[l, k] = gets.get((l, k), 0) + (len(es) if h is None else len(topo.engines(h, core)) // [x[2] for x in c].count(h))
+    srcs = both + plane + mate + near + [rank]
 
     def remote(transfers, engines, rd, sem, n, wr, late, wire=0.3):
-        left = "sq" if sem == "aq" else "sent"
+        left = "sq" if sem[:2] == "aq" else "sent"
 
         def emit():
             g.remote_dma_fused(transfers, local_sem=S[left])
-        add("g", emit, 0.3, rd, ["to" + sem] + ["remote"] * (sem[:2] not in ("aq", "fz")), sem=left, inc=engines)
+        add("g", emit, ISSUE, rd, ["to" + sem, "remote" + left], sem=left, inc=engines)
         ops[-1]["wire"] = wire
         add("a", None, 0.0, ["to" + sem], wr, sem=sem, inc=n, late=late)
 
     def send_all(ap, sem, rd, wr, late):
-        ways = [([c[k][0] for c in calls[:-1]], calls[0][k][1]) for k in range(2)] + [(near, ehome)]
+        ways = list(zip(([both[0]] + mate, [both[1]] + plane, near), deal(eout, 2) + [ehome]))
         tr = [RemoteDMATransfer(dst_ids=[dst(cores[r]) for r in to], dma_engine_mask=bits(es), remote_sem=S[sem], srcs=[ap], dsts=[ap] * len(to)) for to, es in ways]
-        remote(tr, sum(len(es) for to, es in ways), rd, sem, sum(len(to) * len(es) for to, es in ways), wr, late, 4 * width(ap) * LINK)
+        remote(tr, sum(len(es) for to, es in ways), rd, sem, sum(len(to) * len(es) for to, es in ways), wr, late, 6 * width(ap) * LINK)
 
     qown = T.qa[:, rank * TK:(rank + 1) * TK]
     dma("y", qown, T.rq[:], (), ["qown"], "lq")
@@ -212,14 +212,19 @@ def rank_program(g, core, T, topo):
     iota(T.jj[:], [[1, 128]], 0, -1, ["jj"])
     iota(T.gi[:], [[-16, 8]], 0, 1, ["gi"])
     iota(T.ff[:], [[1, 72]], 0, 0, ["ff"])
-    send_all(qown, "aq", ["qown"], ["qa"], LATE["q"])
-    iota(T.si[:], [[-8, 4], [-1, 8], [0, 16]], 0, 1, ["si"])
+    qkey = {rank // 2: "qa0"}
+    for k, to in enumerate((both, mate, plane)):
+        ways = list(zip(to, deal(eout, len(to)))) + [(near[0], ehome)] * (k == 0)
+        tr = [RemoteDMATransfer(dst_ids=[dst(cores[r])], dma_engine_mask=bits(es), remote_sem=S["aq%d" % k], src=qown, dst=qown) for r, es in ways]
+        n = sum(len(es) for r, es in ways)
+        remote(tr, n, ["qown"], "aq%d" % k, n, ["qa%d" % k], LATE["q"] if k == 0 else LATE["far"], 2 * TK * LINK)
+        qkey[to[0] // 2] = "qa%d" % k
     for j in range(4):
         dma("s", T.nb[:, j * 64:(j + 1) * 64], T.ke[32 * j + 15:32 * j + 32:16, :], (), ["nb%d" % j], "lb", 5.0)
     dma("y", T.x0b[:], T.x0[:], (), ["x0b"], "lx", 6.0)
     dma("y", T.mmb[:], T.mm[:], (), ["mmb"], "lm", 6.0)
-    dma("y", T.uw[:], T.ue[:], ["toaq"], ["uw"], "lu", 5.5)
-    dma("y", T.vw[:], T.ve[:], ["toaq"], ["vw"], "lv", 7.5)
+    dma("y", T.uw[:], T.ue[:], ["toaq2"], ["uw"], "lu", 3.0)
+    dma("y", T.vw[:], T.ve[:], ["toaq2"], ["vw"], "lv", 5.0)
 
     def diag(name, at, value, cols=slice(0, 128), key=None):
         vts(T[name][:, cols], T.jj[:, cols], float(at), float(value), A.is_equal, A.mult, ["jj"], [key or name])
@@ -272,14 +277,13 @@ def rank_program(g, core, T, topo):
                 vtt(T["w1" + kind][c, c], T.ta[c, c], T.tc[c, c], A.add, ["ta", "tc"], ["w1" + kind], k=2)
         vts(T["w2" + kind][:], T["w1" + kind][:], -2.0, None, A.mult, None, ["w1" + kind], ["w2" + kind])
     urge[0] = 3
-    SM = ["sm%d" % p for p in range(0, 128, 32)] + ["sz0", "sz1"]
-    for h in range(2):
-        vts(T.sm[64 - 64 * h:128 - 64 * h, h, :], T.si[64 - 64 * h:128 - 64 * h, :], 0.0, None, A.mult, None, ["si"], ["sz%d" % h], k=0.5)
-    for p in range(0, 128, 32):
-        vts(T.sm[p:p + 32, p // 64, :], T.si[p:p + 32, :], float(p), None, A.is_equal, None, ["si"], ["sm%d" % p], k=0.5)
+    SM = ["sm"]
+    iota(T.sm[:], [[0, 1024]], 0, 0, ["sm", "remotesq"])
+    for p in (0, 32):
+        add("g", lambda p=p: g.affine_select(T.sm[:], T.sm[:], [[-64, 2], [-1, 32], [0, 16]], A.not_equal, 1.0, -p, 1), 0.17 + 2048 * CY, (), ["sm"])
     act(T.mmf[:], T.mmb[:], F.Identity, ["mmb"], ["mmf"])
     act(B[6][:, 0:256], T.x0b[:], F.Identity, ["x0b"], ["x"], (6,))
-    act(T.xs0[:], T.x0b[:], F.Identity, ["x0b"], ["xs0"], scale=0.5)
+    act(T.xs[:], T.x0b[:], F.Identity, ["x0b"], ["xs"], scale=0.5)
 
     NB = ["nb%d" % j for j in range(4)]
 
@@ -316,14 +320,14 @@ def rank_program(g, core, T, topo):
         return T.kw[:].indirect(T.nl[:, c * 128 + ch * 32:c * 128 + (ch + 1) * 32])
 
     def scores(l):
-        rest = [ch for ch in range(4) if ch not in FUSED[l]]
+        rest = [ch for ch in range(4) if ch not in FUSED[l]] if l else list(qkey)
         bank = dict(zip(rest, (2, 3, 4, 5) if l == 0 else (2, 3, 2, 3)))
         wide = l == RO - 1
         due(l, "keys")
         for ch in FUSED[l]:
             for c in range(2):
                 k = 4 * c + ch
-                vtt(T.pk[:, k * KC:(k + 1) * KC], names(c, ch), T.qa[:, ch * KC:(ch + 1) * KC], A.mult, ["kw", "nl", "qa", "qown"], ["pk%d" % k], k=GA + 0.12)
+                vtt(T.pk[:, k * KC:(k + 1) * KC], names(c, ch), T.qa[:, ch * KC:(ch + 1) * KC], A.mult, ["kw", "nl", qkey[ch], "qown"], ["pk%d" % k], k=GA + 0.12)
             for i in range(16):
                 o = B[0][32 * ch:32 * ch + 32, i:128:16]
                 mmul(o, T.pk[:, ch * KC + i:(ch + 1) * KC:16], T.boh[:], True, False, ["pk%d" % ch, "pk%d" % (4 + ch), "boh"], ["sc%d_%d" % (ch, i)], 0)
@@ -333,14 +337,14 @@ def rank_program(g, core, T, topo):
             due(l, "keys")
             for c in range(2):
                 o = T.gk[:, (2 * ch + c) * KC:(2 * ch + c + 1) * KC]
-                if ch in VGATH[l]:
+                if rest.index(ch) in VGATH[l]:
                     vcp(o, names(c, ch), ["kw", "nl"], ["gk%d_%d" % (ch, c)], k=GA + 0.12)
                 else:
                     act(o, names(c, ch), F.Identity, ["kw", "nl"], ["gk%d_%d" % (ch, c)], k=GA + 0.15)
                 mmul(B[b][:], (T.ib, T.imb)[c][:], o, c == 0, c == 1, ["ib", "imb", "gk%d_%d" % (ch, c)], ["B%d" % b], b)
             due(l, "now")
             p, one = (T.pw, T.bof) if wide else (T.pk, T.boh)
-            vtt(p[:, ch * KC:(ch + 1) * KC], B[b][:], T.qa[:, ch * KC:(ch + 1) * KC], A.mult, ["B%d" % b, "qa", "qown"], ["pk%d" % ch], (b,))
+            vtt(p[:, ch * KC:(ch + 1) * KC], B[b][:], T.qa[:, ch * KC:(ch + 1) * KC], A.mult, ["B%d" % b, qkey[ch], "qown"], ["pk%d" % ch], (b,))
             for i in range(16):
                 mmul(B[0][32 * ch:32 * ch + 32, i:128:16], p[:, ch * KC + i:(ch + 1) * KC:16], one[:], True, True, ["pk%d" % ch, "boh", "bof"],
                      ["sc%d_%d" % (ch, i)], 0, 4 if wide else 1)
@@ -353,6 +357,7 @@ def rank_program(g, core, T, topo):
             vtt(T.tw[:, k * 128:(k + 1) * 128], B[1][:, (k + 2) * 128:(k + 3) * 128], T.sgn[:], A.mult, ["dif", "sgn"], ["tw%d" % k], (1,))
         for k, name in enumerate(("lo", "hi")):
             vtt(T[name][:], B[1][:, k * 128:(k + 1) * 128], T.tw[:, k * 128:(k + 1) * 128], A.add, ["mid", "tw%d" % k], [name], (1,))
+        due(l, "list")
         mmul(B[0][:, 256:384], T.lo[:], T.i64b[:], True, False, ["lo", "hi", "i64b"], ["wt", "xl"], 0)
         mmul(B[0][:, 256:384], T.hi[:], T.i64b[:], False, True, ["hi", "i64b"], ["wt"], 0)
         if l == RO - 1:
@@ -369,7 +374,7 @@ def rank_program(g, core, T, topo):
         for i in range(16):
             col = gr * 16 + i
             o = col * OW
-            due(l, "rows", 0.0 if byS else 0.054 * (i + 16 * len([x for x in range(gr) if x not in SGROUPS[l]])))
+            due(l, "srow" if byS else "rows", 0.054 * (i + 16 * len([x for x in range(gr) if x not in SGROUPS[l]])))
             if byS:
                 act(T.oh[:, o:o + 64], T.cs[:], F.Relu, ["cs", "lo"], ["oa%d" % col], bias=T.lo[:, col:col + 1], scale=-1.0)
                 act(T.oh[:, o + 64:o + 130], T.cl[:, 64:130], F.Relu, ["cl1", "hi"], ["oh%d" % col], bias=T.hi[:, col:col + 1], scale=-1.0)
@@ -391,7 +396,7 @@ def rank_program(g, core, T, topo):
         kind = "vs"[2 * j in SGROUPS[l]] + "vs"[2 * j + 1 in SGROUPS[l]]
         act(T.ms[:, j * 68:j * 68 + 66], B[b][:, 0:66], F.Identity, ["B%d" % b], ["ms%d" % j], (b,))
         c = slice(j * 64, (j + 1) * 64)
-        fb = 0 if last else 7
+        fb = 7
         o = B[fb][:, 384 + (j % 2) * 64:448 + (j % 2) * 64]
         key = "df%d_%d" % (fb, j % 2)
         mmul(o, T.ib[:], T.nb[:, c], True, False, ["ib", "ms%d" % j, NB[j]], [key], fb)
@@ -404,6 +409,7 @@ def rank_program(g, core, T, topo):
         else:
             vtt(T.nb[:, c], o, T.nb[:, c], A.max, [key], ["nb%d" % j], (fb,))
             dma(BQ if j == 3 else "y", T.kw[32 * j + 15:32 * j + 32:16, :], T.nb[:, c], ["nb%d" % j, "kw"], ["kw%d" % j], "db%d" % l, LATE["bias"])
+            ops[-1]["wire"] = 0.05
 
     def counts(l):
         due(l, "bias")
@@ -417,49 +423,58 @@ def rank_program(g, core, T, topo):
             lastw["kw"] = sum((lastw["kw%d" % j] for j in range(4)), [])
             readers["kw"] = []
 
-    def pick(l, r, halves, byV):
-        buf = T[("ld%d" if r == rank else "st%d") % l]
-        for half in halves:
-            o = buf[:, r, half * TK:(half + 1) * TK]
-            a = (T.uw, T.vw)[half][:].indirect(T.wl[:, r * 16:(r + 1) * 16])
-            rd, wr = ["wl", "uv"[half] + "w"], ["st%d_%d_%d" % (l, r, half)]
-            if byV:
-                vcp(o, a, rd, wr, k=GA + 0.24)
-            else:
-                act(o, a, F.Identity, rd, wr, k=GA + 0.3)
+    def pick(l, rs, half):
+        r, n = min(rs), len(rs)
+        o = T["ld%d" % l][:, r, half * TK:(half + 1) * TK] if rs == [rank] else T["st%d" % l][:, (half * N + r) * TK:(half * N + r + n) * TK]
+        a = (T.uw, T.vw)[half][:].indirect(T.wl[:, r * 16:(r + n) * 16])
+        rd, wr = ["wl", "uv"[half] + "w"], ["st%d_%d_%d" % (l, x, half) for x in rs]
+        if (srcs.index(rs[0]), half) in VPICK[l]:
+            vcp(o, a, rd, wr, k=GA + 0.24 / n)
+        else:
+            act(o, a, F.Identity, rd, wr, k=GA + 0.3 / n)
 
     def hand(l, k, halves):
-        due(l, "pick", 0.1 * k + halves[0])
-        byV = (k, halves[0]) in VPICK[l]
+        due(l, ("pick", "pickv")[halves[0]], 0.1 * k)
         if k == len(calls):
-            pick(l, rank, halves, byV)
+            pick(l, [rank], halves[0])
             return
         tr, rd = [], []
         sem = "%s%d_%d" % ("ab"[halves[0]], l, k)
         c = slice(halves[0] * TK, (halves[-1] + 1) * TK)
-        for r, es, h in calls[k]:
-            pick(l, r, halves, byV)
+        call = plan(rank, FAR[l][halves[0]])[-1][k]
+        for rs in (plane, both, mate, near):
+            if rs[0] in [x[0] for x in call]:
+                pick(l, rs, halves[0])
+        for r, es, h in call:
             rd += ["st%d_%d_%d" % (l, r, half) for half in halves]
-            tr.append(RemoteDMATransfer(dst_ids=[dst(cores[r])], dma_engine_mask=bits(es), remote_sem=S[sem], src=T["st%d" % l][:, r, c], dst=T["ld%d" % l][:, rank, c]))
-        wire = len(halves) * TK * LINK * (0 if len(tr) == 1 else 2 if calls[k][0][0] in both else 1)
-        remote(tr, sum(len(x[1]) for x in calls[k]), rd, sem, gets[l][k], ["ld%d_%d_%d" % (l, k, half) for half in halves], LATE["far"] + LATE["once"][l], wire)
+            src = T["st%d" % l][:, (halves[0] * N + r) * TK:(halves[0] * N + r + 1) * TK]
+            tr.append(RemoteDMATransfer(dst_ids=[dst(cores[r] if h is None else h)], dma_engine_mask=bits(es), remote_sem=S[sem], src=src,
+                                        dst=T["ld%d" % l][:, rank, c] if h is None else src))
+        rd += ["kw"] * (k == 1 and halves[0] == 1)
+        hop = call[-1][2] is not None
+        wire = (len(call) - k) * len(halves) * TK * LINK
+        remote(tr, sum(len(x[1]) for x in call), rd, sem, gets[FAR[l][halves[0]], k], ["ld%d_%d_%d" % (l, k, half) for half in halves],
+               LATE["far"] + LATE["spare"][l] + (LATE["hop"] + wire + LATE["once"] * (l == 0)) * hop, wire * (not hop))
 
     def landed(l, s, half):
-        return "st%d_%d_%d" % (l, s, half) if s == rank else "ld%d_%d_%d" % (l, step[s], half)
+        return "st%d_%d_%d" % (l, s, half) if s == rank else "ld%d_%d_%d" % (l, step[FAR[l][half], s], half)
 
-    def tokens(l, n, yb):
+    def tokens(l, m):
         ld = T["ld%d" % l]
-        pairs = [sorted(srcs[4 * n + 2 * k:4 * n + 2 * k + 2]) for k in range(2)]
+        ps, yb, slot = BATCH[l][m]
+        n, final = m % 2, m == len(BATCH[l]) - 1
+        pairs = [sorted(srcs[2 * p:2 * p + 2]) for p in ps]
         c = slice(n * 64, (n + 1) * 64)
         t = slice(n * 128, (n + 1) * 128)
         d = B[7][:, c]
-        due(l, "dot", n)
-        for j, s in enumerate(pairs[0] + pairs[1]):
+        due(l, "dot", m)
+        for s in sum((srcs[2 * p:2 * p + 2] for p in ps), []):
+            j = sum(pairs, []).index(s)
             vtt(T.pf[:, s * TK:(s + 1) * TK], ld[:, s, 0:TK], B[6][:, 0:TK], A.mult, [landed(l, s, 0), "x"], ["pf%d" % s], (6,))
             for h in range(2):
                 o = n * 64 + h * 32 + j * 8
-                mmul(B[7][:, o:o + 8], T.pf[:, s * TK + h * 128:s * TK + (h + 1) * 128], T.bof[:], True, True, ["pf%d" % s, "bof"], ["d%d_%d" % (h, s)], 7, 4)
-        D = ["d%d_%d" % (h, s) for s in pairs[0] + pairs[1] for h in range(2)]
+                mmul(B[7][:, o:o + 8], T.pf[:, s * TK + h * 128:s * TK + (h + 1) * 128], T.bof[:], True, True, ["pf%d" % s, "bof"], ["d%d_%d" % (n, 4 * h + j)], 7, 4)
+        D = ["d%d_%d" % (n, j) for j in range(8)]
         due(l, "now")
         act(T.tt[:, c], d, F.Tanh, D, ["tt%d" % n], (7,), scale=0.5)
         act(T.t1[:, c], T.tt[:, c], F.Identity, ["tt%d" % n], ["t1%d" % n], bias=0.125, scale=0.125)
@@ -469,47 +484,39 @@ def rank_program(g, core, T, topo):
         for h in range(2):
             mmul(B[7][64 * h:64 * h + 64, 128 + n * 128:256 + n * 128], T.hl[:, n, h, :], T.ib[:], True, True, ["hh%d" % n, "ll%d" % n, "ib"], ["tr%d_%d" % (n, h)], 7)
         act(T.ht[:, t], B[7][:, 128 + n * 128:256 + n * 128], F.Identity, ["tr%d_0" % n, "tr%d_1" % n], ["ht%d" % n], (7,))
-        due(l, "sum4", n)
-        for j in range(4):
+        due(l, "sum4", m)
+        for j in range(2 * len(ps)):
             b = yb[j // 2]
             for h in range(2):
                 o = (j % 2) * TK + h * 128
-                mmul(B[b][:, o:o + 128], T.sm[:, h, j * 128:(j + 1) * 128], T.ht[:, t], True, True, SM + ["ht%d" % n],
+                mmul(B[b][:, o:o + 128], T.sm[:, h * 512 + j * 128:h * 512 + (j + 1) * 128], T.ht[:, t], True, True, SM + ["ht%d" % n],
                      ["B%d" % b] + (["mid", "dif"] if b == 1 else []), b)
-        zz = T["z%d" % l]
-        addv = ADDV[l][n] and not FOLD[l]
-        z = [zz[:, (2 * n + k) * 512:(2 * n + k + 1) * 512] for k in range(2)]
         for k, b in enumerate(yb):
             s0, s1 = pairs[k]
             v = ld[:, s0:s1 + 1:s1 - s0, TK:2 * TK]
             rd = [landed(l, s0, 1), landed(l, s1, 1), "B%d" % b]
-            if k == 1 and addv:
+            z = T.z[:, slot * 512:(slot + 1) * 512]
+            if k or slot != m:
                 vtt(B[b][:], B[b][:], v, A.mult, rd, ["B%d" % b], (b,))
-                vtt(z[0], z[0], B[b][:], A.add, ["B%d" % b], ["z%d_%d" % (l, 2 * n)], (b,))
+                vtt(z, z, B[b][:], A.add, ["B%d" % b], ["z%d" % slot], (b,))
             else:
-                vtt(z[k], B[b][:], v, A.mult, rd, ["z%d_%d" % (l, 2 * n + k)], (b,))
-        o = B[6][:, TK:2 * TK]
-        due(l, "mix", n)
-        xs = T["xs%d" % l]
-        if FOLD[l] and n == 1:
-            es = topo.engines(core, spare)
-            tr = RemoteDMATransfer(dst_ids=[dst(spare)], dma_engine_mask=bits(es), remote_sem=S["fz%d" % l], alu_op=1,
-                                   srcs=[xs[:]] + [zz[:, k * TK:(k + 1) * TK] for k in range(N)], dsts=[T["rlz%d" % l][:]])
-            remote([tr], len(es), ["xs%d" % l] + ["z%d_%d" % (l, k) for k in range(4)], "fz%d" % l, len(es), ["zs"], LATE["fold"], 0.0)
-            mmul(o, T.mmf[:], T["rlz%d" % l][:], True, True, ["mmf", "zs"], ["mx"], 6, 4)
-        elif not FOLD[l]:
-            if n == 0:
-                mmul(o, T.mmf[:], xs[:], True, False, ["mmf", "xs%d" % l], ["mx"], 6, 4)
-            parts = 2 if addv else 4
-            for k in range(parts):
-                mmul(o, T.mmf[:], zz[:, n * 1024 + k * TK:n * 1024 + (k + 1) * TK], False, n == 1 and k == parts - 1, ["mmf", "z%d_%d" % (l, 2 * n + k // 2)], ["mx"], 6, 4)
-        due(l, "now")
-        if n == 1 and l < RO - 1:
-            act(B[6][:, 0:TK], o, F.Tanh, ["mx"], ["x"], (6,))
-            act(T["xs%d" % (l + 1)][:], B[6][:, 0:TK], F.Identity, ["x"], ["xs%d" % (l + 1)], (6,), scale=0.5)
-        elif n == 1:
-            act(T.xo[:], o, F.Tanh, ["mx"], ["xo"], (6,))
-            dma("s", T.yx[:], T.xo[:], ["xo"], (), "oy")
+                vtt(z, B[b][:], v, A.mult, rd, ["z%d" % slot], (b,))
+        parts = [(slot, k) for k in range(2)] if final or BATCH[l][m + 1][2] != slot else []
+        for h, (b, c0, c1) in enumerate(((6, 0, 128), (0, 128, TK)) if l == RO - 1 else ((6, 0, TK),)):
+            o = B[b][:, TK + c0:TK + c1] if b else B[0][:, c0:c1]
+            key = ["mx%d" % h]
+            due(l, "mix", m)
+            if m == 0:
+                mmul(o, T.mmf[:], T.xs[:, c0:c1], True, False, ["mmf", "xs"] + ["wl"] * h, key, b, 4)
+            for p, k in parts:
+                mmul(o, T.mmf[:], T.z[:, p * 512 + k * TK + c0:p * 512 + k * TK + c1], False, final and (p, k) == parts[-1], ["mmf", "z%d" % p], key, b, 4)
+            due(l, "now")
+            if final and l < RO - 1:
+                act(B[6][:, 0:TK], o, F.Tanh, key, ["x"], (6,))
+                act(T.xs[:], B[6][:, 0:TK], F.Identity, ["x"], ["xs"], (6,), scale=0.5)
+            elif final:
+                act(T.xo[:, c0:c1], o, F.Tanh, key, ["xo%d" % h], (b,))
+                dma("ys"[h], T.yx[:, c0:c1], T.xo[:, c0:c1], ["xo%d" % h], (), "oy")
 
     urge[0] = -40
     turn_names(T.nm0, "nm0")
@@ -523,8 +530,8 @@ def rank_program(g, core, T, topo):
         for halves in ([0], [1]) if SPLIT[l] else ([0, 1],):
             for k in range(len(calls) + 1):
                 hand(l, k, halves)
-        for h in range(2):
-            tokens(l, h, (1, 4) if last and h else (4, 5))
+        for m in range(len(BATCH[l])):
+            tokens(l, m)
 
     shared = {}
     for i, o in enumerate(ops):
@@ -542,13 +549,13 @@ def rank_program(g, core, T, topo):
     def gap(a, b):
         return -1.0 if ops[a]["q"] == ops[b]["q"] == "t" else 0.0 if ops[a]["q"] == ops[b]["q"] == "g" and ops[a]["sem"] else ops[a]["late"] + HOP
 
-    def lay(rank_of, back):
+    def lay(rank_of, back, win):
         pre, post = ([o["deps"] for o in ops], after) if not back else (after, [o["deps"] for o in ops])
         left = [len(p) for p in pre]
         can = [0.0] * len(ops)
         ready = {q: [] for q in "vstgya"}
         free = {q: 0.0 for q in list(ready) + ["wire"]}
-        end, order, bankq, opened, behind = {}, [], {}, {}, {}
+        end, order, bankq, opened = {}, [], {}, {}
         for i, o in enumerate(ops):
             if not left[i]:
                 ready[o["q"]].append(i)
@@ -560,11 +567,11 @@ def rank_program(g, core, T, topo):
                     o = ops[i]
                     if o["group"] and o["group"][back] and opened.get(o["banks"][0]):
                         continue
-                    t = max([can[i]] + [end[bankq[b]] + HOP for b in o["banks"] if b in bankq and ops[bankq[b]]["q"] != q])
+                    t = max([can[i]] + [end[bankq[b]] + HOP + ops[bankq[b]]["late"] for b in o["banks"] if b in bankq and ops[bankq[b]]["q"] != q])
                     c.append((free[q] if t <= free[q] else t + WAKE, i))
                 if c:
                     t0 = min(c)[0]
-                    t, i = min((x for x in c if x[0] <= t0 + WIN.get(q, 0.0)), key=lambda x: rank_of[x[1]])
+                    t, i = min((x for x in c if x[0] <= t0 + win.get(q, 0.0)), key=lambda x: rank_of[x[1]])
                     fill = [x for x in c if x[0] + ops[x[1]]["hold"] <= t + 0.01]
                     if fill:
                         t, i = min(fill, key=lambda x: rank_of[x[1]])
@@ -574,8 +581,6 @@ def rank_program(g, core, T, topo):
             o = ops[i]
             ready[o["q"]].remove(i)
             for b in o["banks"]:
-                if b in bankq and ops[bankq[b]]["q"] != o["q"]:
-                    behind.setdefault(i, set()).add(bankq[b])
                 bankq[b] = i
                 if o["group"]:
                     opened[b] = not o["group"][1 - back]
@@ -590,23 +595,25 @@ def rank_program(g, core, T, topo):
                 left[j] -= 1
                 if not left[j]:
                     ready[ops[j]["q"]].append(j)
-        return order, end, behind
+        return order, end
 
-    if "hook" in OPS:
-        OPS["hook"](lay, ops)
-    best = None
-    rank_of = [(i - 1e6 if o["sem"] else o["urge"], i) for i, o in enumerate(ops)]
-    for turn in range(TURNS):
-        order, end, behind = lay(rank_of, 0)
-        span = max(end[i] + ops[i]["late"] for i in order)
-        if best is None or span < best[0]:
-            best = (span, order, end, behind)
-        if turn < TURNS - 1:
-            back = lay([-end[i] for i in range(len(ops))], 1)[1]
-            rank_of = [i - 1e6 if o["sem"] else -back[i] for i, o in enumerate(ops)]
-    span, order, end, behind = best
+    if "best" not in PLAN:
+        for win in WINS:
+            rank_of = [(i - 1e6 if o["sem"] else o["urge"], i) for i, o in enumerate(ops)]
+            for turn in range(TURNS):
+                order, end = lay(rank_of, 0, win)
+                span = max(end[i] + ops[i]["late"] for i in order)
+                if span < PLAN.get("best", (1e9,))[0]:
+                    PLAN["best"] = (span, order, end)
+                back = lay([-end[i] for i in range(len(ops))], 1, win)[1]
+                rank_of = [i - 1e6 if o["sem"] or o["urge"] < -60 else -back[i] for i, o in enumerate(ops)]
+    span, order, end = PLAN["best"]
+    bankq = {}
     for i in order:
-        ops[i]["deps"].update(behind.get(i, ()))
+        for b in ops[i]["banks"]:
+            if b in bankq and ops[bankq[b]]["q"] != ops[i]["q"]:
+                ops[i]["deps"].add(bankq[b])
+            bankq[b] = i
         DBG.append((core, end[i] - ops[i]["hold"], end[i], ops[i]["q"], ops[i]["tag"]))
     OPS[core] = (ops, order, end)
 
@@ -625,7 +632,7 @@ def rank_program(g, core, T, topo):
         need = {}
         for d in o["deps"]:
             name, v = mark[d]
-            if (q == "t" and name == "ct") or name == o["sem"]:
+            if (q, name) in (("t", "ct"), ("g", "sq")) or name == o["sem"]:
                 continue
             need[name] = max(need.get(name, 0), count[name] if ops[d]["sem"] else v)
         for k, v in need.items():

import numpy as np
from concourse.bass import DstId, RemoteDMATransfer
from concourse.mybir import dt, AluOpType as A, ActivationFunctionType as F

N, E, TK, RO = 8, 4096, 256, 3
OW = 136
KC = 512
FUSED = ((), (2, 3), (2, 3))
VGATH = ((1, 3), (), ())
SGROUPS = ((5,), (5,), (3, 5, 7))
VPICK = ((), (), ((0, 0), (6, 0), (7, 0)))
BATCH = [[((3, 1), (4, 5), 0), ((0, 2), (4, 5), 1)]] * 2 + [[((3, 2), (4, 5), 0), ((0, 1), (1, 4), 1)]]
SPLIT = (True, True, True)
ADDV = ((1, 1), (1, 1), (1, 0))

SCRATCH = {
    "kw": ("sbuf", [128, E], "bfloat16"), "uw": ("sbuf", [128, E], "bfloat16"), "vw": ("sbuf", [128, E], "bfloat16"),
    "qa": ("sbuf", [128, N * TK], "bfloat16"), "nmi": ("sbuf", [128, 256], "int32"),
    "x0b": ("sbuf", [128, TK], "bfloat16"), "mmb": ("sbuf", [128, 128], "bfloat16"), "mmf": ("sbuf", [128, 128], "float32"),
    "nl": ("sbuf", [128, 256], "uint16"), "wl": ("sbuf", [128, 128], "uint16"),
    "nm0": ("sbuf", [128, 256], "float16"), "nf": ("sbuf", [128, 256], "float16"),
    "gk": ("sbuf", [128, 8 * KC], "bfloat16"), "pk": ("sbuf", [128, 8 * KC], "float16"), "pw": ("sbuf", [128, 4 * KC], "float32"),
    "sgn": ("sbuf", [128, 128], "bfloat16"), "tw": ("sbuf", [128, 256], "bfloat16"),
    "rr": ("sbuf", [128, 256], "bfloat16"), "lo": ("sbuf", [128, 128], "bfloat16"), "hi": ("sbuf", [128, 128], "bfloat16"),
    "oh": ("sbuf", [128, 128 * OW], "bfloat16"), "ms": ("sbuf", [128, 4 * 68], "float32"),
    "nb": ("sbuf", [128, 256], "bfloat16"), "bm": ("sbuf", [128, 256], "bfloat16"), "nbf": ("sbuf", [128, 256], "float32"),
    "pf": ("sbuf", [128, N * TK], "float32"), "tt": ("sbuf", [128, 128], "float32"), "t1": ("sbuf", [128, 128], "float32"),
    "sg": ("sbuf", [128, 128], "float32"), "hl": ("sbuf", [128, 2, 2, 64], "bfloat16"), "ht": ("sbuf", [128, 256], "bfloat16"),
    "z": ("sbuf", [128, N * TK], "float32"), "xs": ("sbuf", [128, TK], "float32"), "xo": ("sbuf", [128, TK], "float32"),
    "jj": ("sbuf", [128, 128], "float32"), "ff": ("sbuf", [128, 72], "float32"), "gi": ("sbuf", [128, 8], "float32"),
    "sm": ("sbuf", [128, 1024], "bfloat16"),
    "ta": ("sbuf", [128, 128], "float32"), "tb": ("sbuf", [128, 128], "float32"), "tc": ("sbuf", [128, 128], "float32"),
    "ib": ("sbuf", [128, 128], "bfloat16"), "imb": ("sbuf", [128, 128], "bfloat16"),
    "i64b": ("sbuf", [128, 128], "bfloat16"), "ck": ("sbuf", [128, 256], "bfloat16"),
    "ih": ("sbuf", [128, 128], "float16"), "sh": ("sbuf", [128, 128], "float16"),
    "hp": ("sbuf", [128, 128], "float16"), "hm": ("sbuf", [128, 128], "float16"), "hb": ("sbuf", [128, 384], "bfloat16"),
    "aa": ("sbuf", [128, 256], "bfloat16"), "one": ("sbuf", [128, 128], "bfloat16"), "cu": ("sbuf", [128, 256], "bfloat16"), "cb": ("sbuf", [128, 128], "bfloat16"),
    "ga": ("sbuf", [128, 8], "float32"), "bof": ("sbuf", [128, 8], "float32"), "boh": ("sbuf", [128, 8], "float16"),
    "bon": ("sbuf", [128, 8], "float16"), "cl": ("sbuf", [128, OW], "bfloat16"), "cs": ("sbuf", [128, 64], "bfloat16"),
}
for _k in ("vv", "vs", "ss"):
    SCRATCH["w1" + _k] = ("sbuf", [128, 128], "float32")
    SCRATCH["w2" + _k] = ("sbuf", [128, 128], "float32")
for _l in range(RO):
    SCRATCH["st%d" % _l] = ("sbuf", [128, 2 * N * TK], "bfloat16")
    SCRATCH["ld%d" % _l] = ("sbuf", [128, N, 2 * TK], "bfloat16")
for _l in range(RO - 1):
    SCRATCH["wd%d" % _l] = ("sbuf", [128, N * 128], "float16")
SCRATCH["wd2"] = ("sbuf", [128, 128], "float16")
for _b in range(8):
    SCRATCH["B%d" % _b] = ("psum", [128, 512], "float32")

SEMAPHORES = ["cv", "cs", "ct", "cg", "sent", "sq", "lq", "lk", "lu", "lv", "ln", "lx", "lm", "lb", "aq", "oy", "ob"]
for _l in range(RO):
    SEMAPHORES += ["aw%d" % _l, "db%d" % _l, "aq%d" % _l] + ["%s%d_%d" % (_h, _l, _k) for _k in range(2) for _h in "ab"]

DBG = []
OPS = {}
PLAN = {}
WINS = [dict(v=0.45, s=0.6, t=0.3)]
TURNS, WAKE = 2, 0.11
PERIOD = 16.0
DUE = dict(now=(-20, -20, -20), list=(-200, -200, -200), keys=(-27.5, -37, -19.5), rows=(5.5, -11.5, -11.5), srow=(11, 9.5, 11.5), bias=(3.5, 3.5, 15.5),
           sum=(19, -33, 0), turn=(4, 13.5, 0), pick=(-200, -200, -200), pickv=(6, 18.5, -9.5), dot=(11.5, 17.5, 2.5), sum4=(35.5, 2.5, -6.5), mix=(-12.5, -6, 11))
BQ = "y"
LATE = dict(q=2.0, w=1.0, far=1.0, hop=2.2, fold=4.0, once=1.5, spare=(0.7, 0.7, 0.0), bias=1.5)
ISSUE = 0.7
FAR = ((0, 2), (0, 2), (1, 1))
LINK = 0.002
CY, PE, GA, HOP = 0.001, 0.0005, 1.7, 0.19


def rank_program(g, core, T, topo):
    rank = T.rank_of(core)
    cores = list(T.cores)

    def bits(es):
        return int(sum(1 << e for e in es))

    def dst(c):
        a = topo.addr(c)
        return DstId(rid=a[0], pnc=a[1])

    def plan(r0, way):
        src = cores[r0]
        rest = [(r0 + k) % N for k in range(1, N)]
        near = [r for r in rest if topo.chip(cores[r]) == topo.chip(src)]
        far = [r for r in rest if r not in near]
        out = topo.engines(src, cores[far[0]])
        home = [e for e in topo.engines(src, cores[near[0]]) if e not in out]
        free = [c for c in topo.cores_of(src) if c not in cores and topo.die(c) == topo.die(src)]
        free.sort(key=lambda c: sum(topo.may_write(c, cores[r]) for r in far))
        far.sort(key=lambda r: topo.die(cores[r]) == topo.die(src))
        mate = [r for r in far if topo.mates(topo.chip(src), topo.chip(cores[r]))]
        plane = [r for r in far if topo.same_plane(topo.chip(src), topo.chip(cores[r]))]
        both = [r for r in far if r not in mate + plane]
        hop, straight = (plane + both, mate) if way == 2 else (plane, both + mate)
        via = free[:len(plane)] + [[c for c in free if topo.may_write(c, cores[r])][-1] for r in hop[len(plane):]]
        calls = [[(r, es, h if way else None) for r, es, h in zip(hop, deal(home if way else out, len(hop)), via)],
                 [(r, es, None) for r, es in zip(straight + near, deal(out, len(straight)) + [home])]]
        return near, mate, plane, both, out, home, calls

    def deal(es, n):
        return [es[k * len(es) // n:(k + 1) * len(es) // n] for k in range(n)]

    if rank is None:
        left = 0
        for l in range(RO):
            for half in range(2):
                jobs = [(r0, r, es) for r0 in range(N) for r, es, h in plan(r0, FAR[l][half])[-1][0] if h == core]
                if not jobs:
                    continue
                out = topo.engines(core, cores[jobs[0][1]])
                c = slice(half * TK, (half + 1) * TK)
                sem = T.sem["%s%d_0" % ("ab"[half], l)]
                g.wait_ge(sem, sum(len(es) for r0, r, es in jobs))
                g.remote_dma_fused([RemoteDMATransfer(dst_ids=[dst(cores[r])], dma_engine_mask=bits(mine), remote_sem=sem,
                                                      src=T["st%d" % l][:, (half * N + r) * TK:(half * N + r + 1) * TK],
                                                      dst=T["ld%d" % l][:, r0, c]) for (r0, r, es), mine in zip(jobs, deal(out, len(jobs)))], local_sem=T.sem.sent)
                left += len(out)
        if left:
            g.wait_ge(T.sem.sent, left)
        return
    Q = {"v": g.vector, "s": g.scalar, "t": g.tensor, "g": g, "y": g.sync}
    ops = []
    lastw, readers = {}, {}
    urge = [-50]

    def add(q, emit, hold, rd=(), wr=(), banks=(), sem=None, inc=1, late=0.0, group=None):
        deps = set()
        for k in rd:
            deps.update(lastw.get(k, ()))
        for k in wr:
            deps.update(lastw.get(k, ()))
            deps.update(readers.get(k, ()))
        me = len(ops)
        ops.append(dict(q=q, emit=emit, hold=hold, late=late, deps=deps, banks=banks, sem=sem, inc=inc, urge=urge[0], group=group, tag=(list(wr) + [""])[0]))
        for k in rd:
            readers.setdefault(k, []).append(me)
        for k in wr:
            lastw[k] = [me]
            readers[k] = []

    def due(l, what, more=0.0):
        urge[0] = PERIOD * l + DUE[what][l] + more

    S = T.sem
    B = [T["B%d" % b] for b in range(8)]

    def width(ap):
        return int(np.prod(ap.shape[1:]))

    def vts(out, in0, s1, s2, o0, o1, rd, wr, banks=(), k=1.0):
        hold = max(64, width(out) * k) * CY
        if s2 is None:
            add("v", lambda: g.vector.tensor_scalar(out, in0, s1, None, o0), hold, rd, wr, banks)
        else:
            add("v", lambda: g.vector.tensor_scalar(out, in0, s1, s2, o0, o1), hold, rd, wr, banks)

    def vtt(out, a, b, op, rd, wr, banks=(), k=1.0):
        add("v", lambda: g.vector.tensor_tensor(out, a, b, op), max(64, width(out) * k) * CY, rd, wr, banks)

    def vcp(out, a, rd, wr, banks=(), k=1.0):
        add("v", lambda: g.vector.tensor_copy(out, a), max(64, width(out) * k) * CY, rd, wr, banks)

    def vms(out, c, wr):
        add("v", lambda: g.vector.memset(out, c), 64 * CY, (), wr)

    def act(out, a, f, rd, wr, banks=(), bias=0.0, scale=1.0, k=1.0):
        add("s", lambda: g.scalar.activation(out, a, f, bias=bias, scale=scale), (max(66, width(out) * k) + 14) * CY, rd, wr, banks)

    def mmul(out, lhsT, rhs, start, stop, rd, wr, bank, k=1):
        add("t", lambda: g.tensor.matmul(out, lhsT, rhs, start, stop), max(min(64, width(lhsT)), width(rhs)) * k * PE, rd, wr, (bank,),
            group=(start, stop), late=-0.07)

    def dma(q, out, in_, rd, wr, sem, late=2.0):
        add(q, lambda: Q[q].dma_start(out, in_), 0.06, rd, wr, sem=sem, inc=16, late=late)

    def iota(out, pat, base, cm, wr):
        add("g", lambda: g.iota(out, pat, base, cm, allow_small_or_imprecise_dtypes=True), 0.13 + 2 * width(out) * CY, (), wr)

    near, mate, plane, both, eout, ehome, calls = plan(rank, 0)
    step = {}
    gets = {}
    for l in range(3):
        for s in range(N):
            for k, c in enumerate(plan(s, l)[-1]):
                for r, es, h in c:
                    if r == rank:
                        step[l, s] = k
                        gets[l, k] = gets.get((l, k), 0) + (len(es) if h is None else len(topo.engines(h, core)) // [x[2] for x in c].count(h))
    srcs = both + plane + mate + near + [rank]

    def remote(transfers, engines, rd, sem, n, wr, late, wire=0.3):
        left = "sq" if sem[:2] == "aq" else "sent"

        def emit():
            g.remote_dma_fused(transfers, local_sem=S[left])
        add("g", emit, ISSUE, rd, ["to" + sem, "remote" + left], sem=left, inc=engines)
        ops[-1]["wire"] = wire
        add("a", None, 0.0, ["to" + sem], wr, sem=sem, inc=n, late=late)

    def send_all(ap, sem, rd, wr, late):
        ways = list(zip(([both[0]] + mate, [both[1]] + plane, near), deal(eout, 2) + [ehome]))
        tr = [RemoteDMATransfer(dst_ids=[dst(cores[r]) for r in to], dma_engine_mask=bits(es), remote_sem=S[sem], srcs=[ap], dsts=[ap] * len(to)) for to, es in ways]
        remote(tr, sum(len(es) for to, es in ways), rd, sem, sum(len(to) * len(es) for to, es in ways), wr, late, 6 * width(ap) * LINK)

    qown = T.qa[:, rank * TK:(rank + 1) * TK]
    dma("y", qown, T.rq[:], (), ["qown"], "lq")
    dma("s", T.nmi[:], T.nm[:], (), ["nmi"], "ln")
    dma("y", T.kw[:], T.ke[:], (), ["kw"], "lk", 3.2)
    iota(T.jj[:], [[1, 128]], 0, -1, ["jj"])
    iota(T.gi[:], [[-16, 8]], 0, 1, ["gi"])
    iota(T.ff[:], [[1, 72]], 0, 0, ["ff"])
    qkey = {rank // 2: "qa0"}
    for k, to in enumerate((both, mate, plane)):
        ways = list(zip(to, deal(eout, len(to)))) + [(near[0], ehome)] * (k == 0)
        tr = [RemoteDMATransfer(dst_ids=[dst(cores[r])], dma_engine_mask=bits(es), remote_sem=S["aq%d" % k], src=qown, dst=qown) for r, es in ways]
        n = sum(len(es) for r, es in ways)
        remote(tr, n, ["qown"], "aq%d" % k, n, ["qa%d" % k], LATE["q"] if k == 0 else LATE["far"], 2 * TK * LINK)
        qkey[to[0] // 2] = "qa%d" % k
    for j in range(4):
        dma("s", T.nb[:, j * 64:(j + 1) * 64], T.ke[32 * j + 15:32 * j + 32:16, :], (), ["nb%d" % j], "lb", 5.0)
    dma("y", T.x0b[:], T.x0[:], (), ["x0b"], "lx", 6.0)
    dma("y", T.mmb[:], T.mm[:], (), ["mmb"], "lm", 6.0)
    dma("y", T.uw[:], T.ue[:], ["toaq2"], ["uw"], "lu", 3.0)
    dma("y", T.vw[:], T.ve[:], ["toaq2"], ["vw"], "lv", 5.0)

    def diag(name, at, value, cols=slice(0, 128), key=None):
        vts(T[name][:, cols], T.jj[:, cols], float(at), float(value), A.is_equal, A.mult, ["jj"], [key or name])

    vcp(T.nl[:], T.nmi[:], ["nmi"], ["nl"])
    vts(T.nm0[:], T.nmi[:], -2048.0, None, A.add, None, ["nmi"], ["nm0"])
    for name, value in (("ib", 1), ("imb", -1), ("hp", 1 / 128), ("hm", -1 / 128), ("i64b", 64)):
        diag(name, 0, value)
    for k in range(3):
        vts(T.hb[:, k * 128:(k + 1) * 128], T.jj[:], 0.0, 0.5 - k % 2, A.is_equal, A.mult, ["jj"], ["hb%d" % k])
    vts(T.ga[:], T.gi[:], 0.0, 15.0, A.max, A.min, ["gi"], ["ga"])
    vtt(T.bof[:], T.ga[:], T.gi[:], A.is_equal, ["ga", "gi"], ["bof"])
    vtt(T.boh[:], T.ga[:], T.gi[:], A.is_equal, ["ga", "gi"], ["boh"])
    vts(T.bon[:], T.bof[:], -1.0, None, A.mult, None, ["bof"], ["bon"])
    act(T.one[:], T.jj[:], F.Tanh, ["jj"], ["one"], bias=20.0, scale=0.0, k=13.0)
    vms(T.cu[:, 0:128], -1.75, ["cu0"])
    vms(T.cu[0:64, 128:256], 3.0, ["cu1"])
    vms(T.cu[64:128, 128:256], -63.0 / 8192, ["cu2"])
    vts(T.cl[:, 0:64], T.ff[:, 0:64], -64.0, None, A.add, None, ["ff"], ["cl0"])
    vts(T.cl[:, 64:130], T.ff[:, 0:66], 1.0 / 64, -65.0 / 128, A.mult, A.add, ["ff"], ["cl1"])
    urge[0] = 0
    vms(T.cb[:, 0:64], 1.0 / 64, ["cb0"])
    vms(T.cb[:, 64:128], -1.0 / 128, ["cb1"])
    diag("ih", 0, 1)
    vms(T.ck[:], 133.0 * 32, ["ck"])
    diag("sh", 16, 1, slice(16, 128), "sh0")
    diag("sh", 16 - 128, 1, slice(0, 16), "sh1")
    kinds = sorted({"vs"[2 * j in sg] + "vs"[2 * j + 1 in sg] for sg in SGROUPS for j in range(4)})
    diag("ta", 1, 64)
    diag("tb", -1, 64)
    diag("tc", 0, -128)
    vtt(T.ta[:], T.ta[:], T.tb[:], A.add, ["ta", "tb"], ["ta"], k=2)
    for kind in kinds:
        vms(T["w1" + kind][:], 0.0, ["w1" + kind])
        for h in range(2):
            if kind[h] == "v":
                c = slice(64 * h, 64 * h + 64)
                vtt(T["w1" + kind][c, c], T.ta[c, c], T.tc[c, c], A.add, ["ta", "tc"], ["w1" + kind], k=2)
                vms(T["w1" + kind][64 * h:64 * h + 1, 64 * h:64 * h + 1], -64.0, ["w1" + kind])
    if kinds != ["vv"]:
        vts(T.cs[:], T.ff[:, 0:64], -65.0, None, A.add, None, ["ff"], ["cs"])
        diag("ta", 0, -64)
        diag("tb", -1, 128)
        diag("tc", -2, -64)
        vtt(T.ta[:], T.ta[:], T.tb[:], A.add, ["ta", "tb"], ["ta"], k=2)
    for kind in kinds:
        for h in range(2):
            if kind[h] == "s":
                c = slice(64 * h, 64 * h + 64)
                vtt(T["w1" + kind][c, c], T.ta[c, c], T.tc[c, c], A.add, ["ta", "tc"], ["w1" + kind], k=2)
        vts(T["w2" + kind][:], T["w1" + kind][:], -2.0, None, A.mult, None, ["w1" + kind], ["w2" + kind])
    urge[0] = 3
    SM = ["sm"]
    iota(T.sm[:], [[0, 1024]], 0, 0, ["sm", "remotesq"])
    for p in (0, 32):
        add("g", lambda p=p: g.affine_select(T.sm[:], T.sm[:], [[-64, 2], [-1, 32], [0, 16]], A.not_equal, 1.0, -p, 1), 0.17 + 2048 * CY, (), ["sm"])
    act(T.mmf[:], T.mmb[:], F.Identity, ["mmb"], ["mmf"])
    act(B[6][:, 0:256], T.x0b[:], F.Identity, ["x0b"], ["x"], (6,))
    act(T.xs[:], T.x0b[:], F.Identity, ["x0b"], ["xs"], scale=0.5)

    NB = ["nb%d" % j for j in range(4)]

    def turn_names(nf, key):
        vts(T.aa[:], nf[:], 1.0 / 64, 192.0 - 63.0 / 128, A.mult, A.add, [key], ["aa"], k=0.5)
        mid, dif = B[1][:, 0:256], B[1][:, 256:512]
        H = ["hb0", "hb1", "hb2", "aa"]
        mmul(dif, T.aa[:, 0:128], T.hb[:, 0:256], True, False, H, ["dif"], 1)
        mmul(dif, T.aa[:, 128:256], T.hb[:, 128:384], False, False, H, ["dif"], 1)
        mmul(B[1][:, 384:512], nf[:, 0:128], T.hp[:], False, False, [key, "hp"], ["dif"], 1)
        mmul(B[1][:, 384:512], nf[:, 128:256], T.hm[:], False, True, [key, "hm"], ["dif"], 1)
        mmul(mid, T.one[:], T.cu[:], True, False, ["one", "cu0", "cu1", "cu2", "dif"], ["mid"], 1)
        for c in range(2):
            mmul(mid, T.aa[:, c * 128:(c + 1) * 128], T.hb[:, 0:256], False, False, H, ["mid"], 1)
            mmul(B[1][:, 128:256], nf[:, c * 128:(c + 1) * 128], T.hp[:], False, c == 1, [key, "hp"], ["mid"], 1)

    def next_names(l):
        wd = T["wd%d" % l]
        x = B[0][:, 128:384]
        due(l, "sum")
        mmul(x, T.ih[:], T.nm0[:], True, False, ["ih", "nm0", "wd%d" % l], ["xl", "wt"], 0)
        for s in range(N):
            for c in range(2):
                mmul(B[0][:, (c + 1) * 128:(c + 2) * 128], T.sh[:], wd[:, s * 128:(s + 1) * 128], False, False, ["sh0", "sh1", "wd%d" % l, "wo%d" % l], ["xl"], 0)
        mmul(x, T.one[:], T.ck[:], False, True, ["one", "ck"], ["xl"], 0)
        due(l, "now")
        act(T.rr[:], x, F.Identity, ["xl"], ["rr"], (0,), bias=0.5)
        vtt(T.nf[:], x, T.rr[:], A.subtract, ["xl", "rr"], ["nf"], (0,))
        vts(T.nl[:], T.nf[:], 2048.0, None, A.add, None, ["nf"], ["nl"], k=0.5)
        due(l, "turn")
        turn_names(T.nf, "nf")

    def names(c, ch):
        return T.kw[:].indirect(T.nl[:, c * 128 + ch * 32:c * 128 + (ch + 1) * 32])

    def scores(l):
        rest = [ch for ch in range(4) if ch not in FUSED[l]] if l else list(qkey)
        bank = dict(zip(rest, (2, 3, 4, 5) if l == 0 else (2, 3, 2, 3)))
        wide = l == RO - 1
        due(l, "keys")
        for ch in FUSED[l]:
            for c in range(2):
                k = 4 * c + ch
                vtt(T.pk[:, k * KC:(k + 1) * KC], names(c, ch), T.qa[:, ch * KC:(ch + 1) * KC], A.mult, ["kw", "nl", qkey[ch], "qown"], ["pk%d" % k], k=GA + 0.12)
            for i in range(16):
                o = B[0][32 * ch:32 * ch + 32, i:128:16]
                mmul(o, T.pk[:, ch * KC + i:(ch + 1) * KC:16], T.boh[:], True, False, ["pk%d" % ch, "pk%d" % (4 + ch), "boh"], ["sc%d_%d" % (ch, i)], 0)
                mmul(o, T.pk[:, (4 + ch) * KC + i:(5 + ch) * KC:16], T.bon[:], False, True, ["pk%d" % (4 + ch), "bon"], ["sc%d_%d" % (ch, i)], 0)
        for ch in rest:
            b = bank[ch]
            due(l, "keys")
            for c in range(2):
                o = T.gk[:, (2 * ch + c) * KC:(2 * ch + c + 1) * KC]
                if rest.index(ch) in VGATH[l]:
                    vcp(o, names(c, ch), ["kw", "nl"], ["gk%d_%d" % (ch, c)], k=GA + 0.12)
                else:
                    act(o, names(c, ch), F.Identity, ["kw", "nl"], ["gk%d_%d" % (ch, c)], k=GA + 0.15)
                mmul(B[b][:], (T.ib, T.imb)[c][:], o, c == 0, c == 1, ["ib", "imb", "gk%d_%d" % (ch, c)], ["B%d" % b], b)
            due(l, "now")
            p, one = (T.pw, T.bof) if wide else (T.pk, T.boh)
            vtt(p[:, ch * KC:(ch + 1) * KC], B[b][:], T.qa[:, ch * KC:(ch + 1) * KC], A.mult, ["B%d" % b, qkey[ch], "qown"], ["pk%d" % ch], (b,))
            for i in range(16):
                mmul(B[0][32 * ch:32 * ch + 32, i:128:16], p[:, ch * KC + i:(ch + 1) * KC:16], one[:], True, True, ["pk%d" % ch, "boh", "bof"],
                     ["sc%d_%d" % (ch, i)], 0, 4 if wide else 1)

    def winners(l):
        SC = ["sc%d_%d" % (ch, i) for ch in range(4) for i in range(16)]
        due(l, "now")
        act(T.sgn[:], B[0][:, 0:128], F.Sign, SC, ["sgn"], (0,), bias=0.5)
        for k in range(2):
            vtt(T.tw[:, k * 128:(k + 1) * 128], B[1][:, (k + 2) * 128:(k + 3) * 128], T.sgn[:], A.mult, ["dif", "sgn"], ["tw%d" % k], (1,))
        for k, name in enumerate(("lo", "hi")):
            vtt(T[name][:], B[1][:, k * 128:(k + 1) * 128], T.tw[:, k * 128:(k + 1) * 128], A.add, ["mid", "tw%d" % k], [name], (1,))
        due(l, "list")
        mmul(B[0][:, 256:384], T.lo[:], T.i64b[:], True, False, ["lo", "hi", "i64b"], ["wt", "xl"], 0)
        mmul(B[0][:, 256:384], T.hi[:], T.i64b[:], False, True, ["hi", "i64b"], ["wt"], 0)
        if l == RO - 1:
            vts(T.wl[:], B[0][:, 256:384], 4127.5, None, A.add, None, ["wt"], ["wl"], (0,))
            return
        wo = T["wd%d" % l][:, rank * 128:(rank + 1) * 128]
        vts(wo, B[0][:, 256:384], 2079.5, None, A.add, None, ["wt"], ["wo%d" % l], (0,))
        vts(T.wl[:], wo, 2048.0, None, A.add, None, ["wo%d" % l], ["wl"], k=0.5)
        send_all(wo, "aw%d" % l, ["wo%d" % l], ["wd%d" % l], LATE["w"])

    def count_group(l, gr):
        b, p0 = 2 + (gr // 2) % 2, (gr % 2) * 64
        byS = gr in SGROUPS[l]
        for i in range(16):
            col = gr * 16 + i
            o = col * OW
            due(l, "srow" if byS else "rows", 0.054 * (i + 16 * len([x for x in range(gr) if x not in SGROUPS[l]])))
            if byS:
                act(T.oh[:, o:o + 64], T.cs[:], F.Relu, ["cs", "lo"], ["oa%d" % col], bias=T.lo[:, col:col + 1], scale=-1.0)
                act(T.oh[:, o + 64:o + 130], T.cl[:, 64:130], F.Relu, ["cl1", "hi"], ["oh%d" % col], bias=T.hi[:, col:col + 1], scale=-1.0)
            else:
                vts(T.oh[:, o:o + 130], T.cl[:, 0:130], T.lo[:, col:col + 1], T.hi[:, col:col + 1], A.max, A.min,
                    ["cl0", "cl1", "lo", "hi"], ["oh%d" % col, "oa%d" % col], k=0.5)
        for i in range(16):
            col = gr * 16 + i
            o = col * OW
            due(l, "rows", 0.054 * (i + 16 * len([x for x in range(gr) if x not in SGROUPS[l]])))
            rows = range(gr * 16, gr * 16 + 16) if byS and i == 0 else [col]
            mmul(B[b][p0:p0 + 64, 0:66], T.oh[:, o:o + 64], T.oh[:, o + 64:o + 130], i == 0, i == 15,
                 ["oh%d" % c for c in rows] + ["oa%d" % c for c in rows], ["B%d" % b], b)

    def new_bias(l, j):
        last = l == RO - 1
        b = 2 + j % 2
        due(l, "bias")
        kind = "vs"[2 * j in SGROUPS[l]] + "vs"[2 * j + 1 in SGROUPS[l]]
        act(T.ms[:, j * 68:j * 68 + 66], B[b][:, 0:66], F.Identity, ["B%d" % b], ["ms%d" % j], (b,))
        c = slice(j * 64, (j + 1) * 64)
        fb = 7
        o = B[fb][:, 384 + (j % 2) * 64:448 + (j % 2) * 64]
        key = "df%d_%d" % (fb, j % 2)
        mmul(o, T.ib[:], T.nb[:, c], True, False, ["ib", "ms%d" % j, NB[j]], [key], fb)
        mmul(o, T.one[:], T.cb[:, 64 * last:64 * last + 64], False, False, ["one", "cb0", "cb1"], [key], fb)
        for k, w in ((0, "w1"), (1, "w2"), (2, "w1")):
            mmul(o, T[w + kind][:], T.ms[:, j * 68 + k:j * 68 + k + 64], False, k == 2, [w + kind, "ms%d" % j], [key], fb, 4)
        if last:
            vtt(T.nbf[:, c], o, T.bm[:, c], A.max, [key, "bm"], ["nbf%d" % j], (fb,))
            dma("y", T.yb[2 * j:2 * j + 2, :], T.nbf[:, c], ["nbf%d" % j], (), "ob")
        else:
            vtt(T.nb[:, c], o, T.nb[:, c], A.max, [key], ["nb%d" % j], (fb,))
            dma(BQ if j == 3 else "y", T.kw[32 * j + 15:32 * j + 32:16, :], T.nb[:, c], ["nb%d" % j, "kw"], ["kw%d" % j], "db%d" % l, LATE["bias"])
            ops[-1]["wire"] = 0.05

    def counts(l):
        due(l, "bias")
        if l == RO - 1:
            act(T.bm[:], T.nb[:], F.Identity, NB, ["bm"], bias=-3.0)
        for j in range(4):
            count_group(l, 2 * j)
            count_group(l, 2 * j + 1)
            new_bias(l, j)
        if l < RO - 1:
            lastw["kw"] = sum((lastw["kw%d" % j] for j in range(4)), [])
            readers["kw"] = []

    def pick(l, rs, half):
        r, n = min(rs), len(rs)
        o = T["ld%d" % l][:, r, half * TK:(half + 1) * TK] if rs == [rank] else T["st%d" % l][:, (half * N + r) * TK:(half * N + r + n) * TK]
        a = (T.uw, T.vw)[half][:].indirect(T.wl[:, r * 16:(r + n) * 16])
        rd, wr = ["wl", "uv"[half] + "w"], ["st%d_%d_%d" % (l, x, half) for x in rs]
        if (srcs.index(rs[0]), half) in VPICK[l]:
            vcp(o, a, rd, wr, k=GA + 0.24 / n)
        else:
            act(o, a, F.Identity, rd, wr, k=GA + 0.3 / n)

    def hand(l, k, halves):
        due(l, ("pick", "pickv")[halves[0]], 0.1 * k)
        if k == len(calls):
            pick(l, [rank], halves[0])
            return
        tr, rd = [], []
        sem = "%s%d_%d" % ("ab"[halves[0]], l, k)
        c = slice(halves[0] * TK, (halves[-1] + 1) * TK)
        call = plan(rank, FAR[l][halves[0]])[-1][k]
        for rs in (plane, both, mate, near):
            if rs[0] in [x[0] for x in call]:
                pick(l, rs, halves[0])
        for r, es, h in call:
            rd += ["st%d_%d_%d" % (l, r, half) for half in halves]
            src = T["st%d" % l][:, (halves[0] * N + r) * TK:(halves[0] * N + r + 1) * TK]
            tr.append(RemoteDMATransfer(dst_ids=[dst(cores[r] if h is None else h)], dma_engine_mask=bits(es), remote_sem=S[sem], src=src,
                                        dst=T["ld%d" % l][:, rank, c] if h is None else src))
        rd += ["kw"] * (k == 1 and halves[0] == 1)
        hop = call[-1][2] is not None
        wire = (len(call) - k) * len(halves) * TK * LINK
        remote(tr, sum(len(x[1]) for x in call), rd, sem, gets[FAR[l][halves[0]], k], ["ld%d_%d_%d" % (l, k, half) for half in halves],
               LATE["far"] + LATE["spare"][l] + (LATE["hop"] + wire + LATE["once"] * (l == 0)) * hop, wire * (not hop))

    def landed(l, s, half):
        return "st%d_%d_%d" % (l, s, half) if s == rank else "ld%d_%d_%d" % (l, step[FAR[l][half], s], half)

    def tokens(l, m):
        ld = T["ld%d" % l]
        ps, yb, slot = BATCH[l][m]
        n, final = m % 2, m == len(BATCH[l]) - 1
        pairs = [sorted(srcs[2 * p:2 * p + 2]) for p in ps]
        c = slice(n * 64, (n + 1) * 64)
        t = slice(n * 128, (n + 1) * 128)
        d = B[7][:, c]
        due(l, "dot", m)
        for s in sum((srcs[2 * p:2 * p + 2] for p in ps), []):
            j = sum(pairs, []).index(s)
            vtt(T.pf[:, s * TK:(s + 1) * TK], ld[:, s, 0:TK], B[6][:, 0:TK], A.mult, [landed(l, s, 0), "x"], ["pf%d" % s], (6,))
            for h in range(2):
                o = n * 64 + h * 32 + j * 8
                mmul(B[7][:, o:o + 8], T.pf[:, s * TK + h * 128:s * TK + (h + 1) * 128], T.bof[:], True, True, ["pf%d" % s, "bof"], ["d%d_%d" % (n, 4 * h + j)], 7, 4)
        D = ["d%d_%d" % (n, j) for j in range(8)]
        due(l, "now")
        act(T.tt[:, c], d, F.Tanh, D, ["tt%d" % n], (7,), scale=0.5)
        act(T.t1[:, c], T.tt[:, c], F.Identity, ["tt%d" % n], ["t1%d" % n], bias=0.125, scale=0.125)
        vtt(T.hl[:, n, :, 0:32], d, T.t1[:, c], A.mult, D + ["t1%d" % n], ["hh%d" % n], (7,))
        vtt(T.sg[:, c], d, T.t1[:, c], A.mult, D + ["t1%d" % n], ["sg%d" % n], (7,))
        vtt(T.hl[:, n, :, 32:64], T.sg[:, c], T.hl[:, n, :, 0:32], A.subtract, ["sg%d" % n, "hh%d" % n], ["ll%d" % n], k=2)
        for h in range(2):
            mmul(B[7][64 * h:64 * h + 64, 128 + n * 128:256 + n * 128], T.hl[:, n, h, :], T.ib[:], True, True, ["hh%d" % n, "ll%d" % n, "ib"], ["tr%d_%d" % (n, h)], 7)
        act(T.ht[:, t], B[7][:, 128 + n * 128:256 + n * 128], F.Identity, ["tr%d_0" % n, "tr%d_1" % n], ["ht%d" % n], (7,))
        due(l, "sum4", m)
        for j in range(2 * len(ps)):
            b = yb[j // 2]
            for h in range(2):
                o = (j % 2) * TK + h * 128
                mmul(B[b][:, o:o + 128], T.sm[:, h * 512 + j * 128:h * 512 + (j + 1) * 128], T.ht[:, t], True, True, SM + ["ht%d" % n],
                     ["B%d" % b] + (["mid", "dif"] if b == 1 else []), b)
        for k, b in enumerate(yb):
            s0, s1 = pairs[k]
            v = ld[:, s0:s1 + 1:s1 - s0, TK:2 * TK]
            rd = [landed(l, s0, 1), landed(l, s1, 1), "B%d" % b]
            z = T.z[:, slot * 512:(slot + 1) * 512]
            if k or slot != m:
                vtt(B[b][:], B[b][:], v, A.mult, rd, ["B%d" % b], (b,))
                vtt(z, z, B[b][:], A.add, ["B%d" % b], ["z%d" % slot], (b,))
            else:
                vtt(z, B[b][:], v, A.mult, rd, ["z%d" % slot], (b,))
        parts = [(slot, k) for k in range(2)] if final or BATCH[l][m + 1][2] != slot else []
        for h, (b, c0, c1) in enumerate(((6, 0, 128), (0, 128, TK)) if l == RO - 1 else ((6, 0, TK),)):
            o = B[b][:, TK + c0:TK + c1] if b else B[0][:, c0:c1]
            key = ["mx%d" % h]
            due(l, "mix", m)
            if m == 0:
                mmul(o, T.mmf[:], T.xs[:, c0:c1], True, False, ["mmf", "xs"] + ["wl"] * h, key, b, 4)
            for p, k in parts:
                mmul(o, T.mmf[:], T.z[:, p * 512 + k * TK + c0:p * 512 + k * TK + c1], False, final and (p, k) == parts[-1], ["mmf", "z%d" % p], key, b, 4)
            due(l, "now")
            if final and l < RO - 1:
                act(B[6][:, 0:TK], o, F.Tanh, key, ["x"], (6,))
                act(T.xs[:], B[6][:, 0:TK], F.Identity, ["x"], ["xs"], (6,), scale=0.5)
            elif final:
                act(T.xo[:, c0:c1], o, F.Tanh, key, ["xo%d" % h], (b,))
                dma("ys"[h], T.yx[:, c0:c1], T.xo[:, c0:c1], ["xo%d" % h], (), "oy")

    urge[0] = -40
    turn_names(T.nm0, "nm0")
    for l in range(RO):
        last = l == RO - 1
        scores(l)
        winners(l)
        if not last:
            next_names(l)
        counts(l)
        for halves in ([0], [1]) if SPLIT[l] else ([0, 1],):
            for k in range(len(calls) + 1):
                hand(l, k, halves)
        for m in range(len(BATCH[l])):
            tokens(l, m)

    shared = {}
    for i, o in enumerate(ops):
        if o["sem"]:
            shared.setdefault(o["sem"], []).append(i)
    after = [[] for o in ops]
    for i, o in enumerate(ops):
        for d in list(o["deps"]):
            name = ops[d]["sem"]
            if name and name != o["sem"] and o["q"] != "a":
                o["deps"].update(shared[name])
        for d in o["deps"]:
            after[d].append(i)

    def gap(a, b):
        return -1.0 if ops[a]["q"] == ops[b]["q"] == "t" else 0.0 if ops[a]["q"] == ops[b]["q"] == "g" and ops[a]["sem"] else ops[a]["late"] + HOP

    def lay(rank_of, back, win):
        pre, post = ([o["deps"] for o in ops], after) if not back else (after, [o["deps"] for o in ops])
        left = [len(p) for p in pre]
        can = [0.0] * len(ops)
        ready = {q: [] for q in "vstgya"}
        free = {q: 0.0 for q in list(ready) + ["wire"]}
        end, order, bankq, opened = {}, [], {}, {}
        for i, o in enumerate(ops):
            if not left[i]:
                ready[o["q"]].append(i)
        while len(order) < len(ops):
            best = None
            for q in ready:
                c = []
                for i in ready[q]:
                    o = ops[i]
                    if o["group"] and o["group"][back] and opened.get(o["banks"][0]):
                        continue
                    t = max([can[i]] + [end[bankq[b]] + HOP + ops[bankq[b]]["late"] for b in o["banks"] if b in bankq and ops[bankq[b]]["q"] != q])
                    c.append((free[q] if t <= free[q] else t + WAKE, i))
                if c:
                    t0 = min(c)[0]
                    t, i = min((x for x in c if x[0] <= t0 + win.get(q, 0.0)), key=lambda x: rank_of[x[1]])
                    fill = [x for x in c if x[0] + ops[x[1]]["hold"] <= t + 0.01]
                    if fill:
                        t, i = min(fill, key=lambda x: rank_of[x[1]])
                    if best is None or t < best[0]:
                        best = (t, i)
            t, i = best
            o = ops[i]
            ready[o["q"]].remove(i)
            for b in o["banks"]:
                bankq[b] = i
                if o["group"]:
                    opened[b] = not o["group"][1 - back]
            free[o["q"]] = end[i] = t + o["hold"]
            queued = 0.0
            if "wire" in o and not back:
                queued = max(0.0, free["wire"] - end[i]) + o["wire"] if o["wire"] else 0.0
                free["wire"] = max(free["wire"], end[i] + queued)
            order.append(i)
            for j in post[i]:
                can[j] = max(can[j], end[i] + (queued if ops[j]["q"] != "g" else 0.0) + (gap(j, i) + ops[j].get("wire", 0.0) * (o["q"] == "a") if back else gap(i, j)))
                left[j] -= 1
                if not left[j]:
                    ready[ops[j]["q"]].append(j)
        return order, end

    if "best" not in PLAN:
        for win in WINS:
            rank_of = [(i - 1e6 if o["sem"] else o["urge"], i) for i, o in enumerate(ops)]
            for turn in range(TURNS):
                order, end = lay(rank_of, 0, win)
                span = max(end[i] + ops[i]["late"] for i in order)
                if span < PLAN.get("best", (1e9,))[0]:
                    PLAN["best"] = (span, order, end)
                back = lay([-end[i] for i in range(len(ops))], 1, win)[1]
                rank_of = [i - 1e6 if o["sem"] or o["urge"] < -60 else -back[i] for i, o in enumerate(ops)]
    span, order, end = PLAN["best"]
    bankq = {}
    for i in order:
        for b in ops[i]["banks"]:
            if b in bankq and ops[bankq[b]]["q"] != ops[i]["q"]:
                ops[i]["deps"].add(bankq[b])
            bankq[b] = i
        DBG.append((core, end[i] - ops[i]["hold"], end[i], ops[i]["q"], ops[i]["tag"]))
    OPS[core] = (ops, order, end)

    count, mark = {}, {}
    for i in order:
        o = ops[i]
        name = o["sem"] or "c" + o["q"]
        count[name] = count.get(name, 0) + o["inc"]
        mark[i] = (name, count[name])
    seen = {q: {} for q in Q}
    for i in order:
        o = ops[i]
        q = o["q"]
        if o["emit"] is None:
            continue
        need = {}
        for d in o["deps"]:
            name, v = mark[d]
            if (q, name) in (("t", "ct"), ("g", "sq")) or name == o["sem"]:
                continue
            need[name] = max(need.get(name, 0), count[name] if ops[d]["sem"] else v)
        for k, v in need.items():
            if seen[q].get(k, 0) < v:
                Q[q].wait_ge(S[k], v)
                seen[q][k] = v
        ins = o["emit"]()
        if ins is not None:
            ins.then_inc(S[mark[i][0]], o["inc"])
    for k, v in count.items():
        if seen["g"].get(k, 0) < v:
            g.wait_ge(S[k], v)
